import numpy as np, ml_dtypes
CORES = [3,11,19,27,35,43,51,59]
N = 8
import mx_ref
BF = ml_dtypes.bfloat16
def gcols(t, e):
    v = np.concatenate([t.reshape(8, 16, -1, 4), np.zeros((8, 16, 1, 4), BF)], axis=2)
    return np.ascontiguousarray(np.stack([v[g][:, e[g]] for g in range(8)])).reshape(128, -1)
def gpick(z, e):
    return np.concatenate([z[16 * g:16 * g + 16][:, e[g]] for g in range(8)])
def tile(rs):
    return np.stack(rs, axis=2).reshape(128, -1).astype(BF)
def pick(q, e):
    c = np.concatenate([q[0].reshape(128, -1, 4), np.zeros((128, 1, 4), np.uint8)], axis=1); s = np.concatenate([q[1], np.ones((16, 1), np.uint8)], axis=1)
    return (np.ascontiguousarray(c[:, e].reshape(128, -1)), np.ascontiguousarray(s[:, e]))
def join(*qs):
    return (np.concatenate([q[0] for q in qs], axis=1), np.concatenate([q[1] for q in qs], axis=1))
def put(q, e, v):
    c, s = q[0].reshape(128, -1, 4).copy(), q[1].copy(); c[:, e] = v[0].reshape(128, -1, 4); s[:, e] = v[1]
    return (c.reshape(128, -1), s)
def pk(c, s):
    return (np.ascontiguousarray(c), mx_ref.live(s))
def emit(q):
    return q[0], q[1]
def packed(v, rng):
    q = [mx_ref.quantize(np.ascontiguousarray(v[r])) for r in range(N)]
    return np.stack([a for a, b in q]), np.stack([mx_ref.plane(b, rng) for a, b in q])
def values_of_codes():
    e, c = np.zeros((128, 128, 4), np.float32), np.zeros((128, 2, 4), np.uint8)
    e[np.arange(128), np.arange(128), 0] = 1
    c[:127, :, 0] = np.arange(256).reshape(2, 128).T[:127]
    return mx_ref.matmul(mx_ref.quantize(e.reshape(128, 512).astype(BF)), (c.reshape(128, 8), np.full((16, 2), 127, np.uint8))).T.reshape(-1).astype(np.float64)
CODE_VALUE, SCALE_VALUE = values_of_codes(), 2.0 ** (np.arange(256) - 127.0)
def decode(q):
    return (CODE_VALUE[q[0]].reshape(16, 8, -1, 4) * SCALE_VALUE[q[1]][:, None, :, None] + 0.0).reshape(128, -1).astype(np.float32)
def f(rng, *shape):
    return mx_ref.flush((rng.standard_normal(shape, dtype=np.float32) * np.exp2(rng.integers(-2, 3, shape[:-1] + (1,)))).astype(BF))
def wide(rng, *shape, cols=0):
    v = rng.standard_normal(shape, dtype=np.float32) * np.exp2(rng.integers(-12, 13, shape)).astype(np.float32)
    if cols: v *= np.repeat(np.exp2(rng.integers(-cols, cols + 1, shape[:-2] + (1, shape[-1] // 4))) * (rng.random(shape[:-2] + (1, shape[-1] // 4)) > 0.0625), 4, axis=-1).astype(np.float32)
    return mx_ref.flush(v.astype(BF))
C, H, E, K, J, R = 256, 64, 320, 96, 3, 2
def big(v):
    v = v.astype(np.float32)
    v[np.abs(v) < np.float32(2.0 ** -16)] = 0
    return v.astype(BF)
def numbers_of(rng):
    return {"x": big(f(rng, N, 128, 4 * C)), "u": np.array(f(rng, N, 128, 512)), "v": np.array(f(rng, N, 128, 512))}
def layers(rng):
    return big(f(rng, N, 128, 2048)).reshape(N, 8, 16, 4, 8, 16, 4)
def weights(rng, w):
    c, p = packed(np.ascontiguousarray(w).reshape(N, 128, 2048), rng)
    return {"wc": c, "ws": p}
def setup_inputs(rng):
    return {**numbers_of(rng), **weights(rng, layers(rng))}
def setup_inputs_ties(rng):
    d = numbers_of(rng)
    x = d["x"].reshape(N, 8, 16, C, 4)
    x[:, :, 0] = 0
    x[:, :, 0, :, 0] = rng.integers(0, 3, (N, 8, C)).astype(np.float32).astype(BF)
    u = d["u"].reshape(N, 128, 128, 4)
    u[:, :, ::16] = 0
    o = rng.permutation(N)
    for r in range(N):
        for h in range(0, 128, 16): u[r, h, h, 0] = 0.0 if r == o[0] else -1.0 if r == o[1] else 1.0
    w = layers(rng)
    w[:, :, :, :, :, 0] = 0
    return {"x": x.reshape(N, 128, 4 * C), "u": u.reshape(N, 128, 512), "v": d["v"], **weights(rng, w)}
def setup_inputs_near(rng):
    d = numbers_of(rng)
    x = d["x"].astype(np.float32).reshape(N, 8, 16, C, 4)
    u = d["u"].reshape(N, 128, 128, 4)
    o = rng.permutation(N) % 4
    x[:, :, :2] = 0
    x[:, :, 8:] = 0
    x[:, :, 0, :, 0] = 1
    u[:, :, ::16] = 0
    for r in range(N):
        s = rng.integers(0, 16, (8, C))
        low = rng.permutation(8)[:4]
        if o[r] == 3: s[low] = s[low] % 4
        x[r, :, 8] = ((s[:, :, None] >> np.arange(4)) & 1) * np.exp2(np.arange(4) - (23.0 if o[r] < 2 else 28.0))
        if o[r] == 3: x[r, low, 9] = x[r, low, 8]
        if o[r] < 2: x[r, :, 11, :, 0] = 2.0 ** -10
        for g in rng.permutation(8)[:4]: x[r, g, 1, rng.integers(C), 0] = 2.0 ** 28 * rng.choice([-1.0, 1.0])
        k = (1.0, -2.0 ** -30, 2.0 ** -30, -2.0 ** -30)[o[r]]
        for h in range(0, 128, 16):
            u[r, h + 8, h] = k
            if o[r] < 2:
                u[r, h, h, 0] = k
                u[r, h + 11, h, 0] = k
            if o[r] == 2: u[r, h + 1, h, 0] = 1.0
            if o[r] == 3 and h // 16 in low:
                u[r, h + 8, h] = -k
                u[r, h + 9, h] = 1.125 * k
    w = layers(rng)
    for i in (0, 1, 8, 9, 10, 11, 12, 13, 14, 15):
        w[:, :, i] = 0
        w[:, :, :, :, :, i] = 0
    return {"x": x.reshape(N, 128, 4 * C).astype(BF), "u": u.reshape(N, 128, 512), "v": d["v"], **weights(rng, w)}
def setup_inputs_huge(rng):
    d = numbers_of(rng)
    o = rng.permutation(N)
    c = rng.integers(0, 2, (N, 1, 1, C, 1))
    odd = np.arange(16).reshape(1, 1, 16, 1, 1) % 2
    x = np.where(c == odd, 2.0 ** 30 * (0.7 + 0.05 * rng.random((N, 8, 16, C, 4))), 2.0 ** 28 * (0.9 + 0.1 * rng.random((N, 8, 16, C, 4))))
    x[o == 0] = 2.0 ** 30 * (0.75 + 0.0625 * rng.integers(0, 3, (1, 8, 16, C, 4)))
    a = 2.0 ** 30 * (1.0 - 0.1 * rng.random((N, 8, 16, 8, 4)))
    for r in range(N):
        if o[r] == 0: a[r] = 2.0 ** 30 * (rng.permutation(8) % 2 * 2.0 - 1.0)[None, None, :, None]
        elif o[r] < N // 2: a[r] *= -1.0
        else: a[r] *= (1.0 - 2.0 * odd[0]) * rng.choice([-1.0, 1.0], (1, 1, 8, 1))
    u = d["u"].reshape(N, 128, 128, 4)
    u[:, :, ::16] = a.reshape(N, 128, 8, 4).astype(np.float32).astype(BF)
    w = np.zeros((N, 128, 4, 128, 4), np.float32)
    i = np.arange(128)
    for b in range(4): w[:, i, b, i, b] = -1
    return {"x": x.astype(np.float32).reshape(N, 128, 4 * C).astype(BF), "u": u.reshape(N, 128, 512), "v": d["v"], **weights(rng, w.astype(BF))}
def setup_inputs_long(rng):
    d = numbers_of(rng)
    x = d["x"].astype(np.float32).reshape(N, 8, 16, C, 4)
    x[:, :, 0] = 0
    x[:, :, 0, 1::2, 0] = 1
    s = np.arange(E) % 2
    s[E - 2:] = 1, 0
    m = E // 32
    far = np.concatenate([[m - 1], np.arange(m - 3, 0, -1), [0, m - 2]])
    less = np.concatenate([[m - 1], np.arange(m - 3, 0, -1), [m - 2, 0]])
    t = np.stack([m - 1 - far, m - 1 - less, far[::-1], less[::-1]])[rng.integers(0, 4, (N, 32))].reshape(N, E)
    for r in range(N):
        x[r, :, 0, :, 1 + r % 2] = s[:C]
        x[(r + 1) % N, :, 0, :H, 1 + r % 2] = s[C:]
        x[r, :, 1, :, 1 + r % 2] = t[r, :C]
        x[(r + 1) % N, :, 1, :H, 1 + r % 2] = t[r, C:]
    n = (N, 8, 8, C, 4)
    x[:, :, 8:] = (1.0 + (2 * rng.integers(0, 4, n) + 1) * 0.125) * np.exp2(12.0 - rng.integers(8, 15, n)) * (rng.integers(0, 2, n) * 2.0 - 1.0)
    x[:, :, 8, :, 0] = np.where(rng.random((N, 8, C)) < 0.5, 1.96875, 0.0625) * 2.0 ** 12
    u = d["u"].reshape(N, 128, 128, 4)
    for r in range(N):
        k = rng.permutation(8)
        for g in range(8):
            if k[g] < 7:
                u[r, :, 16 * g] = 0
                u[r, 16 * g + (1 if k[g] == 6 else 0), 16 * g, 0 if k[g] < 5 else 1 + r % 2] = -1.0 if k[g] in (3, 4) else 1.0
    w = layers(rng)
    w[:, :, :9] = 0
    return {"x": x.reshape(N, 128, 4 * C).astype(BF), "u": u.reshape(N, 128, 512), "v": d["v"], **weights(rng, w)}
def setup_inputs_spread(rng):
    d = setup_inputs(rng)
    d["x"] = big(wide(rng, N, 128, 4 * C, cols=6))
    return d
def check_inputs(d):
    b = []
    for k in ("x", "u", "v"):
        a = np.abs(d[k].astype(np.float32))
        if not (np.isfinite(a).all() and ((a == 0) | (a >= 2.0 ** -30) & (a <= 2.0 ** 30)).all()): b.append("a value of " + k)
    none, least, most = [emit(mx_ref.quantize(np.full((128, 16), k, np.float32).astype(BF)))[1][0, 0] for k in (0.0, 2.0 ** -30, 2.0 ** 30)]
    for r in range(N):
        if ((d["wc"][r] == 0x7F) | (d["wc"][r] == 0xFF)).any(): b.append("wc: a code that is no number")
        s = mx_ref.live(d["ws"][r])
        if ((s != none) & ((s < least) | (s > most))).any(): b.append("ws: a scale out of range")
    return b
def reference(x, u, v, wc, ws):
    qu = [mx_ref.quantize(u[r]) for r in range(N)]
    lay = [pk(wc[r], ws[r]) for r in range(N)]
    now = [x[r] for r in range(N)]
    mirror = np.zeros((N, 8, E), np.int64)
    place = np.arange(E)
    for t in range(R):
        q = [mx_ref.quantize(now[r]) for r in range(N)]
        left, away, far = [], [], []
        for r in range(N):
            window = join(q[r], pick(q[(r + 1) % N], np.arange(H)))
            s = mx_ref.matmul(qu[r], window)[::16] + np.float32(0.0)
            full = decode(window).astype(BF)
            standing = np.argsort(np.argsort(-s, axis=1, kind="stable"), axis=1)
            o = np.argsort(place + standing // 32, axis=1, kind="stable")
            end = np.maximum.accumulate(o, axis=1) == place
            b = np.minimum.accumulate(np.where(end, place, E)[:, ::-1], axis=1)[:, ::-1]
            a = np.concatenate([np.zeros((8, 1), np.int64), np.maximum.accumulate(np.where(end, place + 1, 0), axis=1)[:, :-1]], axis=1)
            mirror[r] = np.take_along_axis(o, a + b - place, axis=1)
            z = (gcols(full, o[:, :C]).astype(np.float32) - gcols(full, mirror[r][:, :C]).astype(np.float32) * np.float32(0.5)).astype(BF)
            e = np.argsort(-np.abs(o - place)[:, :C], axis=1, kind="stable")[:, :K]
            left.append(z)
            away.append(e)
            far.append(mx_ref.quantize(gcols(z, e)))
        for r in range(N):
            back = np.full((8, C), K)
            np.put_along_axis(back, away[r], np.arange(K)[None, :], axis=1)
            rows = []
            for b in range(4):
                p = mx_ref.matmul(pick(lay[r], np.arange(128 * b, 128 * b + 128)), far[(r - J) % N]) * np.float32(0.03125)
                p = np.concatenate([p, np.zeros((128, 1), np.float32)], axis=1)
                rows.append(gpick(p, back) + left[r][:, b::4].astype(np.float32))
            now[r] = tile(rows)
    y, lm = np.zeros((N, 128, C), np.float32), np.zeros((N, 8, E), np.float32)
    oc, osc = np.zeros((N, 128, 4 * C), np.uint8), np.zeros((N, 16, C), np.uint8)
    for r in range(N):
        q = mx_ref.quantize(now[r])
        y[r] = mx_ref.matmul(mx_ref.quantize(v[r]), q)
        lm[r] = mirror[r]
        oc[r], osc[r] = emit(q)
    return {"y": y, "lm": lm, "oc": oc, "osc": osc}

@@ -1,0 +1,507 @@
+from concourse.mybir import dt, AluOpType, ActivationFunctionType, AxisListType
+
+A = AluOpType
+AF = ActivationFunctionType
+C, H, E, K, J, R = 256, 64, 320, 96, 3, 2
+BIG = 2.0 ** 96
+HOLD = 1024.0
+HOLD2 = 16.0
+TINY = 2.0 ** -18
+CODE, PLANE, BF, F16, F32, U16 = "float8_e4m3fn_x4", "uint8", "bfloat16", "float16", "float32", "uint16"
+HALF = 192
+S_ROWS = (15, 14)
+
+
+def _sb(n, d):
+    return ("sbuf", [128, n], d)
+
+
+SCRATCH = {
+    "xt": _sb(1024, BF), "ut": _sb(512, BF), "vt": _sb(512, BF), "x1": _sb(1024, BF), "x2": _sb(1024, BF),
+    "wq": _sb(512, CODE), "wp": _sb(512, PLANE), "uq": _sb(128, CODE), "up": _sb(128, PLANE),
+    "udq": _sb(128, CODE), "udp": _sb(128, PLANE), "vq": _sb(128, CODE), "vp": _sb(128, PLANE),
+    "eq": _sb(512, CODE), "ep": _sb(512, PLANE), "gq": _sb(128, CODE), "gp": _sb(128, PLANE),
+    "q0": _sb(E, CODE), "p0": _sb(E, PLANE), "q1": _sb(E, CODE), "p1": _sb(E, PLANE), "q2": _sb(C, CODE), "p2": _sb(C, PLANE),
+    "aq0": _sb(K + 128, CODE), "ap0": _sb(K + 128, PLANE), "aq1": _sb(K + 128, CODE), "ap1": _sb(K + 128, PLANE),
+    "tA": _sb(512, BF), "tB": _sb(512, BF), "tC": _sb(768, BF), "tD": _sb(1280, BF), "tE": _sb(1280, BF), "tF": _sb(1280, BF),
+    "qA": _sb(128, CODE), "qB": _sb(128, CODE), "qC": _sb(192, CODE), "qD": _sb(E, CODE), "qE": _sb(E, CODE), "qF": _sb(E, CODE),
+    "pA": _sb(128, PLANE), "pB": _sb(128, PLANE), "pC": _sb(192, PLANE), "pD": _sb(E, PLANE), "pE": _sb(E, PLANE), "pF": _sb(E, PLANE),
+    "at": _sb(512, BF), "a32": _sb(4 * K, BF),
+    "iz": _sb(E + 16, F32), "jj": _sb(520, BF), "wd": _sb(520, BF), "gi": _sb(512, BF), "gt": _sb(512, BF),
+    "col": _sb(16, F32), "ul": _sb(8, U16), "uf": _sb(8, F32),
+    "m1": _sb(E + 16, F32), "c1": _sb(E, BF), "k16": _sb(E, BF), "ct": _sb(E, BF), "le1": _sb(E, BF), "spk": _sb(E, BF), "inc": _sb(E, F32),
+    "kc": _sb(E, F32), "it": _sb(E, F32), "ib": _sb(C, BF), "kx": _sb(E + 16, BF), "cc": _sb(E, BF), "cd": _sb(E, BF),
+    "one": _sb(C, BF), "neg": _sb(E, BF), "i16": _sb(20, F32), "iwh": _sb(20, F32), "iwd": _sb(20, F32), "iws": _sb(16, F32),
+    "val": _sb(E, F32), "hold": _sb(E, F32), "sg": _sb(2 * C, BF), "junk": _sb(16 * 200, BF), "rs": _sb(20, F32), "dr": _sb(E, BF),
+    "s1": _sb(20, F32), "s2": _sb(20, F32), "xh": _sb(2 * E, BF), "uu": _sb(E, BF), "lt": _sb(E, BF), "ng": _sb(E, BF), "ne": _sb(E, BF),
+    "qf": _sb(E, BF), "qb": _sb(E, BF), "cap": _sb(C, F32), "capb": _sb(E, BF), "capv": _sb(C, BF), "capm": _sb(C, BF), "cap2": _sb(E, F32),
+    "cap3": _sb(K, F32), "nd": _sb(E, BF), "vv": _sb(E, BF),
+    "mx": _sb(E, BF), "nen": _sb(E + 16, BF), "cs": _sb(E, BF), "ra": _sb(E, F16), "sm": _sb(E, F16), "vm": _sb(C, BF), "ww": _sb(C, BF), "sc": _sb(2, F32),
+    "nh": _sb(C, BF), "npf": _sb(C, BF), "xx": _sb(C, BF), "eb": _sb(C, BF),
+    "f1": _sb(20, F32), "f2": _sb(16, F32), "f3": _sb(16, F32), "f4": _sb(16, F32), "f5": _sb(16, F32), "f6": _sb(16, F32), "mf": _sb(20, F32),
+    "lpos": _sb(20, U16), "lo": _sb(16, U16), "lmir": _sb(20, U16), "lmm": _sb(16, U16), "lrk": _sb(16, U16), "le": _sb(6, U16), "lsel": _sb(16, U16),
+    "ff": _sb(4 * E, BF), "yy": _sb(4 * C, BF), "gg": _sb(4 * C, BF), "ge": _sb(4 * K, BF), "zw": _sb(4 * (C + K), BF),
+    "lmo": _sb(E, F32), "ob": _sb(E, F32), "yo": _sb(C, F32),
+}
+PART = {}
+for _n, _names in (("cf", "uf i16 iwh iwd iws"), ("df", "f1 f2 f3 f4 f5 f6 mf s1 s2 rs sc"), ("ls", "lpos lo lmir lmm lrk le lsel")):
+    _at = 0
+    for _k in _names.split():
+        _w, (_p, _c), _d = SCRATCH.pop(_k)
+        PART[_k] = (_n, _at, _c)
+        _at += -(-_c // 16) * 16
+    SCRATCH[_n] = _sb(_at, _d)
+for _b in range(8):
+    SCRATCH["ps%d" % _b] = ("psum", [128, 512], F32)
+SEMAPHORES = ["sV", "sS", "sP", "sG", "ldx", "ldu", "ldv", "ldw", "ldp", "arH0", "arH1", "arA0", "arA1", "sent",
+              "st0", "st1", "st2", "st3", "st4", "st5", "st6"]
+
+
+def _meet(a, b):
+    if a[0] != b[0]:
+        return False
+    if a[0].startswith("ps"):
+        return True
+    if a[2] <= b[1] or b[2] <= a[1]:
+        return False
+    return not (a[3] == b[3] and a[3] > 1 and (a[1] - b[1]) % a[3] != 0)
+
+
+def rank_program(g, core, T, topo):
+    rank = T.rank_of(core)
+    if rank is None:
+        return
+    N = len(T.cores)
+    ops = []
+
+    def v(name, a=0, b=None, s=1):
+        if name in PART:
+            name, at, n = PART[name]
+            a, b = at + a, at + (n if b is None else b)
+        b = SCRATCH[name][1][1] if b is None else b
+        return (T[name][:, a:b:s] if s > 1 else T[name][:, a:b], (name, a, b, s))
+
+    def rev(name, a, b):
+        return (T[name][:, b - 1::-1] if a == 0 else T[name][:, b - 1:a - 1:-1], (name, a, b, 1))
+
+    def ind(win, off):
+        return (win[0].indirect(off[0]), win[1], off[1])
+
+    def ap(x):
+        return x[0] if isinstance(x, tuple) else x
+
+    def regs(*xs):
+        return [r for x in xs if isinstance(x, tuple) for r in x[1:]]
+
+    def op(q, call, reads, writes, sem=None, count=16):
+        ops.append([q, call, reads, writes, sem, count])
+
+    def ts(out, in0, s1, o0, s2=None, o1=None):
+        if o1 is None:
+            op("V", lambda: g.vector.tensor_scalar(out[0], in0[0], ap(s1), None, o0), regs(in0, s1), regs(out))
+        else:
+            op("V", lambda: g.vector.tensor_scalar(out[0], in0[0], ap(s1), ap(s2), o0, o1), regs(in0, s1, s2), regs(out))
+
+    def tt(out, a, b, o):
+        op("V", lambda: g.vector.tensor_tensor(out[0], a[0], b[0], o), regs(a, b), regs(out))
+
+    def cp(out, a):
+        op("V", lambda: g.vector.tensor_copy(out[0], a[0]), regs(a) + list(out[2:]), [out[1]])
+
+    def scan(out, d0, d1, init, o0, o1):
+        op("V", lambda: g.vector.tensor_tensor_scan(out[0], d0[0], d1[0], ap(init), o0, o1), regs(d0, d1, init), regs(out))
+
+    def fill(out, c):
+        op("V", lambda: g.vector.memset(out[0], c), [], regs(out))
+
+    def quant(q, p, t):
+        op("V", lambda: g.vector.quantize_mx(q[0], p[0], t[0]), regs(t), regs(q, p))
+
+    def act(out, a, f, bias=None, scale=1.0, acc=None):
+        kw = {"scale": scale}
+        if bias is not None:
+            kw["bias"] = ap(bias)
+        if acc is not None:
+            kw["accum_out"] = acc[0]
+        op("S", lambda: g.scalar.activation(out[0], a[0], f, **kw), regs(a, bias), regs(out, acc))
+
+    def lin(out, a, scale, bias):
+        act(out, a, AF.Identity, bias=bias, scale=scale)
+
+    def mm(bank, n, w, x, start=True, stop=True):
+        out = v("ps%d" % bank, 0, n)
+        op("P", lambda: g.tensor.matmul_mx(out[0], w[0][0], w[1][0], x[0][0], x[1][0], start, stop), regs(*w, *x), regs(out))
+
+    def iota(out, pat, base, cm):
+        op("G", lambda: g.iota(out[0], pat, base, cm, allow_small_or_imprecise_dtypes=True), [], regs(out))
+
+    def gfill(out, c):
+        iota(out, [[0, out[1][2] - out[1][1]]], c, 0)
+
+    def dma(q, out, in_, reads, writes, sem):
+        e = g.sync if q == "Y" else g.scalar
+        op(q, lambda: e.dma_start(out, in_), reads, writes, sem)
+
+    sent = [0]
+
+    def send(dst, qn, pn, a, b, at, sem):
+        rid, pid = topo.addr(dst)[:2]
+        mask = topo.mask(core, dst)
+        n = len(topo.engines(core, dst))
+        so, si = v(pn, at, at + b - a), v(pn, a, b)
+        co, ci = v(qn, at, at + b - a), v(qn, a, b)
+        op("G", lambda: g.remote_dma(co[0].bitcast(dt.uint8), ci[0].bitcast(dt.uint8), T.sem[sem], T.sem.sent, pid, rid, mask), regs(ci), [], "remote")
+        op("G", lambda: g.remote_dma(so[0], si[0], T.sem[sem], T.sem.sent, pid, rid, mask), regs(si), [], "remote")
+        sent[0] += 2 * n
+
+    def lands(src, qn, pn, a, b, sem):
+        op("far", None, [], regs(v(qn, a, b), v(pn, a, b)), sem, 2 * len(topo.engines(src, core)))
+
+    def ps(b, a=0, e=E):
+        return v("ps%d" % b, a, e)
+
+    def col(i):
+        return v("col", i, i + 1)
+
+    def pair(qn, pn, a, b):
+        return (v(qn, a, b), v(pn, a, b))
+
+    prev, nxt = T.cores[(rank - 1) % N], T.cores[(rank + 1) % N]
+    far_to, far_from = T.cores[(rank + J) % N], T.cores[(rank - J) % N]
+
+    dma("Y", T.xt[:], T.x[:], [], regs(v("xt")), "ldx")
+    dma("S", T.ut[:], T.u[:], [], regs(v("ut")), "ldu")
+    for t in range(R):
+        lands(nxt, "q%d" % t, "p%d" % t, C, E, "arH%d" % t)
+        lands(far_from, "aq%d" % t, "ap%d" % t, 0, K, "arA%d" % t)
+    behind = regs(v("q0", C, E))
+    dma("Y", T.wq[:].bitcast(dt.uint8), T.wc[:], behind, regs(v("wq")), "ldw")
+    dma("Y", T.wp[:], T.ws[:], behind, regs(v("wp")), "ldp")
+    dma("Y", T.vt[:], T.v[:], behind, regs(v("vt")), "ldv")
+
+    iota(col(0), [[0, 1]], -15, 2)
+    iota(v("iz"), [[0, 21], [-2, 16]], 0, 2)
+    iota(v("uf"), [[16, 8]], 0, 0)
+    iota(v("gi"), [[1, 8], [0, 64]], 0, 0)
+    M32 = 1.5 * 2.0 ** 28
+    fill(v("c1"), 0.0)
+    fill(v("k16"), 1.0)
+    ts(col(2), col(0), M32, A.add, M32, A.subtract)
+    fill(v("c1", 0, E, 16), 2 * BIG)
+    fill(v("k16", 0, E, 16), 0.0)
+    fill(v("tD", 832), 0.0)
+    ts(col(12), col(0), col(2), A.subtract, 15.0, A.add)
+    ts(v("m1"), v("iz"), col(2), A.not_equal, BIG, A.mult)
+    cp(v("ul"), v("uf"))
+    fill(v("tA", 64), 0.0)
+    fill(v("tB", 320), 0.0)
+    fill(col(11), -0.5 * C)
+    lin(col(1), col(12), 0.5, 0.0)
+    lin(col(3), col(2), 1.0 / 32, 0.0)
+    act(v("kx"), v("m1"), AF.Sign)
+    kb, kf = v("kx", 16, 16 + E), v("kx", 15, 15 + E)
+    lin(v("kc", 0, 1), col(1), -32.0, 32.0 * 192 - 15.5)
+    lin(col(7), col(1), -HOLD, 15 * HOLD)
+    lin(col(8), col(1), -HOLD2, 15 * HOLD2)
+    lin(col(9), col(1), -HOLD, 15 * HOLD - 1)
+    lin(col(6), col(1), HOLD, K + 1 - 15 * HOLD)
+    lin(col(13), col(1), HOLD + 1, K + 1 - 15 * HOLD)
+    lin(col(14), col(1), 1 - HOLD2, 15 * HOLD2)
+    lin(col(15), col(1), 1 - HOLD, 15 * HOLD)
+    lin(col(10), col(1), -1.0, -0.5)
+    lin(col(0), col(2), -1.0, 0.0)
+    lin(v("inc"), kf, 512.0, -479.0)
+    lin(col(4), v("kx", 0, 1), 1.0 - TINY, -1.0)
+    lin(col(5), v("kx", 0, 1), M32 * TINY - M32, M32)
+
+    def picks():
+        quant(v("uq"), v("up"), v("ut"))
+        op("V", lambda: g.vector.tensor_copy(T.udq[:].bitcast(dt.uint32), T.uq[:].bitcast(dt.uint32).indirect(T.ul[:])), regs(v("uq"), v("ul")), regs(v("udq")))
+        cp(v("udp"), ind(v("up"), v("ul")))
+        iota(v("jj"), [[1, 520]], 0, -4)
+        gfill(v("xh"), 0)
+        gfill(v("tF"), 0)
+        iota(v("i16"), [[16, 20]], 0, 0)
+        gfill(v("neg"), -1)
+        gfill(v("nen", 0, 16), 0)
+        gfill(v("one"), 1)
+        iota(v("ib"), [[1, C]], 0, 0)
+        gfill(v("at", 4 * K, 512), 0)
+        iota(v("it"), [[1, E]], 0, 0)
+
+    def constants_0():
+        fill(v("tC", 576), 0.0)
+        fill(v("tE", 1088), 0.0)
+        fill(v("rs", 0, 1), 0.0)
+
+    def constants_1():
+        act(v("le1"), v("iz", 16, 16 + E), AF.Sign, bias=col(0))
+        act(v("spk"), v("le1"), AF.Abs, bias=-0.25)
+        act(v("ct"), v("spk"), AF.Relu, bias=1.5 / TINY - 0.5, scale=2.0 - 2.0 / TINY)
+        ts(v("wd"), v("jj"), 3.0, A.is_equal)
+        scan(v("kc", 1, E), v("inc", 1, E), v("kx", 0, E - 1), v("kc", 0, 1), A.add, A.max)
+        for b in range(4):
+            quant(v("eq", 128 * b, 128 * b + 128), v("ep", 128 * b, 128 * b + 128), v("wd", 3 - b, 515 - b))
+
+    def constants_2():
+        lin(v("cd"), kb, -18 * HOLD2, 17 * HOLD2)
+        lin(v("cc"), kb, -18 * HOLD, 17 * HOLD)
+        lin(v("iwd"), v("i16"), 1.0, col(14))
+        lin(v("iwh"), v("i16"), 1.0, col(15))
+        lin(v("iws"), v("i16", 0, 16), 1.0, col(13))
+
+    UD, GS = pair("udq", "udp", 0, 128), pair("gq", "gp", 0, 128)
+    TILE = {"A": 1, "B": 5, "C": 9, "D": 13, "E": 16}
+
+    def slot(c):
+        n = "ABCDE"[min((c - 1) // 4, 3) if c < 16 else 4]
+        return v("t" + n, c - TILE[n], 64 * c, 4)
+
+    def row_v(c, bank):
+        ts(slot(c), ps(bank, 0, 16 * c), v("hold", 16 * c + 15, 16 * c + 16), A.is_lt)
+
+    def sum_s(c):
+        act(v("junk", 8 * c * (c - 1), 8 * c * (c + 1)), slot(c), AF.Copy, acc=v("rs", c, c + 1))
+
+    def rows_s(cs, bank):
+        for k, c in enumerate(cs):
+            act(v("sg", C * k, C * k + 16 * c), ps(bank, 0, 16 * c), AF.Sign, bias=v("hold", 16 * c + 15, 16 * c + 16), scale=-1.0)
+        for k, c in enumerate(cs):
+            act(slot(c), v("sg", C * k, C * k + 16 * c), AF.Relu, acc=v("rs", c, c + 1))
+
+    def tile_mm(n, qcols, cols, start, stop):
+        quant(v("q" + n, 0, qcols), v("p" + n, 0, qcols), v("t" + n, 0, 4 * qcols))
+        mm(4, min(cols, HALF), GS, pair("q" + n, "p" + n, 0, min(cols, HALF)), start, stop)
+        if cols > HALF:
+            mm(7, E - HALF, GS, pair("q" + n, "p" + n, HALF, E), start, stop)
+
+    def halves(cut, end, banks, start):
+        for a, b, bank in ((0, cut, banks[0]), (cut, end, banks[1])):
+            quant(v("qF", a, b), v("pF", a, b), v("tF", 4 * a, 4 * b))
+            mm(bank, b - a, GS, pair("qF", "pF", a, b), start, True)
+
+    def hold(a, b, bank):
+        tt(v("val", a, b), ps(bank, a, b), v("m1", 16 + a, 16 + b), A.add)
+        scan(v("hold", a, b), v("c1", a, b), v("val", a, b), 0.0, A.add, A.min)
+
+    def catch(out, table, data, n, a=0):
+        scan(v(out, a, n), v(table, a, n), data, 0.0, A.add, A.min)
+        return v(out, 15, n, 16)
+
+    X = ["xt", "x1", "x2"]
+    for t in range(R):
+        qn, pn, last = "q%d" % t, "p%d" % t, t == R - 1
+        quant(v(qn, 0, 128), v(pn, 0, 128), v(X[t], 0, 512))
+        send(prev, qn, pn, 0, H, C, "arH%d" % t)
+        quant(v(qn, 128, C), v(pn, 128, C), v(X[t], 512, 1024))
+        if t == 0:
+            picks()
+        mm(0, C, UD, pair(qn, pn, 0, C))
+        mm(1, C, UD, pair(qn, pn, 0, C))
+        if t == 0:
+            constants_0()
+        d_own, d_halo = v("tD", 3, 4 * C, 4), v("tE", 4 * C, 4 * E, 4)
+        hold(HALF, C, 0)
+        rows_s(S_ROWS, 1)
+        hold(0, HALF, 0)
+        for c in range(15, 0, -1):
+            if c not in S_ROWS:
+                row_v(c, 0)
+                sum_s(c)
+        tt(d_own, ps(0, 0, C), v("hold", 0, C), A.is_le)
+        if t == 0:
+            ts(v("gt"), v("gi"), col(3), A.is_equal)
+            quant(v("gq"), v("gp"), v("gt"))
+        mm(2, E, UD, pair(qn, pn, 0, E))
+        mm(3, E, UD, pair(qn, pn, 0, E))
+        tile_mm("D", E if t == 0 else C, E, True, False)
+        tile_mm("C", 192, 192, False, False)
+        tile_mm("B", 128, 128, False, False)
+        tile_mm("A", 128, 128, False, False)
+        scan(v("dr", 0, C), v("k16", 0, C), d_own, 0.0, A.mult, A.add)
+        if t == 0:
+            constants_1()
+        hold(C, E, 2)
+        rows_s((19,), 3)
+        for c in (18, 17):
+            row_v(c, 2)
+            sum_s(c)
+        row_v(16, 2)
+        tt(d_halo, ps(2, C, E), v("hold", C, E), A.is_le)
+        op("V", lambda: g.vector.tensor_reduce(v("rs", 16, 17)[0], slot(16)[0], AxisListType.X, A.add), regs(slot(16)), regs(v("rs", 16, 17)))
+        scan(v("dr", C, E), v("k16", C, E), d_halo, 0.0, A.mult, A.add)
+        if t == 0:
+            fill(v("ct", 0, E, 16), 0.0)
+        tt(v("s1"), v("dr", 15, E, 16), v("rs"), A.add)
+        tile_mm("E", E, E, False, False)
+        ts(v("s2"), v("s1"), col(4), A.mult)
+        ts(v("xh", 0, E, 16), v("s2"), col(5), A.add, col(5), A.subtract)
+        tt(v("xh", E, 2 * E, 16), v("s2"), v("xh", 0, E, 16), A.subtract)
+        scan(v("tF", 0, 4 * E, 4), v("ct"), v("xh", 0, E), 0.0, A.mult, A.add)
+        scan(v("tF", 1, 4 * E, 4), v("ct"), v("xh", E, 2 * E), 0.0, A.mult, A.add)
+        halves(HALF, E, (4, 7), False)
+        if t == 0:
+            constants_2()
+        for b in range(4):
+            mm(b, E, pair("eq", "ep", 128 * b, 128 * b + 128), pair(qn, pn, 0, E))
+            act(v("ff", E * b, E * b + E), ps(b), AF.Copy)
+        tt(v("uu", 0, HALF), ps(4, 0, HALF), v("kc", 0, HALF), A.add)
+        tt(v("uu", HALF, E), ps(7, 0, E - HALF), v("kc", HALF, E), A.add)
+        mid = 32.0 * 192
+        ts(v("lt"), v("uu"), mid, A.is_gt)
+        ts(v("ng"), v("uu"), mid, A.is_lt, -1.0, A.mult)
+        ts(v("ne"), v("uu"), mid, A.is_equal, -1.0, A.mult)
+        scan(v("qf"), kf, v("lt"), 0.0, A.mult, A.add)
+        scan(rev("qb", 0, E), rev("kx", 16, 16 + E), rev("ng", 0, E), 0.0, A.mult, A.add)
+        scan(v("tF", 0, 4 * E, 4), v("qf"), v("ne"), 0.0, A.max, A.mult)
+        scan(v("tF", 1, 4 * E, 4), v("qb"), v("ne"), 0.0, A.min, A.mult)
+        halves(HALF, E, (5, 4), True)
+        mm(6, E, GS, pair("qF", "pF", 0, E))
+        act(v("nd"), ps(6), AF.Copy, scale=-1.0)
+        catch("capb", "cd", ps(5, 0, HALF), HALF)
+        c_pos = catch("capb", "cd", ps(4, 0, E - HALF), E, HALF)
+        scan(v("mx", 0, HALF), v("neg", 0, HALF), ps(5, 0, HALF), 0.0, A.add, A.max)
+        tt(v("f1"), c_pos, v("iwd"), A.add)
+        scan(v("mx", HALF, E), v("neg", HALF, E), ps(4, 0, E - HALF), v("mx", HALF - 1, HALF), A.add, A.max)
+        act(v("nen", 16, 16 + E), v("mx"), AF.Sign)
+        lin(v("cs"), v("nen", 16, 16 + E), HOLD, 2.0 - HOLD)
+        cp(v("lpos"), v("f1"))
+        cp(ind(v("vv"), v("lpos")), v("nd"))
+        scan(v("ra"), v("neg"), v("nen", 15, 15 + E), 0.0, A.add, A.mult)
+        act(v("ww"), v("vv", 0, C), AF.Abs)
+        act(v("junk", 0, C), v("ww"), AF.Sign, bias=col(10), acc=v("sc", 0, 1))
+        lin(v("sc", 1, 2), v("sc", 0, 1), -0.5, col(11))
+        c_o = catch("capv", "cd", v("vv", 0, C), C)
+        scan(rev("sm", 0, E), rev("cs", 0, E), rev("ra", 0, E), 0.0, A.add, A.max)
+        tt(v("f2"), c_o, v("iwd", 0, 16), A.add)
+        n = E if last else C
+        c_mir = catch("cap2", "cc", v("sm", 0, n), n)
+        cp(v("lo"), v("f2"))
+        act(v("yy", 0, C), ind(v("ff", 0, E), v("lo")), AF.Copy)
+        tt(v("mf", 0, n // 16), c_mir, v("iwh", 0, n // 16), A.add)
+        ts(v("nh"), v("ww"), col(1), A.is_equal, -1.0, A.mult)
+        cp(v("lmir", 0, n // 16), v("mf", 0, n // 16))
+        scan(v("npf"), v("one"), v("nh"), v("sc", 1, 2), A.mult, A.add)
+        act(v("vm"), ind(v("vv"), v("lmir", 0, 16)), AF.Copy)
+        for b in range(1, 4):
+            act(v("yy", C * b, C * b + C), ind(v("ff", E * b, E * b + E), v("lo")), AF.Copy)
+        scan(v("xx"), v("npf"), v("nh"), 0.0, A.min, A.mult)
+        M16 = 1.5 * 2.0 ** 27
+        ts(v("tF", 0, 4 * C, 4), v("xx"), M16, A.add, M16, A.subtract)
+        tt(v("tF", 1, 4 * C, 4), v("xx"), v("tF", 0, 4 * C, 4), A.subtract)
+        c_m = catch("capm", "cd", v("vm"), C)
+        halves(128, C, (7, 5), True)
+        tt(v("f4"), c_m, v("mf", 0, 16), A.add)
+        ts(v("lmm"), v("f4"), col(8), A.add)
+        for b in range(4):
+            act(v("gg", C * b, C * b + C), ind(v("ff", E * b, E * b + E), v("lmm")), AF.Copy, scale=-0.5)
+        catch("cap", "cc", ps(7, 0, 128), 128)
+        c_rk = catch("cap", "cc", ps(5, 0, 128), C, 128)
+        ts(v("lrk"), c_rk, col(9), A.add)
+        cp(ind(v("eb"), v("lrk")), v("ib"))
+        c_e = catch("cap3", "cc", v("eb", 0, K), K)
+        ts(v("f5"), c_rk, col(6), A.is_ge, HOLD, A.mult)
+        ts(v("le"), c_e, col(7), A.add)
+        tt(v("f6"), v("f5"), c_rk, A.add)
+        for b in range(4):
+            act(v("ge", K * b, K * b + K), ind(v("gg", C * b, C * b + C), v("le")), AF.Copy)
+        tt(v("f3"), v("f6"), v("iws"), A.min)
+        ts(v("lsel"), v("f3"), col(9), A.add)
+        for b in range(4):
+            tt(v("at", b, 4 * K, 4), ind(v("yy", C * b, C * b + C), v("le")), v("ge", K * b, K * b + K), A.add)
+        an, sn = "aq%d" % t, "ap%d" % t
+        quant(v(an, K, K + 128), v(sn, K, K + 128), v("at"))
+        send(far_to, an, sn, K, 2 * K, 0, "arA%d" % t)
+        W = C + K
+        for b in range(4):
+            act(v("a32", K * b, K * b + K), v("at", b, 4 * K, 4), AF.Copy, scale=32.0)
+        if t == 0:
+            quant(v("vq"), v("vp"), v("vt"))
+        for b in (2, 3, 0, 1):
+            tt(v("zw", W * b + K, W * b + W), v("yy", C * b, C * b + C), v("gg", C * b, C * b + C), A.add)
+            act(v("zw", W * b + K, W * b + W), v("zw", W * b + K, W * b + W), AF.Copy, scale=32.0)
+        if last:
+            tt(v("ob"), v("vv"), v("it"), A.add)
+        for b in (2, 3, 0, 1):
+            mm(b, 128, pair("wq", "wp", 128 * b, 128 * b + 128), pair(an, sn, 0, 128))
+        for b in (2, 3, 0, 1):
+            tt(v("zw", W * b, W * b + K), ps(b, 0, K), v("a32", K * b, K * b + K), A.add)
+        for b in (2, 3):
+            act(v(X[t + 1], b, 4 * C, 4), ind(v("zw", W * b, W * b + W), v("lsel")), AF.Copy, scale=0.03125)
+        for b in (0, 1):
+            ts(v(X[t + 1], b, 4 * C, 4), ind(v("zw", W * b, W * b + W), v("lsel")), 0.03125, A.mult)
+
+    act(v("lmo"), ind(v("ob"), v("lmir")), AF.Copy)
+    dma("Y", T.lm[:], T.lmo[0:128:16, :], regs(v("lmo")), [], "st0")
+    for k in range(2):
+        quant(v("q2", 128 * k, 128 * k + 128), v("p2", 128 * k, 128 * k + 128), v("x2", 512 * k, 512 * k + 512))
+        mm(4 + k, 128, pair("vq", "vp", 0, 128), pair("q2", "p2", 128 * k, 128 * k + 128))
+    dma("Y", T.oc[:], T.q2[:].bitcast(dt.uint8), regs(v("q2")), [], "st1")
+    cp(v("yo", 0, 128), ps(4, 0, 128))
+    cp(v("yo", 128, C), ps(5, 0, 128))
+    for k in range(4):
+        dma("S" if k % 2 else "Y", T.osc[4 * k:4 * k + 4, :], T.p2[32 * k:32 * k + 4, :], regs(v("p2")), [], "st%d" % (3 + k))
+    dma("S", T.y[:], T.yo[:], regs(v("yo")), [], "st2")
+    emit(g, T, ops, sent[0])
+
+
+def emit(g, T, ops, sent):
+    eng = {"V": g.vector, "S": g.scalar, "P": g.tensor, "G": g, "Y": g.sync}
+    deps = []
+    for i, o in enumerate(ops):
+        d = []
+        for j in range(i):
+            p = ops[j]
+            if o[0] == "P" and p[0] == "P":
+                continue
+            hit = any(_meet(a, b) for a in o[2] + o[3] for b in p[3]) or any(_meet(a, b) for a in o[3] for b in p[2])
+            if not hit and o[0] != p[0]:
+                hit = any(a[0].startswith("ps") and a[0] == b[0] for a in o[2] for b in p[2])
+            if hit and p[4] != "remote":
+                d.append(j)
+        deps.append(d)
+    known = {q: {} for q in eng}
+    clock, waits, marked = [], [], set()
+    for i, o in enumerate(ops):
+        if o[0] == "far":
+            clock.append({o[4]: i})
+            waits.append([])
+            continue
+        k, need = known[o[0]], {}
+        for j in deps[i]:
+            key = ops[j][4] or ops[j][0]
+            need[key] = max(need.get(key, -1), j)
+        w = []
+        for key, j in sorted(need.items(), key=lambda e: -e[1]):
+            if k.get(key, -1) < j:
+                w.append(j)
+                for kk, jj in clock[j].items():
+                    k[kk] = max(k.get(kk, -1), jj)
+        marked.update(w)
+        waits.append(w)
+        c = dict(k)
+        c[o[4] or o[0]] = i
+        clock.append(c)
+    count, value = {q: 0 for q in eng}, {}
+    for i, o in enumerate(ops):
+        if o[4] is None and i in marked:
+            count[o[0]] += 1
+            value[i] = count[o[0]]
+    for i, o in enumerate(ops):
+        if o[0] == "far":
+            continue
+        for j in waits[i]:
+            if ops[j][4] is None:
+                eng[o[0]].wait_ge(T.sem["s" + ops[j][0]], value[j])
+            else:
+                eng[o[0]].wait_ge(T.sem[ops[j][4]], ops[j][5])
+        ins = o[1]()
+        if o[4] is None:
+            if i in marked:
+                ins.then_inc(T.sem["s" + o[0]], 1)
+        elif o[4] != "remote":
+            ins.then_inc(T.sem[o[4]], 16)
+    g.wait_ge(T.sem.sent, sent)
+    for o in ops:
+        if o[4] is not None and o[4].startswith("st"):
+            g.wait_ge(T.sem[o[4]], 16)

@@ -31,7 +31,7 @@ SCRATCH = {
     "col": _sb(16, F32), "ul": _sb(8, U16), "uf": _sb(8, F32),
     "m1": _sb(E + 16, F32), "c1": _sb(E, BF), "k16": _sb(E, BF), "ct": _sb(E, BF), "le1": _sb(E, BF), "spk": _sb(E, BF), "inc": _sb(E, F32),
     "kc": _sb(E, F32), "it": _sb(E, F32), "ib": _sb(C, BF), "kx": _sb(E + 16, BF), "cc": _sb(E, BF), "cd": _sb(E, BF),
-    "one": _sb(C, BF), "neg": _sb(E, BF), "i16": _sb(20, F32), "iwh": _sb(20, F32), "iwd": _sb(20, F32), "iws": _sb(16, F32),
+    "lead": _sb(C, BF), "neg": _sb(E, BF), "i16": _sb(20, F32), "iwh": _sb(20, F32), "iwd": _sb(20, F32), "iws": _sb(16, F32),
     "val": _sb(E, F32), "hold": _sb(E, F32), "sg": _sb(2 * C, BF), "junk": _sb(16 * 200, BF), "rs": _sb(20, F32), "dr": _sb(E, BF),
     "s1": _sb(20, F32), "s2": _sb(20, F32), "xh": _sb(2 * E, BF), "uu": _sb(E, BF), "lt": _sb(E, BF), "ng": _sb(E, BF), "ne": _sb(E, BF),
     "qf": _sb(E, BF), "qb": _sb(E, BF), "cap": _sb(C, F32), "capb": _sb(E, BF), "capv": _sb(C, BF), "capm": _sb(C, BF), "cap2": _sb(E, F32),
@@ -195,7 +195,6 @@ def rank_program(g, core, T, topo):
     cp(v("ul"), v("uf"))
     fill(v("tA", 64), 0.0)
     fill(v("tB", 320), 0.0)
-    fill(col(11), -0.5 * C)
     lin(col(1), col(12), 0.5, 0.0)
     lin(col(3), col(2), 1.0 / 32, 0.0)
     act(v("kx"), v("m1"), AF.Sign)
@@ -203,12 +202,12 @@ def rank_program(g, core, T, topo):
     lin(v("kc", 0, 1), col(1), -32.0, 32.0 * 192 - 15.5)
     lin(col(7), col(1), -HOLD, 15 * HOLD)
     lin(col(8), col(1), -HOLD2, 15 * HOLD2)
-    lin(col(9), col(1), -HOLD, 15 * HOLD - 1)
-    lin(col(6), col(1), HOLD, K + 1 - 15 * HOLD)
-    lin(col(13), col(1), HOLD + 1, K + 1 - 15 * HOLD)
+    lin(col(9), col(1), -HOLD, 15 * HOLD - 4)
+    lin(col(6), col(1), HOLD, 4 * K + 4 - 15 * HOLD)
+    lin(col(13), col(1), HOLD + 4, 4 * K + 4 - 15 * HOLD)
     lin(col(14), col(1), 1 - HOLD2, 15 * HOLD2)
     lin(col(15), col(1), 1 - HOLD, 15 * HOLD)
-    lin(col(10), col(1), -1.0, -0.5)
+    lin(col(10), col(1), 1.0, 0.5)
     lin(col(0), col(2), -1.0, 0.0)
     lin(v("inc"), kf, 512.0, -479.0)
     lin(col(4), v("kx", 0, 1), 1.0 - TINY, -1.0)
@@ -224,15 +223,18 @@ def rank_program(g, core, T, topo):
         iota(v("i16"), [[16, 20]], 0, 0)
         gfill(v("neg"), -1)
         gfill(v("nen", 0, 16), 0)
-        gfill(v("one"), 1)
+        gfill(v("lead", 0, 1), -C)
+        gfill(v("lead", 1, C), 0)
         iota(v("ib"), [[1, C]], 0, 0)
         gfill(v("at", 4 * K, 512), 0)
         iota(v("it"), [[1, E]], 0, 0)
 
     def constants_0():
+        ts(v("gt"), v("gi"), col(3), A.is_equal)
         fill(v("tC", 576), 0.0)
         fill(v("tE", 1088), 0.0)
         fill(v("rs", 0, 1), 0.0)
+        quant(v("gq"), v("gp"), v("gt"))
 
     def constants_1():
         act(v("le1"), v("iz", 16, 16 + E), AF.Sign, bias=col(0))
@@ -248,7 +250,7 @@ def rank_program(g, core, T, topo):
         lin(v("cc"), kb, -18 * HOLD, 17 * HOLD)
         lin(v("iwd"), v("i16"), 1.0, col(14))
         lin(v("iwh"), v("i16"), 1.0, col(15))
-        lin(v("iws"), v("i16", 0, 16), 1.0, col(13))
+        lin(v("iws"), v("i16", 0, 16), 4.0, col(13))
 
     UD, GS = pair("udq", "udp", 0, 128), pair("gq", "gp", 0, 128)
     TILE = {"A": 1, "B": 5, "C": 9, "D": 13, "E": 16}
@@ -275,13 +277,14 @@ def rank_program(g, core, T, topo):
         if cols > HALF:
             mm(7, E - HALF, GS, pair("q" + n, "p" + n, HALF, E), start, stop)
 
-    def halves(cut, end, banks, start):
-        for a, b, bank in ((0, cut, banks[0]), (cut, end, banks[1])):
-            quant(v("qF", a, b), v("pF", a, b), v("tF", 4 * a, 4 * b))
-            mm(bank, b - a, GS, pair("qF", "pF", a, b), start, True)
+    def part(a, b, bank, start):
+        quant(v("qF", a, b), v("pF", a, b), v("tF", 4 * a, 4 * b))
+        mm(bank, b - a, GS, pair("qF", "pF", a, b), start, True)
 
-    def hold(a, b, bank):
+    def masked(a, b, bank):
         tt(v("val", a, b), ps(bank, a, b), v("m1", 16 + a, 16 + b), A.add)
+
+    def hold(a, b):
         scan(v("hold", a, b), v("c1", a, b), v("val", a, b), 0.0, A.add, A.min)
 
     def catch(out, table, data, n, a=0):
@@ -301,45 +304,48 @@ def rank_program(g, core, T, topo):
         if t == 0:
             constants_0()
         d_own, d_halo = v("tD", 3, 4 * C, 4), v("tE", 4 * C, 4 * E, 4)
-        hold(HALF, C, 0)
+        masked(HALF, C, 0)
+        masked(0, HALF, 0)
+        hold(HALF, C)
         rows_s(S_ROWS, 1)
-        hold(0, HALF, 0)
+        hold(0, HALF)
         for c in range(15, 0, -1):
             if c not in S_ROWS:
                 row_v(c, 0)
                 sum_s(c)
-        tt(d_own, ps(0, 0, C), v("hold", 0, C), A.is_le)
-        if t == 0:
-            ts(v("gt"), v("gi"), col(3), A.is_equal)
-            quant(v("gq"), v("gp"), v("gt"))
+            if c == 8:
+                tt(d_own, ps(0, 0, C), v("hold", 0, C), A.is_le)
         mm(2, E, UD, pair(qn, pn, 0, E))
         mm(3, E, UD, pair(qn, pn, 0, E))
         tile_mm("D", E if t == 0 else C, E, True, False)
         tile_mm("C", 192, 192, False, False)
-        tile_mm("B", 128, 128, False, False)
-        tile_mm("A", 128, 128, False, False)
         scan(v("dr", 0, C), v("k16", 0, C), d_own, 0.0, A.mult, A.add)
         if t == 0:
             constants_1()
-        hold(C, E, 2)
+        masked(C, E, 2)
+        tile_mm("B", 128, 128, False, False)
+        hold(C, E)
         rows_s((19,), 3)
-        for c in (18, 17):
-            row_v(c, 2)
-            sum_s(c)
+        row_v(18, 2)
+        sum_s(18)
         row_v(16, 2)
         tt(d_halo, ps(2, C, E), v("hold", C, E), A.is_le)
+        row_v(17, 2)
+        sum_s(17)
         op("V", lambda: g.vector.tensor_reduce(v("rs", 16, 17)[0], slot(16)[0], AxisListType.X, A.add), regs(slot(16)), regs(v("rs", 16, 17)))
         scan(v("dr", C, E), v("k16", C, E), d_halo, 0.0, A.mult, A.add)
         if t == 0:
             fill(v("ct", 0, E, 16), 0.0)
-        tt(v("s1"), v("dr", 15, E, 16), v("rs"), A.add)
         tile_mm("E", E, E, False, False)
+        tt(v("s1"), v("dr", 15, E, 16), v("rs"), A.add)
         ts(v("s2"), v("s1"), col(4), A.mult)
         ts(v("xh", 0, E, 16), v("s2"), col(5), A.add, col(5), A.subtract)
+        tile_mm("A", 128, 128, False, False)
         tt(v("xh", E, 2 * E, 16), v("s2"), v("xh", 0, E, 16), A.subtract)
         scan(v("tF", 0, 4 * E, 4), v("ct"), v("xh", 0, E), 0.0, A.mult, A.add)
         scan(v("tF", 1, 4 * E, 4), v("ct"), v("xh", E, 2 * E), 0.0, A.mult, A.add)
-        halves(HALF, E, (4, 7), False)
+        part(0, HALF, 4, False)
+        part(HALF, E, 7, False)
         if t == 0:
             constants_2()
         for b in range(4):
@@ -355,7 +361,8 @@ def rank_program(g, core, T, topo):
         scan(rev("qb", 0, E), rev("kx", 16, 16 + E), rev("ng", 0, E), 0.0, A.mult, A.add)
         scan(v("tF", 0, 4 * E, 4), v("qf"), v("ne"), 0.0, A.max, A.mult)
         scan(v("tF", 1, 4 * E, 4), v("qb"), v("ne"), 0.0, A.min, A.mult)
-        halves(HALF, E, (5, 4), True)
+        part(0, HALF, 5, True)
+        part(HALF, E, 4, True)
         mm(6, E, GS, pair("qF", "pF", 0, E))
         act(v("nd"), ps(6), AF.Copy, scale=-1.0)
         catch("capb", "cd", ps(5, 0, HALF), HALF)
@@ -367,46 +374,47 @@ def rank_program(g, core, T, topo):
         lin(v("cs"), v("nen", 16, 16 + E), HOLD, 2.0 - HOLD)
         cp(v("lpos"), v("f1"))
         cp(ind(v("vv"), v("lpos")), v("nd"))
-        scan(v("ra"), v("neg"), v("nen", 15, 15 + E), 0.0, A.add, A.mult)
         act(v("ww"), v("vv", 0, C), AF.Abs)
-        act(v("junk", 0, C), v("ww"), AF.Sign, bias=col(10), acc=v("sc", 0, 1))
-        lin(v("sc", 1, 2), v("sc", 0, 1), -0.5, col(11))
+        act(v("junk", 0, C), v("ww"), AF.Sign, bias=col(10), scale=-1.0, acc=v("sc", 0, 1))
+        scan(v("ra"), v("neg"), v("nen", 15, 15 + E), 0.0, A.add, A.mult)
         c_o = catch("capv", "cd", v("vv", 0, C), C)
         scan(rev("sm", 0, E), rev("cs", 0, E), rev("ra", 0, E), 0.0, A.add, A.max)
         tt(v("f2"), c_o, v("iwd", 0, 16), A.add)
+        ts(v("nh"), v("ww"), col(1), A.is_equal, -2.0, A.mult)
+        cp(v("lo"), v("f2"))
+        for b in range(2):
+            act(v("yy", C * b, C * b + C), ind(v("ff", E * b, E * b + E), v("lo")), AF.Copy)
         n = E if last else C
         c_mir = catch("cap2", "cc", v("sm", 0, n), n)
-        cp(v("lo"), v("f2"))
-        act(v("yy", 0, C), ind(v("ff", 0, E), v("lo")), AF.Copy)
+        scan(v("npf"), v("lead"), v("nh"), v("sc", 0, 1), A.add, A.add)
         tt(v("mf", 0, n // 16), c_mir, v("iwh", 0, n // 16), A.add)
-        ts(v("nh"), v("ww"), col(1), A.is_equal, -1.0, A.mult)
-        cp(v("lmir", 0, n // 16), v("mf", 0, n // 16))
-        scan(v("npf"), v("one"), v("nh"), v("sc", 1, 2), A.mult, A.add)
-        act(v("vm"), ind(v("vv"), v("lmir", 0, 16)), AF.Copy)
-        for b in range(1, 4):
-            act(v("yy", C * b, C * b + C), ind(v("ff", E * b, E * b + E), v("lo")), AF.Copy)
         scan(v("xx"), v("npf"), v("nh"), 0.0, A.min, A.mult)
-        M16 = 1.5 * 2.0 ** 27
-        ts(v("tF", 0, 4 * C, 4), v("xx"), M16, A.add, M16, A.subtract)
+        cp(v("lmir", 0, n // 16), v("mf", 0, n // 16))
+        act(v("vm"), ind(v("vv"), v("lmir", 0, 16)), AF.Copy)
+        for b in range(2, 4):
+            act(v("yy", C * b, C * b + C), ind(v("ff", E * b, E * b + E), v("lo")), AF.Copy)
+        M64 = 1.5 * 2.0 ** 29
+        ts(v("tF", 0, 4 * C, 4), v("xx"), M64, A.add, M64, A.subtract)
         tt(v("tF", 1, 4 * C, 4), v("xx"), v("tF", 0, 4 * C, 4), A.subtract)
         c_m = catch("capm", "cd", v("vm"), C)
-        halves(128, C, (7, 5), True)
+        part(0, 128, 7, True)
         tt(v("f4"), c_m, v("mf", 0, 16), A.add)
+        part(128, C, 5, True)
         ts(v("lmm"), v("f4"), col(8), A.add)
+        catch("cap", "cc", ps(7, 0, 128), 128)
         for b in range(4):
             act(v("gg", C * b, C * b + C), ind(v("ff", E * b, E * b + E), v("lmm")), AF.Copy, scale=-0.5)
-        catch("cap", "cc", ps(7, 0, 128), 128)
         c_rk = catch("cap", "cc", ps(5, 0, 128), C, 128)
-        ts(v("lrk"), c_rk, col(9), A.add)
+        ts(v("lrk"), c_rk, col(9), A.add, 0.25, A.mult)
+        ts(v("f5"), c_rk, col(6), A.is_ge, 2 * HOLD, A.mult)
         cp(ind(v("eb"), v("lrk")), v("ib"))
         c_e = catch("cap3", "cc", v("eb", 0, K), K)
-        ts(v("f5"), c_rk, col(6), A.is_ge, HOLD, A.mult)
         ts(v("le"), c_e, col(7), A.add)
         tt(v("f6"), v("f5"), c_rk, A.add)
+        tt(v("f3"), v("f6"), v("iws"), A.min)
+        ts(v("lsel"), v("f3"), col(9), A.add, 0.25, A.mult)
         for b in range(4):
             act(v("ge", K * b, K * b + K), ind(v("gg", C * b, C * b + C), v("le")), AF.Copy)
-        tt(v("f3"), v("f6"), v("iws"), A.min)
-        ts(v("lsel"), v("f3"), col(9), A.add)
         for b in range(4):
             tt(v("at", b, 4 * K, 4), ind(v("yy", C * b, C * b + C), v("le")), v("ge", K * b, K * b + K), A.add)
         an, sn = "aq%d" % t, "ap%d" % t
@@ -428,8 +436,10 @@ def rank_program(g, core, T, topo):
             tt(v("zw", W * b, W * b + K), ps(b, 0, K), v("a32", K * b, K * b + K), A.add)
         for b in (2, 3):
             act(v(X[t + 1], b, 4 * C, 4), ind(v("zw", W * b, W * b + W), v("lsel")), AF.Copy, scale=0.03125)
-        for b in (0, 1):
-            ts(v(X[t + 1], b, 4 * C, 4), ind(v("zw", W * b, W * b + W), v("lsel")), 0.03125, A.mult)
+        cut = 10
+        act(v(X[t + 1], 1 + 64 * cut, 4 * C, 4), ind(v("zw", W, 2 * W), v("lsel", cut, 16)), AF.Copy, scale=0.03125)
+        ts(v(X[t + 1], 0, 4 * C, 4), ind(v("zw", 0, W), v("lsel")), 0.03125, A.mult)
+        ts(v(X[t + 1], 1, 64 * cut, 4), ind(v("zw", W, 2 * W), v("lsel", 0, cut)), 0.03125, A.mult)
 
     act(v("lmo"), ind(v("ob"), v("lmir")), AF.Copy)
     dma("Y", T.lm[:], T.lmo[0:128:16, :], regs(v("lmo")), [], "st0")

@@ -5,11 +5,15 @@ AF = ActivationFunctionType
 C, H, E, K, J, R = 256, 64, 320, 96, 3, 2
 BIG = 2.0 ** 96
 HOLD = 1024.0
-HOLD2 = 16.0
+LIFT, DROP = 512.0, 1152.0
 TINY = 2.0 ** -18
-CODE, PLANE, BF, F16, F32, U16 = "float8_e4m3fn_x4", "uint8", "bfloat16", "float16", "float32", "uint16"
-HALF = 192
-S_ROWS = (15, 14)
+CODE, PLANE, BF, F16, F32, U16, I32 = "float8_e4m3fn_x4", "uint8", "bfloat16", "float16", "float32", "uint16", "int32"
+S_ROWS, V_SUMS = (17, 16, 15, 14, 13), 18
+FAR_ROWS, STEP = (17, 16, 19, 18), 304
+TILE = {"D": (13, 0), "C": (9, 320), "B": (5, 608), "A": (1, 736), "E": (16, 864)}
+G_CUT, A_CUTS = 56, (0, 4, 14, 24)
+W = C + K
+HF = E // 2
 
 
 def _sb(n, d):
@@ -20,31 +24,32 @@ SCRATCH = {
     "xt": _sb(1024, BF), "ut": _sb(512, BF), "vt": _sb(512, BF), "x1": _sb(1024, BF), "x2": _sb(1024, BF),
     "wq": _sb(512, CODE), "wp": _sb(512, PLANE), "uq": _sb(128, CODE), "up": _sb(128, PLANE),
     "udq": _sb(128, CODE), "udp": _sb(128, PLANE), "vq": _sb(128, CODE), "vp": _sb(128, PLANE),
-    "eq": _sb(512, CODE), "ep": _sb(512, PLANE), "gq": _sb(128, CODE), "gp": _sb(128, PLANE),
+    "eq": _sb(512, CODE), "ep": _sb(512, PLANE), "gq": _sb(384, CODE), "gp": _sb(384, PLANE),
     "q0": _sb(E, CODE), "p0": _sb(E, PLANE), "q1": _sb(E, CODE), "p1": _sb(E, PLANE), "q2": _sb(C, CODE), "p2": _sb(C, PLANE),
     "aq0": _sb(K + 128, CODE), "ap0": _sb(K + 128, PLANE), "aq1": _sb(K + 128, CODE), "ap1": _sb(K + 128, PLANE),
-    "tA": _sb(512, BF), "tB": _sb(512, BF), "tC": _sb(768, BF), "tD": _sb(1280, BF), "tE": _sb(1280, BF), "tF": _sb(1280, BF),
-    "qA": _sb(128, CODE), "qB": _sb(128, CODE), "qC": _sb(192, CODE), "qD": _sb(E, CODE), "qE": _sb(E, CODE), "qF": _sb(E, CODE),
-    "pA": _sb(128, PLANE), "pB": _sb(128, PLANE), "pC": _sb(192, PLANE), "pD": _sb(E, PLANE), "pE": _sb(E, PLANE), "pF": _sb(E, PLANE),
+    "tl": _sb(4 * 1184, BF), "ql": _sb(1184, CODE), "pl": _sb(1184, PLANE),
+    "tF": _sb(4 * HF, BF), "qF": _sb(HF, CODE), "pF": _sb(HF, PLANE), "tG": _sb(4 * HF, BF), "qG": _sb(HF, CODE), "pG": _sb(HF, PLANE),
     "at": _sb(512, BF), "a32": _sb(4 * K, BF),
-    "iz": _sb(E + 16, F32), "jj": _sb(520, BF), "wd": _sb(520, BF), "gi": _sb(512, BF), "gt": _sb(512, BF),
-    "col": _sb(16, F32), "ul": _sb(8, U16), "uf": _sb(8, F32),
-    "m1": _sb(E + 16, F32), "c1": _sb(E, BF), "k16": _sb(E, BF), "ct": _sb(E, BF), "le1": _sb(E, BF), "spk": _sb(E, BF), "inc": _sb(E, F32),
-    "kc": _sb(E, F32), "it": _sb(E, F32), "ib": _sb(C, BF), "kx": _sb(E + 16, BF), "cc": _sb(E, BF), "cd": _sb(E, BF),
-    "lead": _sb(C, BF), "neg": _sb(E, BF), "i16": _sb(20, F32), "iwh": _sb(20, F32), "iwd": _sb(20, F32), "iws": _sb(16, F32),
-    "val": _sb(E, F32), "hold": _sb(E, F32), "sg": _sb(2 * C, BF), "junk": _sb(16 * 200, BF), "rs": _sb(20, F32), "dr": _sb(E, BF),
-    "s1": _sb(20, F32), "s2": _sb(20, F32), "xh": _sb(2 * E, BF), "uu": _sb(E, BF), "lt": _sb(E, BF), "ng": _sb(E, BF), "ne": _sb(E, BF),
-    "qf": _sb(E, BF), "qb": _sb(E, BF), "cap": _sb(C, F32), "capb": _sb(E, BF), "capv": _sb(C, BF), "capm": _sb(C, BF), "cap2": _sb(E, F32),
-    "cap3": _sb(K, F32), "nd": _sb(E, BF), "vv": _sb(E, BF),
-    "mx": _sb(E, BF), "nen": _sb(E + 16, BF), "cs": _sb(E, BF), "ra": _sb(E, F16), "sm": _sb(E, F16), "vm": _sb(C, BF), "ww": _sb(C, BF), "sc": _sb(2, F32),
-    "nh": _sb(C, BF), "npf": _sb(C, BF), "xx": _sb(C, BF), "eb": _sb(C, BF),
-    "f1": _sb(20, F32), "f2": _sb(16, F32), "f3": _sb(16, F32), "f4": _sb(16, F32), "f5": _sb(16, F32), "f6": _sb(16, F32), "mf": _sb(20, F32),
-    "lpos": _sb(20, U16), "lo": _sb(16, U16), "lmir": _sb(20, U16), "lmm": _sb(16, U16), "lrk": _sb(16, U16), "le": _sb(6, U16), "lsel": _sb(16, U16),
-    "ff": _sb(4 * E, BF), "yy": _sb(4 * C, BF), "gg": _sb(4 * C, BF), "ge": _sb(4 * K, BF), "zw": _sb(4 * (C + K), BF),
+    "tm": _sb(E + 16, BF), "ih": _sb(E, F16), "wd": _sb(520, BF), "gi": _sb(512, BF), "gt": _sb(1040, BF),
+    "col": _sb(16, F32), "pi": _sb(8, I32), "ul": _sb(8, U16), "uf": _sb(16, F32), "lt_": _sb(2, U16),
+    "m1": _sb(E + 16, BF), "c1": _sb(E, BF), "k16": _sb(544, BF), "ct": _sb(HF, BF), "le1": _sb(HF, BF), "spk": _sb(HF, BF),
+    "inc": _sb(E, F32), "kn": _sb(E, F32), "it": _sb(E, F32), "ib": _sb(C, BF), "kx": _sb(E + 16, BF), "cc": _sb(K, BF),
+    "eqa": _sb(E, BF), "t1": _sb(E, F16), "sp": _sb(E, F16), "tab": _sb(E, F16),
+    "tm4": _sb(E + 4, BF), "k4a": _sb(E + 4, BF), "k4": _sb(E + 4, BF), "eq4": _sb(E, BF), "t14": _sb(E, F16), "sp4": _sb(E, F16), "tab4": _sb(E, F16),
+    "lead": _sb(C, BF), "neg": _sb(E, BF), "one": _sb(E, BF), "iws": _sb(16, F32),
+    "val": _sb(E, F32), "hold": _sb(E, F32), "sg": _sb(6 * E, BF), "junk": _sb(16 * 210, BF), "rs": _sb(20, F32), "dr": _sb(E, BF),
+    "s1": _sb(20 * STEP, F16), "s2": _sb(20, F32), "xh": _sb(2 * E, BF),
+    "uu": _sb(E, BF), "lt": _sb(E, BF), "ng": _sb(E, BF), "ne": _sb(E, BF), "na": _sb(E, BF), "qf": _sb(E, BF), "qb": _sb(E, BF),
+    "capb": _sb(E, F16), "capv": _sb(E, F16), "cap2": _sb(E, F16), "cap3": _sb(K, F32), "nd": _sb(E, BF), "vv": _sb(E, BF),
+    "mx": _sb(E, BF), "nen": _sb(E + 16, BF), "cs": _sb(E, BF), "ra": _sb(E, F16), "sm": _sb(E, F16), "ww": _sb(C, BF), "sc": _sb(2, F32),
+    "nh": _sb(C, BF), "npf": _sb(C, BF), "xx": _sb(C + 32, BF), "tr": _sb(544, BF), "su": _sb(544, BF), "eb": _sb(C, BF),
+    "f3": _sb(16, F32), "f4": _sb(16, F32), "f5": _sb(16, F32), "f6": _sb(16, F32),
+    "lpos": _sb(20, U16), "lo": _sb(80, U16), "lmir": _sb(64, U16), "lrk": _sb(16, U16), "le": _sb(24, U16), "lsel": _sb(16, U16),
+    "ff": _sb(4 * E, BF), "yy": _sb(4 * E, BF), "gg": _sb(4 * C, BF), "ge": _sb(4 * K, BF), "zw": _sb(4 * W, BF),
     "lmo": _sb(E, F32), "ob": _sb(E, F32), "yo": _sb(C, F32),
 }
 PART = {}
-for _n, _names in (("cf", "uf i16 iwh iwd iws"), ("df", "f1 f2 f3 f4 f5 f6 mf s1 s2 rs sc"), ("ls", "lpos lo lmir lmm lrk le lsel")):
+for _n, _names in (("cf", "uf iws"), ("df", "f3 f4 f5 f6 s2 rs sc"), ("ls", "lpos lo lmir lrk le lsel"), ("lc", "ul lt_")):
     _at = 0
     for _k in _names.split():
         _w, (_p, _c), _d = SCRATCH.pop(_k)
@@ -53,8 +58,9 @@ for _n, _names in (("cf", "uf i16 iwh iwd iws"), ("df", "f1 f2 f3 f4 f5 f6 mf s1
     SCRATCH[_n] = _sb(_at, _d)
 for _b in range(8):
     SCRATCH["ps%d" % _b] = ("psum", [128, 512], F32)
-SEMAPHORES = ["sV", "sS", "sP", "sG", "ldx", "ldu", "ldv", "ldw", "ldp", "arH0", "arH1", "arA0", "arA1", "sent",
+SEMAPHORES = ["sV", "sS", "sP", "sG", "ldx0", "ldx1", "ldu", "ldv", "ldw", "ldp", "arH0", "arH1", "arA0", "arA1", "sent",
               "st0", "st1", "st2", "st3", "st4", "st5", "st6"]
+CYC, WAKE, ISSUE, FIRST, FLIGHT, LOAD = 0.83, 150.0, 300.0, 1000.0, 2200.0, 1700.0
 
 
 def _meet(a, b):
@@ -93,54 +99,71 @@ def rank_program(g, core, T, topo):
     def regs(*xs):
         return [r for x in xs if isinstance(x, tuple) for r in x[1:]]
 
-    def op(q, call, reads, writes, sem=None, count=16):
-        ops.append([q, call, reads, writes, sem, count])
+    def num(x):
+        n, a, b, s = x[-1]
+        return 16 * (b - a) if len(x) == 3 else -(-(b - a) // s)
+
+    def cost(out, *ins, rate=None):
+        if len(out) == 3:
+            return 50 + 3.5 * CYC * num(out)
+        if len(ins[0]) == 3:
+            return 60 + 1.5 * CYC * num(out)
+        if rate is None:
+            rate = 0.5 if all(SCRATCH[x[1][0]][2] in (BF, F16, U16) for x in (out,) + ins) else 1.0
+        return 25 + CYC * max(64, rate * num(ins[0]))
+
+    def op(q, call, reads, writes, busy, sem=None, count=16, done=None):
+        ops.append([q, call, reads, writes, sem, count, busy, busy if done is None else done])
 
     def ts(out, in0, s1, o0, s2=None, o1=None):
         if o1 is None:
-            op("V", lambda: g.vector.tensor_scalar(out[0], in0[0], ap(s1), None, o0), regs(in0, s1), regs(out))
+            op("V", lambda: g.vector.tensor_scalar(out[0], in0[0], ap(s1), None, o0), regs(in0, s1), regs(out), cost(out, in0))
         else:
-            op("V", lambda: g.vector.tensor_scalar(out[0], in0[0], ap(s1), ap(s2), o0, o1), regs(in0, s1, s2), regs(out))
+            op("V", lambda: g.vector.tensor_scalar(out[0], in0[0], ap(s1), ap(s2), o0, o1), regs(in0, s1, s2), regs(out), cost(out, in0))
 
     def tt(out, a, b, o):
-        op("V", lambda: g.vector.tensor_tensor(out[0], a[0], b[0], o), regs(a, b), regs(out))
+        both = not a[1][0].startswith("ps")
+        op("V", lambda: g.vector.tensor_tensor(out[0], a[0], b[0], o), regs(a, b), regs(out), cost(out, a, rate=2.0 if both else 1.0))
 
     def cp(out, a):
-        op("V", lambda: g.vector.tensor_copy(out[0], a[0]), regs(a) + list(out[2:]), [out[1]])
+        op("V", lambda: g.vector.tensor_copy(out[0], a[0]), regs(a) + list(out[2:]), [out[1]], cost(out, a))
 
     def scan(out, d0, d1, init, o0, o1):
-        op("V", lambda: g.vector.tensor_tensor_scan(out[0], d0[0], d1[0], ap(init), o0, o1), regs(d0, d1, init), regs(out))
+        op("V", lambda: g.vector.tensor_tensor_scan(out[0], d0[0], d1[0], ap(init), o0, o1), regs(d0, d1, init), regs(out), cost(out, d0, d1))
+
+    def turn(out, a):
+        op("V", lambda: g.vector.transpose(out[0], a[0]), regs(a), regs(out), cost(out, a))
 
     def fill(out, c):
-        op("V", lambda: g.vector.memset(out[0], c), [], regs(out))
+        op("V", lambda: g.vector.memset(out[0], c), [], regs(out), cost(out, out))
 
     def quant(q, p, t):
-        op("V", lambda: g.vector.quantize_mx(q[0], p[0], t[0]), regs(t), regs(q, p))
+        op("V", lambda: g.vector.quantize_mx(q[0], p[0], t[0]), regs(t), regs(q, p), 37 + 0.22 * num(t))
 
     def act(out, a, f, bias=None, scale=1.0, acc=None):
-        kw = {"scale": scale}
+        kw = {} if scale == 1.0 else {"scale": ap(scale)}
         if bias is not None:
             kw["bias"] = ap(bias)
         if acc is not None:
             kw["accum_out"] = acc[0]
-        op("S", lambda: g.scalar.activation(out[0], a[0], f, **kw), regs(a, bias), regs(out, acc))
+        op("S", lambda: g.scalar.activation(out[0], a[0], f, **kw), regs(a, bias, scale), regs(out, acc), cost(out, a, rate=1.0) + (20 if acc else 0))
 
     def lin(out, a, scale, bias):
         act(out, a, AF.Identity, bias=bias, scale=scale)
 
     def mm(bank, n, w, x, start=True, stop=True):
         out = v("ps%d" % bank, 0, n)
-        op("P", lambda: g.tensor.matmul_mx(out[0], w[0][0], w[1][0], x[0][0], x[1][0], start, stop), regs(*w, *x), regs(out))
+        op("P", lambda: g.tensor.matmul_mx(out[0], w[0][0], w[1][0], x[0][0], x[1][0], start, stop), regs(*w, *x), regs(out), 0.63 * (n + 16))
 
     def iota(out, pat, base, cm):
-        op("G", lambda: g.iota(out[0], pat, base, cm, allow_small_or_imprecise_dtypes=True), [], regs(out))
+        op("G", lambda: g.iota(out[0], pat, base, cm, allow_small_or_imprecise_dtypes=True), [], regs(out), 130 + 2 * CYC * num(out))
 
     def gfill(out, c):
         iota(out, [[0, out[1][2] - out[1][1]]], c, 0)
 
     def dma(q, out, in_, reads, writes, sem):
         e = g.sync if q == "Y" else g.scalar
-        op(q, lambda: e.dma_start(out, in_), reads, writes, sem)
+        op(q, lambda: e.dma_start(out, in_), reads, writes, 60, sem, done=LOAD)
 
     sent = [0]
 
@@ -150,12 +173,12 @@ def rank_program(g, core, T, topo):
         n = len(topo.engines(core, dst))
         so, si = v(pn, at, at + b - a), v(pn, a, b)
         co, ci = v(qn, at, at + b - a), v(qn, a, b)
-        op("G", lambda: g.remote_dma(co[0].bitcast(dt.uint8), ci[0].bitcast(dt.uint8), T.sem[sem], T.sem.sent, pid, rid, mask), regs(ci), [], "remote")
-        op("G", lambda: g.remote_dma(so[0], si[0], T.sem[sem], T.sem.sent, pid, rid, mask), regs(si), [], "remote")
+        op("G", lambda: g.remote_dma(co[0].bitcast(dt.uint8), ci[0].bitcast(dt.uint8), T.sem[sem], T.sem.sent, pid, rid, mask), regs(ci), [(sem, 0, 1, 1)], ISSUE + (0 if sent[0] else FIRST), "remote")
+        op("G", lambda: g.remote_dma(so[0], si[0], T.sem[sem], T.sem.sent, pid, rid, mask), regs(si), [(sem, 1, 2, 1)], ISSUE, "remote")
         sent[0] += 2 * n
 
     def lands(src, qn, pn, a, b, sem):
-        op("far", None, [], regs(v(qn, a, b), v(pn, a, b)), sem, 2 * len(topo.engines(src, core)))
+        op("far", None, [(sem, 0, 2, 1)], regs(v(qn, a, b), v(pn, a, b)), 0, sem, 2 * len(topo.engines(src, core)), done=FLIGHT)
 
     def ps(b, a=0, e=E):
         return v("ps%d" % b, a, e)
@@ -169,335 +192,373 @@ def rank_program(g, core, T, topo):
     prev, nxt = T.cores[(rank - 1) % N], T.cores[(rank + 1) % N]
     far_to, far_from = T.cores[(rank + J) % N], T.cores[(rank - J) % N]
 
-    dma("Y", T.xt[:], T.x[:], [], regs(v("xt")), "ldx")
+    dma("Y", T.xt[:, 0:512], T.x[:, 0:512], [], regs(v("xt", 0, 512)), "ldx0")
     dma("S", T.ut[:], T.u[:], [], regs(v("ut")), "ldu")
-    for t in range(R):
-        lands(nxt, "q%d" % t, "p%d" % t, C, E, "arH%d" % t)
-        lands(far_from, "aq%d" % t, "ap%d" % t, 0, K, "arA%d" % t)
-    behind = regs(v("q0", C, E))
-    dma("Y", T.wq[:].bitcast(dt.uint8), T.wc[:], behind, regs(v("wq")), "ldw")
-    dma("Y", T.wp[:], T.ws[:], behind, regs(v("wp")), "ldp")
-    dma("Y", T.vt[:], T.v[:], behind, regs(v("vt")), "ldv")
+    dma("Y", T.xt[:, 512:1024], T.x[:, 512:1024], [], regs(v("xt", 512, 1024)), "ldx1")
 
-    iota(col(0), [[0, 1]], -15, 2)
-    iota(v("iz"), [[0, 21], [-2, 16]], 0, 2)
-    iota(v("uf"), [[16, 8]], 0, 0)
-    iota(v("gi"), [[1, 8], [0, 64]], 0, 0)
-    M32 = 1.5 * 2.0 ** 28
-    fill(v("c1"), 0.0)
-    fill(v("k16"), 1.0)
-    ts(col(2), col(0), M32, A.add, M32, A.subtract)
-    fill(v("c1", 0, E, 16), 2 * BIG)
-    fill(v("k16", 0, E, 16), 0.0)
-    fill(v("tD", 832), 0.0)
-    ts(col(12), col(0), col(2), A.subtract, 15.0, A.add)
-    ts(v("m1"), v("iz"), col(2), A.not_equal, BIG, A.mult)
-    cp(v("ul"), v("uf"))
-    fill(v("tA", 64), 0.0)
-    fill(v("tB", 320), 0.0)
-    lin(col(1), col(12), 0.5, 0.0)
-    lin(col(3), col(2), 1.0 / 32, 0.0)
+    ca, cg, cpar = col(0), col(1), col(2)
+    iota(v("pi", 0, 1), [[0, 1]], 0, 1)
+    iota(v("pi", 1, 2), [[0, 1]], 0, 17)
+    ts(v("pi", 4, 5), v("pi", 0, 1), 15, A.bitwise_and)
+    ts(v("pi", 5, 6), v("pi", 0, 1), 4, A.logical_shift_right)
+    ts(v("pi", 6, 7), v("pi", 1, 2), 4, A.logical_shift_right, 1, A.bitwise_and)
+    ts(v("pi", 7, 8), v("pi", 0, 1), 2, A.logical_shift_right, 3, A.bitwise_and)
+    cp(v("col", 0, 4), v("pi", 4, 8))
+    ts(v("pi", 2, 3), v("pi", 0, 1), 3, A.bitwise_and)
+    cp(col(11), v("pi", 2, 3))
+    iota(v("tm"), [[0, 21], [1, 16]], 0, 0)
+    iota(v("uf"), [[16, 16]], 0, 0)
+    iota(v("gi"), [[1, 8], [0, 32], [100, 2]], 0, 0)
+    cp(v("ul"), v("uf", 0, 8))
+    ts(v("m1"), v("tm"), ca, A.not_equal, BIG, A.mult)
     act(v("kx"), v("m1"), AF.Sign)
-    kb, kf = v("kx", 16, 16 + E), v("kx", 15, 15 + E)
-    lin(v("kc", 0, 1), col(1), -32.0, 32.0 * 192 - 15.5)
-    lin(col(7), col(1), -HOLD, 15 * HOLD)
-    lin(col(8), col(1), -HOLD2, 15 * HOLD2)
-    lin(col(9), col(1), -HOLD, 15 * HOLD - 4)
-    lin(col(6), col(1), HOLD, 4 * K + 4 - 15 * HOLD)
-    lin(col(13), col(1), HOLD + 4, 4 * K + 4 - 15 * HOLD)
-    lin(col(14), col(1), 1 - HOLD2, 15 * HOLD2)
-    lin(col(15), col(1), 1 - HOLD, 15 * HOLD)
-    lin(col(10), col(1), 1.0, 0.5)
-    lin(col(0), col(2), -1.0, 0.0)
-    lin(v("inc"), kf, 512.0, -479.0)
+    kb, kf = v("kx", 0, E), v("kx", 15, 15 + E)
+    act(v("k16", 0, E), v("tm", 0, E), AF.Sign)
+    act(v("k16", E, 544), v("tm", 0, 544 - E), AF.Sign)
+    lin(v("c1"), v("k16", 0, E), -2 * BIG, 2 * BIG)
+    for a, b in ((208, 320), (464, 608), (688, 864), (1136, 1184)):
+        fill(v("tl", 4 * a, 4 * b), 0.0)
+    fill(v("rs", 0, 1), 0.0)
+    M32 = 1.5 * 2.0 ** 28
     lin(col(4), v("kx", 0, 1), 1.0 - TINY, -1.0)
     lin(col(5), v("kx", 0, 1), M32 * TINY - M32, M32)
+    lin(col(6), v("kx", 0, 1), -DROP, DROP - LIFT)
+    lin(col(9), cpar, 272.0, 15.0)
+    lin(col(10), ca, 1.0, 0.5)
+    ts(v("lt_", 0, 1), ca, 16.0, A.mult, col(9), A.add)
+    ts(v("iws"), v("uf"), ca, A.add, float(K), A.add)
+    ts(v("gt", 0, 512, 2), v("gi", 0, 512, 2), cg, A.is_equal)
+    ts(v("gt", 1, 512, 2), v("gi", 0, 512, 2), cg, A.is_equal)
+    fill(v("gt", 512, 513), 0.0)
+    ts(v("gt", 513, 1025), v("gi"), cg, A.is_equal)
+    for k, a in enumerate((0, 513, 512)):
+        quant(v("gq", 128 * k, 128 * k + 128), v("gp", 128 * k, 128 * k + 128), v("gt", a, a + 512))
+    act(v("le1"), v("tm", 0, HF), AF.Sign, bias=ca, scale=-1.0)
+    act(v("spk"), v("le1"), AF.Abs, bias=-0.25)
+    act(v("ct"), v("spk"), AF.Relu, bias=1.5 / TINY - 0.5, scale=2.0 - 2.0 / TINY)
+    fill(v("ct", 0, HF, 16), 0.0)
+    lin(v("kn", 0, 1), ca, 32.0, 15.5 - 32.0 * 192)
+    lin(v("inc"), kf, -512.0, 479.0)
+    scan(v("kn", 1, E), v("inc", 1, E), v("kx", 0, E - 1), v("kn", 0, 1), A.add, A.min)
+    quant(v("q0", 0, 128), v("p0", 0, 128), v("xt", 0, 512))
+    quant(v("q0", 128, C), v("p0", 128, C), v("xt", 512, 1024))
+    send(prev, "q0", "p0", 0, H, C, "arH0")
+    gfill(v("one"), 1)
+    gfill(v("xh"), 0)
+    op("G", lambda: g.affine_select(T.wd[:], T.xh[:, 0:520], [[1, 520]], A.not_equal, 1.0, -3, -4), regs(v("xh", 0, 520)), regs(v("wd")), 170 + 2 * CYC * 520)
+    for b in range(4):
+        quant(v("eq", 128 * b, 128 * b + 128), v("ep", 128 * b, 128 * b + 128), v("wd", 3 - b, 515 - b))
+    iota(v("it"), [[1, E]], int(LIFT + DROP), 0)
+    lin(v("eqa"), kb, -1.0, 1.0)
+    lin(v("t1"), v("kx", 1, E + 1), DROP, -DROP)
+    act(v("ih"), v("it"), AF.Copy)
+    scan(v("sp"), v("ih"), v("eqa"), 0.0, A.max, A.mult)
+    scan(v("tab"), v("t1"), v("sp"), -DROP, A.min, A.add)
+    iota(v("tm4"), [[0, 81], [1, 4]], 0, 0)
+    act(v("k4a"), v("tm4"), AF.Abs, bias=col(3), scale=-1.0)
+    act(v("k4"), v("k4a"), AF.Sign)
+    lin(v("eq4"), v("k4", 0, E), -1.0, 1.0)
+    lin(v("t14"), v("k4", 1, E + 1), DROP, -DROP)
+    scan(v("sp4"), v("ih"), v("eq4"), 0.0, A.max, A.mult)
+    scan(v("tab4"), v("t14"), v("sp4"), -DROP, A.min, A.add)
+    lin(v("cc"), v("k4", 0, K), -18 * HOLD, 17 * HOLD)
+    lin(col(12), col(11), 1.0, 4 * (DROP - LIFT))
+    lin(col(8), v("k4", 0, 1), -4 * DROP, col(12))
+    lin(col(13), col(11), 1.0, 12 * HOLD)
+    lin(col(7), col(3), -4 * HOLD, col(13))
+    gfill(v("neg"), -1)
+    gfill(v("nen", 0, 16), 0)
+    gfill(v("xx", 0, 16), 0)
+    gfill(v("xx", C + 16, C + 32), 0)
+    gfill(v("lead", 0, 1), -C)
+    gfill(v("lead", 1, C), 0)
+    iota(v("ib"), [[1, C]], 0, 0)
+    gfill(v("at", 4 * K, 512), 0)
+    quant(v("uq"), v("up"), v("ut"))
+    op("V", lambda: g.vector.tensor_copy(T.udq[:].bitcast(dt.uint32), T.uq[:].bitcast(dt.uint32).indirect(v("ul")[0])), regs(v("uq"), v("ul")), regs(v("udq")), 220)
+    act(v("udp"), ind(v("up"), v("ul")), AF.Copy)
 
-    def picks():
-        quant(v("uq"), v("up"), v("ut"))
-        op("V", lambda: g.vector.tensor_copy(T.udq[:].bitcast(dt.uint32), T.uq[:].bitcast(dt.uint32).indirect(T.ul[:])), regs(v("uq"), v("ul")), regs(v("udq")))
-        cp(v("udp"), ind(v("up"), v("ul")))
-        iota(v("jj"), [[1, 520]], 0, -4)
-        gfill(v("xh"), 0)
-        gfill(v("tF"), 0)
-        iota(v("i16"), [[16, 20]], 0, 0)
-        gfill(v("neg"), -1)
-        gfill(v("nen", 0, 16), 0)
-        gfill(v("lead", 0, 1), -C)
-        gfill(v("lead", 1, C), 0)
-        iota(v("ib"), [[1, C]], 0, 0)
-        gfill(v("at", 4 * K, 512), 0)
-        iota(v("it"), [[1, E]], 0, 0)
+    UD, GS, GE, GO = pair("udq", "udp", 0, 128), pair("gq", "gp", 0, 128), pair("gq", "gp", 128, 256), pair("gq", "gp", 256, 384)
 
-    def constants_0():
-        ts(v("gt"), v("gi"), col(3), A.is_equal)
-        fill(v("tC", 576), 0.0)
-        fill(v("tE", 1088), 0.0)
-        fill(v("rs", 0, 1), 0.0)
-        quant(v("gq"), v("gp"), v("gt"))
+    def slot(c, a, b):
+        first, at = TILE["ABCDE"[min((c - 1) // 4, 3) if c < 16 else 4]]
+        return v("tl", 4 * (at + a) + c - first, 4 * (at + b), 4)
 
-    def constants_1():
-        act(v("le1"), v("iz", 16, 16 + E), AF.Sign, bias=col(0))
-        act(v("spk"), v("le1"), AF.Abs, bias=-0.25)
-        act(v("ct"), v("spk"), AF.Relu, bias=1.5 / TINY - 0.5, scale=2.0 - 2.0 / TINY)
-        ts(v("wd"), v("jj"), 3.0, A.is_equal)
-        scan(v("kc", 1, E), v("inc", 1, E), v("kx", 0, E - 1), v("kc", 0, 1), A.add, A.max)
-        for b in range(4):
-            quant(v("eq", 128 * b, 128 * b + 128), v("ep", 128 * b, 128 * b + 128), v("wd", 3 - b, 515 - b))
+    def pivot(c):
+        return v("hold", 16 * c + 15, 16 * c + 16)
 
-    def constants_2():
-        lin(v("cd"), kb, -18 * HOLD2, 17 * HOLD2)
-        lin(v("cc"), kb, -18 * HOLD, 17 * HOLD)
-        lin(v("iwd"), v("i16"), 1.0, col(14))
-        lin(v("iwh"), v("i16"), 1.0, col(15))
-        lin(v("iws"), v("i16", 0, 16), 4.0, col(13))
+    def row(c, bank_v, bank_s):
+        n, total = 16 * c, v("rs", c, c + 1)
+        if c in S_ROWS:
+            at = E * S_ROWS.index(c)
+            act(v("sg", at, at + n), ps(bank_s, 0, n), AF.Sign, bias=pivot(c), scale=-1.0)
+            act(slot(c, 0, n), v("sg", at, at + n), AF.Relu, acc=total)
+            return
+        ts(slot(c, 0, n), ps(bank_v, 0, n), pivot(c), A.is_lt)
+        if c >= V_SUMS:
+            scan(v("s1", STEP * (c + 1) - n, STEP * (c + 1)), v("one", 0, n), slot(c, 0, n), v("dr", n + 15, n + 16), A.mult, A.add)
+        else:
+            act(v("junk", 8 * c * (c - 1), 8 * c * (c + 1)), slot(c, 0, n), AF.Copy, acc=total)
 
-    UD, GS = pair("udq", "udp", 0, 128), pair("gq", "gp", 0, 128)
-    TILE = {"A": 1, "B": 5, "C": 9, "D": 13, "E": 16}
+    def flags(a, b):
+        quant(v("ql", a, b), v("pl", a, b), v("tl", 4 * a, 4 * b))
 
-    def slot(c):
-        n = "ABCDE"[min((c - 1) // 4, 3) if c < 16 else 4]
-        return v("t" + n, c - TILE[n], 64 * c, 4)
+    def down(bank, a, n, start=False, stop=False):
+        mm(bank, n, GS, pair("ql", "pl", a, a + n), start, stop)
 
-    def row_v(c, bank):
-        ts(slot(c), ps(bank, 0, 16 * c), v("hold", 16 * c + 15, 16 * c + 16), A.is_lt)
-
-    def sum_s(c):
-        act(v("junk", 8 * c * (c - 1), 8 * c * (c + 1)), slot(c), AF.Copy, acc=v("rs", c, c + 1))
-
-    def rows_s(cs, bank):
-        for k, c in enumerate(cs):
-            act(v("sg", C * k, C * k + 16 * c), ps(bank, 0, 16 * c), AF.Sign, bias=v("hold", 16 * c + 15, 16 * c + 16), scale=-1.0)
-        for k, c in enumerate(cs):
-            act(slot(c), v("sg", C * k, C * k + 16 * c), AF.Relu, acc=v("rs", c, c + 1))
-
-    def tile_mm(n, qcols, cols, start, stop):
-        quant(v("q" + n, 0, qcols), v("p" + n, 0, qcols), v("t" + n, 0, 4 * qcols))
-        mm(4, min(cols, HALF), GS, pair("q" + n, "p" + n, 0, min(cols, HALF)), start, stop)
-        if cols > HALF:
-            mm(7, E - HALF, GS, pair("q" + n, "p" + n, HALF, E), start, stop)
-
-    def part(a, b, bank, start):
-        quant(v("qF", a, b), v("pF", a, b), v("tF", 4 * a, 4 * b))
-        mm(bank, b - a, GS, pair("qF", "pF", a, b), start, True)
-
-    def masked(a, b, bank):
-        tt(v("val", a, b), ps(bank, a, b), v("m1", 16 + a, 16 + b), A.add)
-
-    def hold(a, b):
+    def hold(a, b, bank, at):
+        tt(v("val", a, b), ps(bank, a - at, b - at), v("m1", a, b), A.add)
         scan(v("hold", a, b), v("c1", a, b), v("val", a, b), 0.0, A.add, A.min)
 
-    def catch(out, table, data, n, a=0):
-        scan(v(out, a, n), v(table, a, n), data, 0.0, A.add, A.min)
-        return v(out, 15, n, 16)
+    def catch(out, data, a, b, tab="tab"):
+        scan(v(out, a, b), data, v(tab, a, b), -DROP, A.max, A.add)
 
-    X = ["xt", "x1", "x2"]
+    def listed(out, caught, n):
+        ts(v(out, 0, n // 16), v(caught, 15, n, 16), col(6), A.add)
+
+    def listed4(out, caught, n):
+        ts(v(out), v(caught, 3, n, 4), 4.0, A.mult, col(8), A.add)
+
+    X, first, late = ["xt", "x1", "x2"], len(ops), set()
     for t in range(R):
         qn, pn, last = "q%d" % t, "p%d" % t, t == R - 1
-        quant(v(qn, 0, 128), v(pn, 0, 128), v(X[t], 0, 512))
-        send(prev, qn, pn, 0, H, C, "arH%d" % t)
-        quant(v(qn, 128, C), v(pn, 128, C), v(X[t], 512, 1024))
+        pad = 64 if t == 0 else 0
+        if t:
+            send(prev, qn, pn, 0, H, C, "arH%d" % t)
+        lands(nxt, qn, pn, C, E, "arH%d" % t)
         if t == 0:
-            picks()
+            behind = regs(v("q0", C, E))
+            dma("Y", T.wq[:].bitcast(dt.uint8), T.wc[:], behind, regs(v("wq")), "ldw")
+            dma("Y", T.wp[:], T.ws[:], behind, regs(v("wp")), "ldp")
+            dma("Y", T.vt[:], T.v[:], behind, regs(v("vt")), "ldv")
+        mm(6, 128, UD, pair(qn, pn, 0, 128))
         mm(0, C, UD, pair(qn, pn, 0, C))
         mm(1, C, UD, pair(qn, pn, 0, C))
-        if t == 0:
-            constants_0()
-        d_own, d_halo = v("tD", 3, 4 * C, 4), v("tE", 4 * C, 4 * E, 4)
-        masked(HALF, C, 0)
-        masked(0, HALF, 0)
-        hold(HALF, C)
-        rows_s(S_ROWS, 1)
-        hold(0, HALF)
-        for c in range(15, 0, -1):
-            if c not in S_ROWS:
-                row_v(c, 0)
-                sum_s(c)
-            if c == 8:
-                tt(d_own, ps(0, 0, C), v("hold", 0, C), A.is_le)
-        mm(2, E, UD, pair(qn, pn, 0, E))
+        d_own, d_far = v("tl", 3, 4 * C, 4), slot(16, C, E)
+        hold(128, C, 0, 0)
+        hold(0, 128, 6, 0)
+        mm(5, 128, UD, pair(qn, pn, E - 128, E))
         mm(3, E, UD, pair(qn, pn, 0, E))
-        tile_mm("D", E if t == 0 else C, E, True, False)
-        tile_mm("C", 192, 192, False, False)
+        mm(2, E, UD, pair(qn, pn, 0, E))
+        hold(C, E, 5, E - 128)
+        tt(d_far, ps(5, 64, 128), v("hold", C, E), A.is_le)
+        scan(v("dr", C, E), v("k16", 0, H), d_far, 0.0, A.mult, A.add)
+        for c in FAR_ROWS:
+            row(c, 2, 3)
+        for c in range(15, 0, -1):
+            row(c, 0, 1)
+        tt(d_own, ps(0, 0, C), v("hold", 0, C), A.is_le)
         scan(v("dr", 0, C), v("k16", 0, C), d_own, 0.0, A.mult, A.add)
-        if t == 0:
-            constants_1()
-        masked(C, E, 2)
-        tile_mm("B", 128, 128, False, False)
-        hold(C, E)
-        rows_s((19,), 3)
-        row_v(18, 2)
-        sum_s(18)
-        row_v(16, 2)
-        tt(d_halo, ps(2, C, E), v("hold", C, E), A.is_le)
-        row_v(17, 2)
-        sum_s(17)
-        op("V", lambda: g.vector.tensor_reduce(v("rs", 16, 17)[0], slot(16)[0], AxisListType.X, A.add), regs(slot(16)), regs(v("rs", 16, 17)))
-        scan(v("dr", C, E), v("k16", C, E), d_halo, 0.0, A.mult, A.add)
-        if t == 0:
-            fill(v("ct", 0, E, 16), 0.0)
-        tile_mm("E", E, E, False, False)
-        tt(v("s1"), v("dr", 15, E, 16), v("rs"), A.add)
-        ts(v("s2"), v("s1"), col(4), A.mult)
+        tt(v("s1", STEP - 1, STEP * V_SUMS, STEP), v("dr", 15, 16 * V_SUMS, 16), v("rs", 0, V_SUMS), A.add)
+        ts(v("s2"), v("s1", STEP - 1, STEP * 20, STEP), col(4), A.mult)
         ts(v("xh", 0, E, 16), v("s2"), col(5), A.add, col(5), A.subtract)
-        tile_mm("A", 128, 128, False, False)
         tt(v("xh", E, 2 * E, 16), v("s2"), v("xh", 0, E, 16), A.subtract)
-        scan(v("tF", 0, 4 * E, 4), v("ct"), v("xh", 0, E), 0.0, A.mult, A.add)
-        scan(v("tF", 1, 4 * E, 4), v("ct"), v("xh", E, 2 * E), 0.0, A.mult, A.add)
-        part(0, HALF, 4, False)
-        part(HALF, E, 7, False)
-        if t == 0:
-            constants_2()
+        for k in range(4):
+            scan(v("tG", k, 4 * HF, 4), v("ct"), v("xh", HF * k, HF * k + HF), 0.0, A.mult, A.add)
+        quant(v("qG"), v("pG"), v("tG"))
+        flags(0, 256 + pad)
+        down(4, 0, HF, start=True)
+        down(7, HF, HF, start=True)
+        flags(320, 512 + pad * 3 // 2)
+        down(4, 320, HF)
+        down(7, 320 + HF, 128)
+        flags(608, 800 + pad)
+        down(4, 608, 128)
+        down(4, 736, 128)
+        for k in range(2):
+            flags(864 + HF * k, 864 + HF * k + HF)
+            down(4 + 3 * k, 864 + HF * k, HF)
+        mm(4, HF, GE, pair("qG", "pG", 0, HF), False, True)
+        mm(7, HF, GO, pair("qG", "pG", 0, HF), False, True)
         for b in range(4):
             mm(b, E, pair("eq", "ep", 128 * b, 128 * b + 128), pair(qn, pn, 0, E))
-            act(v("ff", E * b, E * b + E), ps(b), AF.Copy)
-        tt(v("uu", 0, HALF), ps(4, 0, HALF), v("kc", 0, HALF), A.add)
-        tt(v("uu", HALF, E), ps(7, 0, E - HALF), v("kc", HALF, E), A.add)
+            act(v("ff", b, 4 * E, 4), ps(b), AF.Copy)
+        for k in range(2):
+            tt(v("uu", HF * k, HF * k + HF), ps(4 + 3 * k, 0, HF), v("kn", HF * k, HF * k + HF), A.subtract)
         mid = 32.0 * 192
-        ts(v("lt"), v("uu"), mid, A.is_gt)
-        ts(v("ng"), v("uu"), mid, A.is_lt, -1.0, A.mult)
-        ts(v("ne"), v("uu"), mid, A.is_equal, -1.0, A.mult)
+        for k in range(2):
+            act(v("na", HF * k, HF * k + HF), v("uu", HF * k, HF * k + HF), AF.Abs, bias=-mid)
+        for k in range(2):
+            act(v("ne", HF * k, HF * k + HF), v("na", HF * k, HF * k + HF), AF.Relu, bias=1.0, scale=-1.0)
+        ts(v("lt"), v("uu"), mid, A.is_gt, -1.0, A.mult)
+        ts(v("ng"), v("uu"), mid, A.is_lt)
         scan(v("qf"), kf, v("lt"), 0.0, A.mult, A.add)
-        scan(rev("qb", 0, E), rev("kx", 16, 16 + E), rev("ng", 0, E), 0.0, A.mult, A.add)
-        scan(v("tF", 0, 4 * E, 4), v("qf"), v("ne"), 0.0, A.max, A.mult)
-        scan(v("tF", 1, 4 * E, 4), v("qb"), v("ne"), 0.0, A.min, A.mult)
-        part(0, HALF, 5, True)
-        part(HALF, E, 4, True)
-        mm(6, E, GS, pair("qF", "pF", 0, E))
-        act(v("nd"), ps(6), AF.Copy, scale=-1.0)
-        catch("capb", "cd", ps(5, 0, HALF), HALF)
-        c_pos = catch("capb", "cd", ps(4, 0, E - HALF), E, HALF)
-        scan(v("mx", 0, HALF), v("neg", 0, HALF), ps(5, 0, HALF), 0.0, A.add, A.max)
-        tt(v("f1"), c_pos, v("iwd"), A.add)
-        scan(v("mx", HALF, E), v("neg", HALF, E), ps(4, 0, E - HALF), v("mx", HALF - 1, HALF), A.add, A.max)
-        act(v("nen", 16, 16 + E), v("mx"), AF.Sign)
+        scan(rev("qb", 0, E), rev("kx", 0, E), rev("ng", 0, E), 0.0, A.mult, A.add)
+        for k in range(2):
+            scan(v("tF", k, 4 * HF, 4), v("qf", HF * k, HF * k + HF), v("ne", HF * k, HF * k + HF), 0.0, A.min, A.mult)
+            scan(v("tF", 2 + k, 4 * HF, 4), v("qb", HF * k, HF * k + HF), v("ne", HF * k, HF * k + HF), 0.0, A.max, A.mult)
+        quant(v("qF"), v("pF"), v("tF"))
+        for bank, G in ((5, GE), (4, GE), (6, GO), (7, GO)):
+            mm(bank, HF, G, pair("qF", "pF", 0, HF))
+        act(v("nd", 0, HF), ps(4, 0, HF), AF.Copy, scale=-1.0)
+        act(v("nd", HF, E), ps(7, 0, HF), AF.Copy, scale=-1.0)
+        catch("capb", ps(5, 0, HF), 0, HF)
+        catch("capb", ps(6, 0, HF), HF, E)
+        listed("lpos", "capb", E)
+        scan(v("mx"), v("one"), v("nd"), 0.0, A.add, A.min)
+        act(v("nen", 16, 16 + E), v("mx"), AF.Sign, scale=-1.0)
         lin(v("cs"), v("nen", 16, 16 + E), HOLD, 2.0 - HOLD)
-        cp(v("lpos"), v("f1"))
         cp(ind(v("vv"), v("lpos")), v("nd"))
         act(v("ww"), v("vv", 0, C), AF.Abs)
         act(v("junk", 0, C), v("ww"), AF.Sign, bias=col(10), scale=-1.0, acc=v("sc", 0, 1))
-        scan(v("ra"), v("neg"), v("nen", 15, 15 + E), 0.0, A.add, A.mult)
-        c_o = catch("capv", "cd", v("vv", 0, C), C)
-        scan(rev("sm", 0, E), rev("cs", 0, E), rev("ra", 0, E), 0.0, A.add, A.max)
-        tt(v("f2"), c_o, v("iwd", 0, 16), A.add)
-        ts(v("nh"), v("ww"), col(1), A.is_equal, -2.0, A.mult)
-        cp(v("lo"), v("f2"))
-        for b in range(2):
-            act(v("yy", C * b, C * b + C), ind(v("ff", E * b, E * b + E), v("lo")), AF.Copy)
-        n = E if last else C
-        c_mir = catch("cap2", "cc", v("sm", 0, n), n)
+        catch("capv", v("vv"), 0, E, "tab4")
+        listed4("lo", "capv", E)
+        act(v("yy"), ind(v("ff"), v("lo")), AF.Copy)
+        ts(v("nh"), v("ww"), ca, A.is_equal, -2.0, A.mult)
         scan(v("npf"), v("lead"), v("nh"), v("sc", 0, 1), A.add, A.add)
-        tt(v("mf", 0, n // 16), c_mir, v("iwh", 0, n // 16), A.add)
-        scan(v("xx"), v("npf"), v("nh"), 0.0, A.min, A.mult)
-        cp(v("lmir", 0, n // 16), v("mf", 0, n // 16))
-        act(v("vm"), ind(v("vv"), v("lmir", 0, 16)), AF.Copy)
-        for b in range(2, 4):
-            act(v("yy", C * b, C * b + C), ind(v("ff", E * b, E * b + E), v("lo")), AF.Copy)
-        M64 = 1.5 * 2.0 ** 29
-        ts(v("tF", 0, 4 * C, 4), v("xx"), M64, A.add, M64, A.subtract)
-        tt(v("tF", 1, 4 * C, 4), v("xx"), v("tF", 0, 4 * C, 4), A.subtract)
-        c_m = catch("capm", "cd", v("vm"), C)
-        part(0, 128, 7, True)
-        tt(v("f4"), c_m, v("mf", 0, 16), A.add)
-        part(128, C, 5, True)
-        ts(v("lmm"), v("f4"), col(8), A.add)
-        catch("cap", "cc", ps(7, 0, 128), 128)
-        for b in range(4):
-            act(v("gg", C * b, C * b + C), ind(v("ff", E * b, E * b + E), v("lmm")), AF.Copy, scale=-0.5)
-        c_rk = catch("cap", "cc", ps(5, 0, 128), C, 128)
-        ts(v("lrk"), c_rk, col(9), A.add, 0.25, A.mult)
-        ts(v("f5"), c_rk, col(6), A.is_ge, 2 * HOLD, A.mult)
+        scan(v("xx", 16, C + 16), v("npf"), v("nh"), 0.0, A.min, A.mult)
+        turn(v("tr", 0, C), v("xx", 16, C + 16))
+        turn(v("tr", C, 544), v("xx"))
+        scan(v("su"), v("k16"), v("tr"), 0.0, A.mult, A.add)
+        ts(v("lrk"), ind(v("su"), v("lt_", 0, 1)), -4.0, A.add, 0.25, A.mult)
+        scan(v("ra"), v("neg"), v("nen", 15, 15 + E), 0.0, A.add, A.mult)
+        scan(rev("sm", 0, E), rev("cs", 0, E), rev("ra", 0, E), 0.0, A.add, A.max)
+        catch("cap2", v("sm", 0, C), 0, C, "tab4")
+        listed4("lmir", "cap2", C)
+        act(v("gg", 0, 16 * G_CUT), ind(v("yy"), v("lmir", 0, G_CUT)), AF.Copy, scale=-0.5)
         cp(ind(v("eb"), v("lrk")), v("ib"))
-        c_e = catch("cap3", "cc", v("eb", 0, K), K)
-        ts(v("le"), c_e, col(7), A.add)
-        tt(v("f6"), v("f5"), c_rk, A.add)
-        tt(v("f3"), v("f6"), v("iws"), A.min)
-        ts(v("lsel"), v("f3"), col(9), A.add, 0.25, A.mult)
-        for b in range(4):
-            act(v("ge", K * b, K * b + K), ind(v("gg", C * b, C * b + C), v("le")), AF.Copy)
-        for b in range(4):
-            tt(v("at", b, 4 * K, 4), ind(v("yy", C * b, C * b + C), v("le")), v("ge", K * b, K * b + K), A.add)
+        scan(v("cap3"), v("cc"), v("eb", 0, K), 0.0, A.add, A.min)
+        ts(v("le"), v("cap3", 3, K, 4), 4.0, A.mult, col(7), A.add)
+        if G_CUT < 64:
+            ts(v("gg", 16 * G_CUT, 4 * C), ind(v("yy"), v("lmir", G_CUT, 64)), -0.5, A.mult)
+        for a, b in zip(A_CUTS, A_CUTS[1:]):
+            act(v("ge", 16 * a, 16 * b), ind(v("gg"), v("le", a, b)), AF.Copy)
+            tt(v("at", 16 * a, 16 * b), ind(v("yy"), v("le", a, b)), v("ge", 16 * a, 16 * b), A.add)
         an, sn = "aq%d" % t, "ap%d" % t
         quant(v(an, K, K + 128), v(sn, K, K + 128), v("at"))
         send(far_to, an, sn, K, 2 * K, 0, "arA%d" % t)
-        W = C + K
-        for b in range(4):
-            act(v("a32", K * b, K * b + K), v("at", b, 4 * K, 4), AF.Copy, scale=32.0)
-        if t == 0:
-            quant(v("vq"), v("vp"), v("vt"))
+        lands(far_from, an, sn, 0, K, "arA%d" % t)
+        mark = len(ops)
+        ts(v("f4"), ind(v("su"), v("lt_", 0, 1)), -4.0, A.add, 0.25, A.mult)
+        ts(v("f5"), v("f4"), float(K), A.is_ge, HOLD, A.mult)
+        tt(v("f6"), v("f5"), v("f4"), A.add)
+        tt(v("f3"), v("f6"), v("iws"), A.min)
+        cp(v("lsel"), v("f3"))
+        act(v("a32"), v("at", 0, 4 * K), AF.Copy, scale=32.0)
         for b in (2, 3, 0, 1):
-            tt(v("zw", W * b + K, W * b + W), v("yy", C * b, C * b + C), v("gg", C * b, C * b + C), A.add)
+            tt(v("zw", W * b + K, W * b + W), v("yy", b, 4 * C, 4), v("gg", b, 4 * C, 4), A.add)
             act(v("zw", W * b + K, W * b + W), v("zw", W * b + K, W * b + W), AF.Copy, scale=32.0)
-        if last:
-            tt(v("ob"), v("vv"), v("it"), A.add)
+        if not last:
+            quant(v("vq"), v("vp"), v("vt"))
+        else:
+            catch("capb", v("sm"), 0, E)
+            listed("lpos", "capb", E)
+            scan(v("ob"), v("vv"), v("it"), LIFT, A.min, A.add)
+            act(v("lmo"), ind(v("ob"), v("lpos")), AF.Identity, bias=-(LIFT + DROP))
+            dma("Y", T.lm[:], T.lmo[0:128:16, :], regs(v("lmo")), [], "st0")
+        late.update(range(mark, len(ops)))
         for b in (2, 3, 0, 1):
             mm(b, 128, pair("wq", "wp", 128 * b, 128 * b + 128), pair(an, sn, 0, 128))
-        for b in (2, 3, 0, 1):
-            tt(v("zw", W * b, W * b + K), ps(b, 0, K), v("a32", K * b, K * b + K), A.add)
-        for b in (2, 3):
-            act(v(X[t + 1], b, 4 * C, 4), ind(v("zw", W * b, W * b + W), v("lsel")), AF.Copy, scale=0.03125)
-        cut = 10
-        act(v(X[t + 1], 1 + 64 * cut, 4 * C, 4), ind(v("zw", W, 2 * W), v("lsel", cut, 16)), AF.Copy, scale=0.03125)
-        ts(v(X[t + 1], 0, 4 * C, 4), ind(v("zw", 0, W), v("lsel")), 0.03125, A.mult)
-        ts(v(X[t + 1], 1, 64 * cut, 4), ind(v("zw", W, 2 * W), v("lsel", 0, cut)), 0.03125, A.mult)
+            tt(v("zw", W * b, W * b + K), ps(b, 0, K), v("a32", b, 4 * K, 4), A.add)
+        for k in range(2):
+            for b in (2, 3, 0, 1):
+                out, src = v(X[t + 1], 512 * k + b, 512 * k + 512, 4), ind(v("zw", W * b, W * b + W), v("lsel", 8 * k, 8 * k + 8))
+                if b >= 2 - k:
+                    act(out, src, AF.Copy, scale=0.03125)
+                else:
+                    ts(out, src, 0.03125, A.mult)
+                    late.add(len(ops) - 1)
+            quant(v("q%d" % (t + 1), 128 * k, 128 * k + 128), v("p%d" % (t + 1), 128 * k, 128 * k + 128), v(X[t + 1], 512 * k, 512 * k + 512))
 
-    act(v("lmo"), ind(v("ob"), v("lmir")), AF.Copy)
-    dma("Y", T.lm[:], T.lmo[0:128:16, :], regs(v("lmo")), [], "st0")
     for k in range(2):
-        quant(v("q2", 128 * k, 128 * k + 128), v("p2", 128 * k, 128 * k + 128), v("x2", 512 * k, 512 * k + 512))
         mm(4 + k, 128, pair("vq", "vp", 0, 128), pair("q2", "p2", 128 * k, 128 * k + 128))
+        cp(v("yo", 128 * k, 128 * k + 128), ps(4 + k, 0, 128))
     dma("Y", T.oc[:], T.q2[:].bitcast(dt.uint8), regs(v("q2")), [], "st1")
-    cp(v("yo", 0, 128), ps(4, 0, 128))
-    cp(v("yo", 128, C), ps(5, 0, 128))
     for k in range(4):
         dma("S" if k % 2 else "Y", T.osc[4 * k:4 * k + 4, :], T.p2[32 * k:32 * k + 4, :], regs(v("p2")), [], "st%d" % (3 + k))
     dma("S", T.y[:], T.yo[:], regs(v("yo")), [], "st2")
-    emit(g, T, ops, sent[0])
+    emit(g, T, ops, sent[0], first, late)
 
 
-def emit(g, T, ops, sent):
-    eng = {"V": g.vector, "S": g.scalar, "P": g.tensor, "G": g, "Y": g.sync}
-    deps = []
-    for i, o in enumerate(ops):
-        d = []
-        for j in range(i):
-            p = ops[j]
-            if o[0] == "P" and p[0] == "P":
+def ordered(ops, deps, first, late):
+    n, place = len(ops), {}
+
+    def visit(i):
+        if i not in place:
+            for j in deps[i]:
+                visit(j)
+            place[i] = len(place)
+    for i in range(first, n):
+        visit(i)
+    users, open_ = [[] for o in ops], [len(d) for d in deps]
+    for i in range(n):
+        for j in deps[i]:
+            users[j].append(i)
+    ready, start, free, now = {i: 0.0 for i in range(n) if not deps[i]}, {}, {}, 0.0
+    while ready:
+        moved = False
+        for q in "YGPVSf":
+            if free.get(q, 0.0) > now:
                 continue
-            hit = any(_meet(a, b) for a in o[2] + o[3] for b in p[3]) or any(_meet(a, b) for a in o[3] for b in p[2])
-            if not hit and o[0] != p[0]:
-                hit = any(a[0].startswith("ps") and a[0] == b[0] for a in o[2] for b in p[2])
-            if hit and p[4] != "remote":
-                d.append(j)
-        deps.append(d)
+            soon = BIG
+            for i in sorted((i for i in ready if ops[i][0][0] == q), key=lambda i: place[i]):
+                if ready[i] > now:
+                    soon = min(soon, ready[i])
+                elif now + ops[i][6] * (1.0 if i in late else 1.0 - SHARE[i >= first]) <= soon:
+                    start[i], free[q], moved = now, now + ops[i][6], True
+                    del ready[i]
+                    for k in users[i]:
+                        open_[k] -= 1
+                        if not open_[k]:
+                            ready[k] = max(start[j] + (ops[j][6] if ops[k][0] == ops[j][0] in "PG" else ops[j][7] + WAKE) for j in deps[k])
+                    break
+        if not moved:
+            now = min(x for x in list(ready.values()) + list(free.values()) if x > now)
+    return sorted(range(n), key=lambda i: (start[i], place[i]))
+
+
+SHARE, KEPT = (0.7, 0.6), {}
+
+
+def emit(g, T, ops, sent, first, late):
+    eng = {"V": g.vector, "S": g.scalar, "P": g.tensor, "G": g, "Y": g.sync}
+    if not KEPT:
+        deps = []
+        for i, o in enumerate(ops):
+            d = []
+            for j in range(i):
+                p = ops[j]
+                hit = any(_meet(a, b) for a in o[2] + o[3] for b in p[3]) or any(_meet(a, b) for a in o[3] for b in p[2])
+                if not hit and o[0] != p[0]:
+                    hit = any(a[0].startswith("ps") and a[0] == b[0] for a in o[2] for b in p[2])
+                if hit:
+                    d.append(j)
+            deps.append(d)
+        row = [i for i, o in enumerate(ops) if o[0] == "G"]
+        KEPT[0] = (deps, ordered(ops, [d + [row[row.index(i) - 1]] if i in row[1:] else d for i, d in enumerate(deps)], first, late))
+    deps, order = KEPT[0]
+    place = {i: k for k, i in enumerate(order)}
     known = {q: {} for q in eng}
-    clock, waits, marked = [], [], set()
-    for i, o in enumerate(ops):
+    clock, waits, marked = {}, {}, set()
+    for i in order:
+        o = ops[i]
         if o[0] == "far":
-            clock.append({o[4]: i})
-            waits.append([])
+            clock[i] = {o[4]: place[i]}
             continue
         k, need = known[o[0]], {}
         for j in deps[i]:
+            if ops[j][4] == "remote" or o[0] == ops[j][0] == "P":
+                continue
             key = ops[j][4] or ops[j][0]
-            need[key] = max(need.get(key, -1), j)
+            need[key] = max(need.get(key, -1), place[j])
         w = []
-        for key, j in sorted(need.items(), key=lambda e: -e[1]):
-            if k.get(key, -1) < j:
-                w.append(j)
-                for kk, jj in clock[j].items():
+        for key, at in sorted(need.items(), key=lambda e: -e[1]):
+            if k.get(key, -1) < at:
+                w.append(order[at])
+                for kk, jj in clock[order[at]].items():
                     k[kk] = max(k.get(kk, -1), jj)
         marked.update(w)
-        waits.append(w)
+        waits[i] = w
         c = dict(k)
-        c[o[4] or o[0]] = i
-        clock.append(c)
+        c[o[4] or o[0]] = place[i]
+        clock[i] = c
     count, value = {q: 0 for q in eng}, {}
-    for i, o in enumerate(ops):
-        if o[4] is None and i in marked:
-            count[o[0]] += 1
-            value[i] = count[o[0]]
-    for i, o in enumerate(ops):
+    for i in order:
+        if ops[i][4] is None and i in marked:
+            count[ops[i][0]] += 1
+            value[i] = count[ops[i][0]]
+    for i in order:
+        o = ops[i]
         if o[0] == "far":
             continue
         for j in waits[i]:

@@ -10,8 +10,10 @@ TINY = 2.0 ** -18
 CODE, PLANE, BF, F16, F32, U16, I32 = "float8_e4m3fn_x4", "uint8", "bfloat16", "float16", "float32", "uint16", "int32"
 S_ROWS, V_SUMS = (17, 16, 15, 14, 13), 18
 FAR_ROWS, STEP = (17, 16, 19, 18), 304
-TILE = {"D": (13, 0), "C": (9, 320), "B": (5, 608), "A": (1, 736), "E": (16, 864)}
-G_CUT, A_CUTS = 56, (0, 4, 14, 24)
+TILE = {"D": (13, 0), "C": (9, 320), "B": (5, 576), "A": (1, 704), "E": (16, 832)}
+G_CUT, A_CUTS = 56, (("V", 0, 6), ("S", 6, 14), ("S", 14, 24))
+X_CUTS = (("S", 2, 0, 16), ("S", 3, 0, 16), ("V", 0, 0, 16), ("V", 1, 0, 12), ("S", 1, 12, 16))
+U_CUTS, H_CUTS = ((0, 8), (8, 16)), ((192, 256), (128, 192))
 W = C + K
 HF = E // 2
 
@@ -27,29 +29,30 @@ SCRATCH = {
     "eq": _sb(512, CODE), "ep": _sb(512, PLANE), "gq": _sb(384, CODE), "gp": _sb(384, PLANE),
     "q0": _sb(E, CODE), "p0": _sb(E, PLANE), "q1": _sb(E, CODE), "p1": _sb(E, PLANE), "q2": _sb(C, CODE), "p2": _sb(C, PLANE),
     "aq0": _sb(K + 128, CODE), "ap0": _sb(K + 128, PLANE), "aq1": _sb(K + 128, CODE), "ap1": _sb(K + 128, PLANE),
-    "tl": _sb(4 * 1184, BF), "ql": _sb(1184, CODE), "pl": _sb(1184, PLANE),
-    "tF": _sb(4 * HF, BF), "qF": _sb(HF, CODE), "pF": _sb(HF, PLANE), "tG": _sb(4 * HF, BF), "qG": _sb(HF, CODE), "pG": _sb(HF, PLANE),
+    "tl": _sb(4 * 1168, BF), "ql": _sb(1152, CODE), "pl": _sb(1152, PLANE),
+    "tF": _sb(4 * E, BF), "qF": _sb(E, CODE), "pF": _sb(E, PLANE),
     "at": _sb(512, BF), "a32": _sb(4 * K, BF),
-    "tm": _sb(E + 16, BF), "ih": _sb(E, F16), "wd": _sb(520, BF), "gi": _sb(512, BF), "gt": _sb(1040, BF),
-    "col": _sb(16, F32), "pi": _sb(8, I32), "ul": _sb(8, U16), "uf": _sb(16, F32), "lt_": _sb(2, U16),
-    "m1": _sb(E + 16, BF), "c1": _sb(E, BF), "k16": _sb(544, BF), "ct": _sb(HF, BF), "le1": _sb(HF, BF), "spk": _sb(HF, BF),
-    "inc": _sb(E, F32), "kn": _sb(E, F32), "it": _sb(E, F32), "ib": _sb(C, BF), "kx": _sb(E + 16, BF), "cc": _sb(K, BF),
+    "tm": _sb(E + 16, BF), "ih": _sb(E, F16), "wd": _sb(520, BF), "gi": _sb(256, BF), "mr": _sb(128, BF), "gt": _sb(1040, BF),
+    "col": _sb(16, F32), "pi": _sb(16, F32), "ul": _sb(8, U16), "uf": _sb(16, F32), "lt_": _sb(2, U16),
+    "m1": _sb(E + 16, BF), "c1": _sb(E, BF), "k16": _sb(E, BF),
+    "inc": _sb(E, F32), "kn": _sb(E, F32), "xf": _sb(E, F32), "it": _sb(E, F32), "ib": _sb(C, BF), "kx": _sb(E + 16, BF), "cc": _sb(K, BF),
     "eqa": _sb(E, BF), "t1": _sb(E, F16), "sp": _sb(E, F16), "tab": _sb(E, F16),
     "tm4": _sb(E + 4, BF), "k4a": _sb(E + 4, BF), "k4": _sb(E + 4, BF), "eq4": _sb(E, BF), "t14": _sb(E, F16), "sp4": _sb(E, F16), "tab4": _sb(E, F16),
     "lead": _sb(C, BF), "neg": _sb(E, BF), "one": _sb(E, BF), "iws": _sb(16, F32),
-    "val": _sb(E, F32), "hold": _sb(E, F32), "sg": _sb(6 * E, BF), "junk": _sb(16 * 210, BF), "rs": _sb(20, F32), "dr": _sb(E, BF),
-    "s1": _sb(20 * STEP, F16), "s2": _sb(20, F32), "xh": _sb(2 * E, BF),
-    "uu": _sb(E, BF), "lt": _sb(E, BF), "ng": _sb(E, BF), "ne": _sb(E, BF), "na": _sb(E, BF), "qf": _sb(E, BF), "qb": _sb(E, BF),
+    "val": _sb(E, F32), "hold": _sb(E, F32), "sg": _sb(6 * E, BF), "junk": _sb(16 * 210, BF), "rs": _sb(20, F32), "dr": _sb(C, BF), "dh": _sb(H, F32),
+    "wb": _sb(STEP + 640, BF), "tb": _sb(640, BF), "k32": _sb(512, BF), "hf": _sb(STEP + 32, BF), "c128": _sb(32, BF), "lh": _sb(16, U16), "xh": _sb(2 * C, BF),
+    "uu": _sb(E, BF), "ne": _sb(E, BF), "na": _sb(E, BF), "qf": _sb(E + 16, BF), "qb": _sb(E + 16, BF),
     "capb": _sb(E, F16), "capv": _sb(E, F16), "cap2": _sb(E, F16), "cap3": _sb(K, F32), "nd": _sb(E, BF), "vv": _sb(E, BF),
     "mx": _sb(E, BF), "nen": _sb(E + 16, BF), "cs": _sb(E, BF), "ra": _sb(E, F16), "sm": _sb(E, F16), "ww": _sb(C, BF), "sc": _sb(2, F32),
-    "nh": _sb(C, BF), "npf": _sb(C, BF), "xx": _sb(C + 32, BF), "tr": _sb(544, BF), "su": _sb(544, BF), "eb": _sb(C, BF),
+    "nh": _sb(C, BF), "xm": _sb(C + 32, BF), "xx": _sb(C + 32, BF), "tr": _sb(544, BF), "tn": _sb(544, BF), "su": _sb(544, BF), "eb": _sb(C, BF),
     "f3": _sb(16, F32), "f4": _sb(16, F32), "f5": _sb(16, F32), "f6": _sb(16, F32),
     "lpos": _sb(20, U16), "lo": _sb(80, U16), "lmir": _sb(64, U16), "lrk": _sb(16, U16), "le": _sb(24, U16), "lsel": _sb(16, U16),
     "ff": _sb(4 * E, BF), "yy": _sb(4 * E, BF), "gg": _sb(4 * C, BF), "ge": _sb(4 * K, BF), "zw": _sb(4 * W, BF),
     "lmo": _sb(E, F32), "ob": _sb(E, F32), "yo": _sb(C, F32),
 }
 PART = {}
-for _n, _names in (("cf", "uf iws"), ("df", "f3 f4 f5 f6 s2 rs sc"), ("ls", "lpos lo lmir lrk le lsel"), ("lc", "ul lt_")):
+for _n, _names in (("cf", "uf iws"), ("df", "f3 f4 f5 f6 rs sc"), ("ls", "lpos lo lmir lrk le lsel"), ("lc", "ul lt_ lh"),
+                   ("cb", "hf c128 cc eq4 eqa lead neg one ib")):
     _at = 0
     for _k in _names.split():
         _w, (_p, _c), _d = SCRATCH.pop(_k)
@@ -58,9 +61,9 @@ for _n, _names in (("cf", "uf iws"), ("df", "f3 f4 f5 f6 s2 rs sc"), ("ls", "lpo
     SCRATCH[_n] = _sb(_at, _d)
 for _b in range(8):
     SCRATCH["ps%d" % _b] = ("psum", [128, 512], F32)
-SEMAPHORES = ["sV", "sS", "sP", "sG", "ldx0", "ldx1", "ldu", "ldv", "ldw", "ldp", "arH0", "arH1", "arA0", "arA1", "sent",
-              "st0", "st1", "st2", "st3", "st4", "st5", "st6"]
-CYC, WAKE, ISSUE, FIRST, FLIGHT, LOAD = 0.83, 150.0, 300.0, 1000.0, 2200.0, 1700.0
+SEMAPHORES = ["sV", "sS", "sP", "sG", "ldx0", "ldx1", "ldu", "ldv", "ldw", "ldp", "ldz0", "ldz1", "ldz2", "arH0", "arH1", "arA0", "arA1", "sent",
+              "st0", "st1", "st2", "st3", "st4", "st5", "st6", "st7"]
+CYC, WAKE, ISSUE, FIRST, FLIGHT, LOAD = 0.83, 200.0, 300.0, 1000.0, 1900.0, 1400.0
 
 
 def _meet(a, b):
@@ -87,8 +90,8 @@ def rank_program(g, core, T, topo):
         b = SCRATCH[name][1][1] if b is None else b
         return (T[name][:, a:b:s] if s > 1 else T[name][:, a:b], (name, a, b, s))
 
-    def rev(name, a, b):
-        return (T[name][:, b - 1::-1] if a == 0 else T[name][:, b - 1:a - 1:-1], (name, a, b, 1))
+    def rev(name, a, b, s=1):
+        return (T[name][:, b - 1::-s] if a < s else T[name][:, b - 1:a - 1:-s], (name, a, b, s))
 
     def ind(win, off):
         return (win[0].indirect(off[0]), win[1], off[1])
@@ -122,7 +125,7 @@ def rank_program(g, core, T, topo):
             op("V", lambda: g.vector.tensor_scalar(out[0], in0[0], ap(s1), ap(s2), o0, o1), regs(in0, s1, s2), regs(out), cost(out, in0))
 
     def tt(out, a, b, o):
-        both = not a[1][0].startswith("ps")
+        both = not (a[1][0].startswith("ps") or b[1][0].startswith("ps"))
         op("V", lambda: g.vector.tensor_tensor(out[0], a[0], b[0], o), regs(a, b), regs(out), cost(out, a, rate=2.0 if both else 1.0))
 
     def cp(out, a):
@@ -159,7 +162,7 @@ def rank_program(g, core, T, topo):
         op("G", lambda: g.iota(out[0], pat, base, cm, allow_small_or_imprecise_dtypes=True), [], regs(out), 130 + 2 * CYC * num(out))
 
     def gfill(out, c):
-        iota(out, [[0, out[1][2] - out[1][1]]], c, 0)
+        iota(out, [[0, num(out)]], c, 0)
 
     def dma(q, out, in_, reads, writes, sem):
         e = g.sync if q == "Y" else g.scalar
@@ -196,58 +199,65 @@ def rank_program(g, core, T, topo):
     dma("S", T.ut[:], T.u[:], [], regs(v("ut")), "ldu")
     dma("Y", T.xt[:, 512:1024], T.x[:, 512:1024], [], regs(v("xt", 512, 1024)), "ldx1")
 
-    ca, cg, cpar = col(0), col(1), col(2)
-    iota(v("pi", 0, 1), [[0, 1]], 0, 1)
-    iota(v("pi", 1, 2), [[0, 1]], 0, 17)
-    ts(v("pi", 4, 5), v("pi", 0, 1), 15, A.bitwise_and)
-    ts(v("pi", 5, 6), v("pi", 0, 1), 4, A.logical_shift_right)
-    ts(v("pi", 6, 7), v("pi", 1, 2), 4, A.logical_shift_right, 1, A.bitwise_and)
-    ts(v("pi", 7, 8), v("pi", 0, 1), 2, A.logical_shift_right, 3, A.bitwise_and)
-    cp(v("col", 0, 4), v("pi", 4, 8))
-    ts(v("pi", 2, 3), v("pi", 0, 1), 3, A.bitwise_and)
-    cp(col(11), v("pi", 2, 3))
-    iota(v("tm"), [[0, 21], [1, 16]], 0, 0)
+    ca, cg, cpar = col(0), col(15), col(1)
+    cp_, M1 = v("pi", 0, 1), 1.5 * 2.0 ** 23
+    iota(cp_, [[0, 1]], 0, 1)
+    ts(v("pi", 4, 5), cp_, 1 / 16, A.mult, 1 / 64 - 0.5, A.add)
+    ts(cg, v("pi", 4, 5), M1, A.add, M1, A.subtract)
+    ts(ca, cg, -16.0, A.mult, cp_, A.add)
+    for k, m in enumerate((1 / 32, 1 / 4, 17 / 32)):
+        lin(v("pi", 1 + k, 2 + k), cp_, m, 1 / 64 - 0.5)
+    lin(v("pi", 5, 8), v("pi", 1, 4), 1.0, M1)
+    lin(v("pi", 10, 13), v("pi", 5, 8), 1.0, -M1)
+    lin(col(14), v("pi", 10, 11), -32.0, cp_)
+    lin(col(11), v("pi", 11, 12), -4.0, cp_)
+    lin(col(3), cg, -4.0, v("pi", 11, 12))
+    lin(col(2), v("pi", 12, 13), -2.0, cp_)
+    lin(cpar, cg, 1.0, col(2))
     iota(v("uf"), [[16, 16]], 0, 0)
-    iota(v("gi"), [[1, 8], [0, 32], [100, 2]], 0, 0)
+    iota(v("gi"), [[1, 8], [0, 32]], 0, 0)
+    iota(v("mr"), [[1, 128]], 0, 0)
+    iota(v("tm"), [[0, 21], [1, 16]], 0, 0)
+    fill(v("wd"), 0.0)
+    ts(v("wd", 3, 515, 4), v("mr"), cp_, A.is_equal)
+    for b in range(4):
+        quant(v("eq", 128 * b, 128 * b + 128), v("ep", 128 * b, 128 * b + 128), v("wd", 3 - b, 515 - b))
     cp(v("ul"), v("uf", 0, 8))
     ts(v("m1"), v("tm"), ca, A.not_equal, BIG, A.mult)
     act(v("kx"), v("m1"), AF.Sign)
     kb, kf = v("kx", 0, E), v("kx", 15, 15 + E)
     act(v("k16", 0, E), v("tm", 0, E), AF.Sign)
-    act(v("k16", E, 544), v("tm", 0, 544 - E), AF.Sign)
     lin(v("c1"), v("k16", 0, E), -2 * BIG, 2 * BIG)
-    for a, b in ((208, 320), (464, 608), (688, 864), (1136, 1184)):
-        fill(v("tl", 4 * a, 4 * b), 0.0)
-    fill(v("rs", 0, 1), 0.0)
-    M32 = 1.5 * 2.0 ** 28
-    lin(col(4), v("kx", 0, 1), 1.0 - TINY, -1.0)
-    lin(col(5), v("kx", 0, 1), M32 * TINY - M32, M32)
+    fill(v("tl", 4 * 656, 4 * 832), 0.0)
+    for k, (a, b) in enumerate(((464, 576), (208, 320), (1088, 1168))):
+        dma("Y", T.tl[:, 4 * a:4 * b], T.tl[:, 4 * 656:4 * (656 + b - a)], regs(v("tl", 4 * 656, 4 * (656 + b - a)), v("xt")), regs(v("tl", 4 * a, 4 * b)), "ldz%d" % k)
+    lin(v("rs", 0, 1), ca, 0.0, 0.0)
     lin(col(6), v("kx", 0, 1), -DROP, DROP - LIFT)
-    lin(col(9), cpar, 272.0, 15.0)
+    lin(col(9), cpar, 272.0, 0.0)
     lin(col(10), ca, 1.0, 0.5)
     ts(v("lt_", 0, 1), ca, 16.0, A.mult, col(9), A.add)
-    ts(v("iws"), v("uf"), ca, A.add, float(K), A.add)
-    ts(v("gt", 0, 512, 2), v("gi", 0, 512, 2), cg, A.is_equal)
-    ts(v("gt", 1, 512, 2), v("gi", 0, 512, 2), cg, A.is_equal)
-    fill(v("gt", 512, 513), 0.0)
-    ts(v("gt", 513, 1025), v("gi"), cg, A.is_equal)
-    for k, a in enumerate((0, 513, 512)):
+    lin(v("iws"), v("uf"), 1.0, ca)
+    lin(v("iws"), v("iws"), 1.0, float(K))
+    fill(v("gt", 512, 1026, 2), 0.0)
+    for a in (0, 1, 513):
+        ts(v("gt", a, a + 511, 2), v("gi"), cg, A.is_equal)
+    for k, a in enumerate((0, 513)):
         quant(v("gq", 128 * k, 128 * k + 128), v("gp", 128 * k, 128 * k + 128), v("gt", a, a + 512))
-    act(v("le1"), v("tm", 0, HF), AF.Sign, bias=ca, scale=-1.0)
-    act(v("spk"), v("le1"), AF.Abs, bias=-0.25)
-    act(v("ct"), v("spk"), AF.Relu, bias=1.5 / TINY - 0.5, scale=2.0 - 2.0 / TINY)
-    fill(v("ct", 0, HF, 16), 0.0)
     lin(v("kn", 0, 1), ca, 32.0, 15.5 - 32.0 * 192)
     lin(v("inc"), kf, -512.0, 479.0)
     scan(v("kn", 1, E), v("inc", 1, E), v("kx", 0, E - 1), v("kn", 0, 1), A.add, A.min)
     quant(v("q0", 0, 128), v("p0", 0, 128), v("xt", 0, 512))
     quant(v("q0", 128, C), v("p0", 128, C), v("xt", 512, 1024))
     send(prev, "q0", "p0", 0, H, C, "arH0")
-    gfill(v("one"), 1)
+    gfill(v("hf", STEP, STEP + 32), 0)
+    act(v("hf", 0, STEP), v("tm", 0, STEP), AF.Identity, bias=-0.5, scale=0.0)
+    for c in range(16, 20):
+        lin(v("kn", 16 * c, 16 * c + 16), v("kn", 16 * c, 16 * c + 16), 1.0, 128.0 if c < V_SUMS else 8.0 * c)
+    ts(v("lh"), v("uf"), 2.0, A.mult, col(14), A.add)
+    gfill(v("k32"), 1)
+    gfill(v("k32", 0, 512, 32), 0)
     gfill(v("xh"), 0)
-    op("G", lambda: g.affine_select(T.wd[:], T.xh[:, 0:520], [[1, 520]], A.not_equal, 1.0, -3, -4), regs(v("xh", 0, 520)), regs(v("wd")), 170 + 2 * CYC * 520)
-    for b in range(4):
-        quant(v("eq", 128 * b, 128 * b + 128), v("ep", 128 * b, 128 * b + 128), v("wd", 3 - b, 515 - b))
+    gfill(v("c128"), -128)
     iota(v("it"), [[1, E]], int(LIFT + DROP), 0)
     lin(v("eqa"), kb, -1.0, 1.0)
     lin(v("t1"), v("kx", 1, E + 1), DROP, -DROP)
@@ -266,10 +276,12 @@ def rank_program(g, core, T, topo):
     lin(col(8), v("k4", 0, 1), -4 * DROP, col(12))
     lin(col(13), col(11), 1.0, 12 * HOLD)
     lin(col(7), col(3), -4 * HOLD, col(13))
+    gfill(v("one"), 1)
     gfill(v("neg"), -1)
     gfill(v("nen", 0, 16), 0)
-    gfill(v("xx", 0, 16), 0)
-    gfill(v("xx", C + 16, C + 32), 0)
+    for x in ("xx", "xm"):
+        gfill(v(x, 0, 16), 0)
+        gfill(v(x, C + 16, C + 32), 0)
     gfill(v("lead", 0, 1), -C)
     gfill(v("lead", 1, C), 0)
     iota(v("ib"), [[1, C]], 0, 0)
@@ -278,7 +290,7 @@ def rank_program(g, core, T, topo):
     op("V", lambda: g.vector.tensor_copy(T.udq[:].bitcast(dt.uint32), T.uq[:].bitcast(dt.uint32).indirect(v("ul")[0])), regs(v("uq"), v("ul")), regs(v("udq")), 220)
     act(v("udp"), ind(v("up"), v("ul")), AF.Copy)
 
-    UD, GS, GE, GO = pair("udq", "udp", 0, 128), pair("gq", "gp", 0, 128), pair("gq", "gp", 128, 256), pair("gq", "gp", 256, 384)
+    UD, GS, GE = pair("udq", "udp", 0, 128), pair("gq", "gp", 0, 128), pair("gq", "gp", 128, 256)
 
     def slot(c, a, b):
         first, at = TILE["ABCDE"[min((c - 1) // 4, 3) if c < 16 else 4]]
@@ -296,7 +308,8 @@ def rank_program(g, core, T, topo):
             return
         ts(slot(c, 0, n), ps(bank_v, 0, n), pivot(c), A.is_lt)
         if c >= V_SUMS:
-            scan(v("s1", STEP * (c + 1) - n, STEP * (c + 1)), v("one", 0, n), slot(c, 0, n), v("dr", n + 15, n + 16), A.mult, A.add)
+            end = STEP + 32 * (c - 15)
+            scan(v("wb", end - n - 32, end), v("hf", STEP - n, STEP + 32), slot(c, 0, n + 32), v("dh", n + 15 - C, n + 16 - C), A.add, A.add)
         else:
             act(v("junk", 8 * c * (c - 1), 8 * c * (c + 1)), slot(c, 0, n), AF.Copy, acc=total)
 
@@ -335,65 +348,68 @@ def rank_program(g, core, T, topo):
         mm(0, C, UD, pair(qn, pn, 0, C))
         mm(1, C, UD, pair(qn, pn, 0, C))
         d_own, d_far = v("tl", 3, 4 * C, 4), slot(16, C, E)
-        hold(128, C, 0, 0)
+        for a, b in H_CUTS:
+            hold(a, b, 0, 0)
         hold(0, 128, 6, 0)
         mm(5, 128, UD, pair(qn, pn, E - 128, E))
         mm(3, E, UD, pair(qn, pn, 0, E))
         mm(2, E, UD, pair(qn, pn, 0, E))
         hold(C, E, 5, E - 128)
-        tt(d_far, ps(5, 64, 128), v("hold", C, E), A.is_le)
-        scan(v("dr", C, E), v("k16", 0, H), d_far, 0.0, A.mult, A.add)
-        for c in FAR_ROWS:
-            row(c, 2, 3)
         for c in range(15, 0, -1):
             row(c, 0, 1)
         tt(d_own, ps(0, 0, C), v("hold", 0, C), A.is_le)
         scan(v("dr", 0, C), v("k16", 0, C), d_own, 0.0, A.mult, A.add)
-        tt(v("s1", STEP - 1, STEP * V_SUMS, STEP), v("dr", 15, 16 * V_SUMS, 16), v("rs", 0, V_SUMS), A.add)
-        ts(v("s2"), v("s1", STEP - 1, STEP * 20, STEP), col(4), A.mult)
-        ts(v("xh", 0, E, 16), v("s2"), col(5), A.add, col(5), A.subtract)
-        tt(v("xh", E, 2 * E, 16), v("s2"), v("xh", 0, E, 16), A.subtract)
-        for k in range(4):
-            scan(v("tG", k, 4 * HF, 4), v("ct"), v("xh", HF * k, HF * k + HF), 0.0, A.mult, A.add)
-        quant(v("qG"), v("pG"), v("tG"))
         flags(0, 256 + pad)
-        down(4, 0, HF, start=True)
-        down(7, HF, HF, start=True)
-        flags(320, 512 + pad * 3 // 2)
-        down(4, 320, HF)
-        down(7, 320 + HF, 128)
-        flags(608, 800 + pad)
-        down(4, 608, 128)
-        down(4, 736, 128)
-        for k in range(2):
-            flags(864 + HF * k, 864 + HF * k + HF)
-            down(4 + 3 * k, 864 + HF * k, HF)
-        mm(4, HF, GE, pair("qG", "pG", 0, HF), False, True)
-        mm(7, HF, GO, pair("qG", "pG", 0, HF), False, True)
+        down(4, 0, 128, start=True)
+        down(7, 128, 192, start=True)
+        tt(v("xh", 0, 512, 32), v("dr", 15, C, 16), v("rs", 0, 16), A.add)
+        scan(v("wb", STEP + 128), v("k32"), v("xh"), 0.0, A.mult, A.add)
+        turn(v("tb", 128), v("wb", STEP + 128))
+        tt(d_far, ps(5, 64, 128), v("hold", C, E), A.is_le)
+        scan(v("dh"), v("k16", 0, H), d_far, 0.0, A.mult, A.add)
+        for c in FAR_ROWS:
+            row(c, 2, 3)
+        for c in range(16, V_SUMS):
+            ts(v("wb", STEP + 32 * (c - 16), STEP + 32 * (c - 15)), v("c128"), v("rs", c, c + 1), A.add, v("dh", 16 * c + 15 - C, 16 * c + 16 - C), A.add)
+        turn(v("tb", 0, 128), v("wb", STEP, STEP + 128))
+        flags(320, 512 + pad)
+        down(4, 320, 128)
+        down(7, 448, 128)
+        flags(576, 768 + pad)
+        down(4, 576, 128)
+        down(4, 704, 128)
+        flags(832, 960)
+        down(4, 832, 128, stop=True)
+        flags(960, 1152)
+        down(7, 960, 192, stop=True)
         for b in range(4):
             mm(b, E, pair("eq", "ep", 128 * b, 128 * b + 128), pair(qn, pn, 0, E))
             act(v("ff", b, 4 * E, 4), ps(b), AF.Copy)
-        for k in range(2):
-            tt(v("uu", HF * k, HF * k + HF), ps(4 + 3 * k, 0, HF), v("kn", HF * k, HF * k + HF), A.subtract)
-        mid = 32.0 * 192
-        for k in range(2):
-            act(v("na", HF * k, HF * k + HF), v("uu", HF * k, HF * k + HF), AF.Abs, bias=-mid)
-        for k in range(2):
-            act(v("ne", HF * k, HF * k + HF), v("na", HF * k, HF * k + HF), AF.Relu, bias=1.0, scale=-1.0)
-        ts(v("lt"), v("uu"), mid, A.is_gt, -1.0, A.mult)
-        ts(v("ng"), v("uu"), mid, A.is_lt)
-        scan(v("qf"), kf, v("lt"), 0.0, A.mult, A.add)
-        scan(rev("qb", 0, E), rev("kx", 0, E), rev("ng", 0, E), 0.0, A.mult, A.add)
-        for k in range(2):
-            scan(v("tF", k, 4 * HF, 4), v("qf", HF * k, HF * k + HF), v("ne", HF * k, HF * k + HF), 0.0, A.min, A.mult)
-            scan(v("tF", 2 + k, 4 * HF, 4), v("qb", HF * k, HF * k + HF), v("ne", HF * k, HF * k + HF), 0.0, A.max, A.mult)
-        quant(v("qF"), v("pF"), v("tF"))
-        for bank, G in ((5, GE), (4, GE), (6, GO), (7, GO)):
-            mm(bank, HF, G, pair("qF", "pF", 0, HF))
-        act(v("nd", 0, HF), ps(4, 0, HF), AF.Copy, scale=-1.0)
-        act(v("nd", HF, E), ps(7, 0, HF), AF.Copy, scale=-1.0)
-        catch("capb", ps(5, 0, HF), 0, HF)
-        catch("capb", ps(6, 0, HF), HF, E)
+        tt(v("xf", 0, 128), ps(4, 0, 128), v("kn", 0, 128), A.subtract)
+        tt(v("xf", 128, E), ps(7, 0, 192), v("kn", 128, E), A.subtract)
+        for a, b in U_CUTS:
+            tt(v("uu", 16 * a, 16 * b), ind(v("tb", 128), v("lh", a, b)), v("xf", 16 * a, 16 * b), A.subtract)
+        tt(v("uu", C, E), ind(v("tb", 0, 128), v("lh", 0, 4)), v("xf", C, E), A.subtract)
+        mid, halves = -32.0 * 192, ((0, HF), (HF, E))
+        for a, b in halves:
+            act(v("na", a, b), v("uu", a, b), AF.Abs, bias=-mid)
+        for a, b in halves:
+            act(v("ne", a, b), v("na", a, b), AF.Relu, bias=1.0, scale=-1.0)
+        for a, b in ((0, HF + 16), (HF + 16, E)):
+            ts(v("tF", 4 * a + 1, 4 * b, 4), v("uu", a, b), mid, A.is_lt, -1.0, A.mult)
+            ts(v("tF", 4 * a + 3, 4 * b, 4), v("uu", a, b), mid, A.is_gt)
+        scan(v("qf", 0, HF), v("kx", 15, 15 + HF), v("tF", 1, 4 * HF, 4), 0.0, A.mult, A.add)
+        scan(v("qf", HF, E + 16), v("kx", HF - 1, E + 15), v("tF", 4 * (HF - 16) + 1, 4 * E, 4), 0.0, A.mult, A.add)
+        scan(rev("qb", 0, HF + 16), rev("kx", 0, HF + 16), rev("tF", 3, 4 * (HF + 16), 4), 0.0, A.mult, A.add)
+        scan(rev("qb", HF + 16, E + 16), rev("kx", HF, E), rev("tF", 4 * HF + 3, 4 * E, 4), 0.0, A.mult, A.add)
+        for k, (a, b) in enumerate(halves):
+            scan(v("tF", 4 * a, 4 * b, 4), v("qf", a + 16 * k, b + 16 * k), v("ne", a, b), 0.0, A.min, A.mult)
+            scan(v("tF", 4 * a + 2, 4 * b, 4), v("qb", a + 16 * k, b + 16 * k), v("ne", a, b), 0.0, A.max, A.mult)
+            quant(v("qF", a, b), v("pF", a, b), v("tF", 4 * a, 4 * b))
+            mm(5 + k, b - a, GE, pair("qF", "pF", a, b))
+            mm(4 + 3 * k, b - a, GE, pair("qF", "pF", a, b))
+            act(v("nd", a, b), ps(4 + 3 * k, 0, b - a), AF.Copy, scale=-1.0)
+            catch("capb", ps(5 + k, 0, b - a), a, b)
         listed("lpos", "capb", E)
         scan(v("mx"), v("one"), v("nd"), 0.0, A.add, A.min)
         act(v("nen", 16, 16 + E), v("mx"), AF.Sign, scale=-1.0)
@@ -405,12 +421,13 @@ def rank_program(g, core, T, topo):
         listed4("lo", "capv", E)
         act(v("yy"), ind(v("ff"), v("lo")), AF.Copy)
         ts(v("nh"), v("ww"), ca, A.is_equal, -2.0, A.mult)
-        scan(v("npf"), v("lead"), v("nh"), v("sc", 0, 1), A.add, A.add)
-        scan(v("xx", 16, C + 16), v("npf"), v("nh"), 0.0, A.min, A.mult)
-        turn(v("tr", 0, C), v("xx", 16, C + 16))
-        turn(v("tr", C, 544), v("xx"))
-        scan(v("su"), v("k16"), v("tr"), 0.0, A.mult, A.add)
-        ts(v("lrk"), ind(v("su"), v("lt_", 0, 1)), -4.0, A.add, 0.25, A.mult)
+        scan(v("xx", 16, C + 16), v("lead"), v("nh"), v("sc", 0, 1), A.add, A.add)
+        ts(v("xm", 16, C + 16), v("ww"), ca, A.is_le, -HOLD, A.mult)
+        for x, y in (("xx", "tr"), ("xm", "tn")):
+            turn(v(y, 0, C), v(x, 16, C + 16))
+            turn(v(y, C, 544), v(x))
+        scan(rev("su", 0, 544), rev("tn", 0, 544), rev("tr", 0, 544), 0.0, A.add, A.max)
+        ts(v("lrk"), ind(v("su"), v("lt_", 0, 1)), 2.0, A.add, -0.5, A.mult)
         scan(v("ra"), v("neg"), v("nen", 15, 15 + E), 0.0, A.add, A.mult)
         scan(rev("sm", 0, E), rev("cs", 0, E), rev("ra", 0, E), 0.0, A.add, A.max)
         catch("cap2", v("sm", 0, C), 0, C, "tab4")
@@ -421,15 +438,20 @@ def rank_program(g, core, T, topo):
         ts(v("le"), v("cap3", 3, K, 4), 4.0, A.mult, col(7), A.add)
         if G_CUT < 64:
             ts(v("gg", 16 * G_CUT, 4 * C), ind(v("yy"), v("lmir", G_CUT, 64)), -0.5, A.mult)
-        for a, b in zip(A_CUTS, A_CUTS[1:]):
-            act(v("ge", 16 * a, 16 * b), ind(v("gg"), v("le", a, b)), AF.Copy)
+            ops[-1][2] += regs(v("eb"))
+        for q, a, b in A_CUTS:
+            if q == "S":
+                act(v("ge", 16 * a, 16 * b), ind(v("gg"), v("le", a, b)), AF.Copy)
+            else:
+                cp(v("ge", 16 * a, 16 * b), ind(v("gg"), v("le", a, b)))
+        for q, a, b in A_CUTS:
             tt(v("at", 16 * a, 16 * b), ind(v("yy"), v("le", a, b)), v("ge", 16 * a, 16 * b), A.add)
         an, sn = "aq%d" % t, "ap%d" % t
         quant(v(an, K, K + 128), v(sn, K, K + 128), v("at"))
         send(far_to, an, sn, K, 2 * K, 0, "arA%d" % t)
         lands(far_from, an, sn, 0, K, "arA%d" % t)
         mark = len(ops)
-        ts(v("f4"), ind(v("su"), v("lt_", 0, 1)), -4.0, A.add, 0.25, A.mult)
+        ts(v("f4"), ind(v("su"), v("lt_", 0, 1)), 2.0, A.add, -0.5, A.mult)
         ts(v("f5"), v("f4"), float(K), A.is_ge, HOLD, A.mult)
         tt(v("f6"), v("f5"), v("f4"), A.add)
         tt(v("f3"), v("f6"), v("iws"), A.min)
@@ -444,29 +466,29 @@ def rank_program(g, core, T, topo):
             catch("capb", v("sm"), 0, E)
             listed("lpos", "capb", E)
             scan(v("ob"), v("vv"), v("it"), LIFT, A.min, A.add)
-            act(v("lmo"), ind(v("ob"), v("lpos")), AF.Identity, bias=-(LIFT + DROP))
-            dma("Y", T.lm[:], T.lmo[0:128:16, :], regs(v("lmo")), [], "st0")
         late.update(range(mark, len(ops)))
         for b in (2, 3, 0, 1):
             mm(b, 128, pair("wq", "wp", 128 * b, 128 * b + 128), pair(an, sn, 0, 128))
             tt(v("zw", W * b, W * b + K), ps(b, 0, K), v("a32", b, 4 * K, 4), A.add)
+        for q, b, lo, hi in X_CUTS:
+            out, src = v(X[t + 1], 64 * lo + b, 64 * hi, 4), ind(v("zw", W * b, W * b + W), v("lsel", lo, hi))
+            if q == "S":
+                act(out, src, AF.Copy, scale=0.03125)
+            else:
+                ts(out, src, 0.03125, A.mult)
         for k in range(2):
-            for b in (2, 3, 0, 1):
-                out, src = v(X[t + 1], 512 * k + b, 512 * k + 512, 4), ind(v("zw", W * b, W * b + W), v("lsel", 8 * k, 8 * k + 8))
-                if b >= 2 - k:
-                    act(out, src, AF.Copy, scale=0.03125)
-                else:
-                    ts(out, src, 0.03125, A.mult)
-                    late.add(len(ops) - 1)
             quant(v("q%d" % (t + 1), 128 * k, 128 * k + 128), v("p%d" % (t + 1), 128 * k, 128 * k + 128), v(X[t + 1], 512 * k, 512 * k + 512))
 
+    act(v("lmo"), ind(v("ob"), v("lpos")), AF.Identity, bias=-(LIFT + DROP))
+    ops[-1][2] += regs(v("x2"))
+    dma("Y", T.lm[:], T.lmo[0:128:16, :], regs(v("lmo")), [], "st0")
     for k in range(2):
         mm(4 + k, 128, pair("vq", "vp", 0, 128), pair("q2", "p2", 128 * k, 128 * k + 128))
         cp(v("yo", 128 * k, 128 * k + 128), ps(4 + k, 0, 128))
+        dma("YS"[k], T.y[:, 128 * k:128 * k + 128], T.yo[:, 128 * k:128 * k + 128], regs(v("yo", 128 * k, 128 * k + 128)), [], "st%d" % (2 + 5 * k))
     dma("Y", T.oc[:], T.q2[:].bitcast(dt.uint8), regs(v("q2")), [], "st1")
     for k in range(4):
         dma("S" if k % 2 else "Y", T.osc[4 * k:4 * k + 4, :], T.p2[32 * k:32 * k + 4, :], regs(v("p2")), [], "st%d" % (3 + k))
-    dma("S", T.y[:], T.yo[:], regs(v("yo")), [], "st2")
     emit(g, T, ops, sent[0], first, late)
 
 
@@ -478,12 +500,30 @@ def ordered(ops, deps, first, late):
             for j in deps[i]:
                 visit(j)
             place[i] = len(place)
-    for i in range(first, n):
+    for i in list(range(first, n)) + list(range(first)):
         visit(i)
-    users, open_ = [[] for o in ops], [len(d) for d in deps]
-    for i in range(n):
+    users, tail = [[] for o in ops], [o[7] for o in ops]
+    for i in range(n - 1, -1, -1):
         for j in deps[i]:
             users[j].append(i)
+            tail[j] = max(tail[j], ops[j][7] + WAKE + tail[i])
+    plain, best = eager(ops, deps, users, place, late), None
+    for share in SHARES:
+        ahead = sorted(range(n), key=lambda i: (plain[i] - share * (plain[i] + tail[i]), place[i]))
+        start = eager(ops, deps, users, {i: k for k, i in enumerate(ahead)}, late) if share else plain
+        back = placed(ops, users, sorted(range(n), key=lambda i: (-start[i] - ops[i][7], -place[i])), True)
+        start = placed(ops, deps, sorted(range(n), key=lambda i: (-back[i] - ops[i][6], place[i])), False)
+        end = max(start[i] + ops[i][7] for i in start)
+        if best is None or end < best[0]:
+            best = (end, start)
+    return sorted(range(n), key=lambda i: (best[1][i], place[i]))
+
+
+SHARES = (0.0, 0.2, 0.5, 1.0)
+
+
+def eager(ops, deps, users, place, late):
+    n, open_ = len(ops), [len(d) for d in deps]
     ready, start, free, now = {i: 0.0 for i in range(n) if not deps[i]}, {}, {}, 0.0
     while ready:
         moved = False
@@ -494,7 +534,7 @@ def ordered(ops, deps, first, late):
             for i in sorted((i for i in ready if ops[i][0][0] == q), key=lambda i: place[i]):
                 if ready[i] > now:
                     soon = min(soon, ready[i])
-                elif now + ops[i][6] * (1.0 if i in late else 1.0 - SHARE[i >= first]) <= soon:
+                elif i not in late or now + ops[i][6] <= soon:
                     start[i], free[q], moved = now, now + ops[i][6], True
                     del ready[i]
                     for k in users[i]:
@@ -504,10 +544,31 @@ def ordered(ops, deps, first, late):
                     break
         if not moved:
             now = min(x for x in list(ready.values()) + list(free.values()) if x > now)
-    return sorted(range(n), key=lambda i: (start[i], place[i]))
+    return start
 
 
-SHARE, KEPT = (0.7, 0.6), {}
+def placed(ops, before, order, back):
+    start, taken = {}, {}
+    for i in order:
+        busy, done = ops[i][6], ops[i][7]
+        at = done - busy if back else 0.0
+        for j in before[i]:
+            if ops[i][0] == ops[j][0] in "PG":
+                at = max(at, start[j] + ops[j][6])
+            else:
+                at = max(at, start[j] + ops[j][6] + WAKE + done - busy if back else start[j] + ops[j][7] + WAKE)
+        row = taken.setdefault(ops[i][0], [])
+        for a, b in row:
+            if at + busy <= a:
+                break
+            at = max(at, b)
+        start[i] = at
+        row.append((at, at + busy))
+        row.sort()
+    return start
+
+
+KEPT = {}
 
 
 def emit(g, T, ops, sent, first, late):

from concourse.mybir import dt, AluOpType, ActivationFunctionType, AxisListType

A = AluOpType
AF = ActivationFunctionType
C, H, E, K, J, R = 256, 64, 320, 96, 3, 2
BIG = 2.0 ** 96
HOLD = 1024.0
LIFT, DROP = 512.0, 1152.0
TINY = 2.0 ** -18
CODE, PLANE, BF, F16, F32, U16, I32 = "float8_e4m3fn_x4", "uint8", "bfloat16", "float16", "float32", "uint16", "int32"
S_ROWS, V_SUMS = (17, 16, 15, 14, 13), 18
FAR_ROWS, STEP = (17, 16, 19, 18), 304
TILE = {"D": (13, 0), "C": (9, 320), "B": (5, 576), "A": (1, 704), "E": (16, 832)}
G_CUT, A_CUTS = 56, (("V", 0, 6), ("S", 6, 14), ("S", 14, 24))
X_CUTS = (("S", 2, 0, 16), ("S", 3, 0, 16), ("V", 0, 0, 16), ("V", 1, 0, 12), ("S", 1, 12, 16))
U_CUTS, H_CUTS = ((0, 8), (8, 16)), ((192, 256), (128, 192))
W = C + K
HF = E // 2


def _sb(n, d):
    return ("sbuf", [128, n], d)


SCRATCH = {
    "xt": _sb(1024, BF), "ut": _sb(512, BF), "vt": _sb(512, BF), "x1": _sb(1024, BF), "x2": _sb(1024, BF),
    "wq": _sb(512, CODE), "wp": _sb(512, PLANE), "uq": _sb(128, CODE), "up": _sb(128, PLANE),
    "udq": _sb(128, CODE), "udp": _sb(128, PLANE), "vq": _sb(128, CODE), "vp": _sb(128, PLANE),
    "eq": _sb(512, CODE), "ep": _sb(512, PLANE), "gq": _sb(384, CODE), "gp": _sb(384, PLANE),
    "q0": _sb(E, CODE), "p0": _sb(E, PLANE), "q1": _sb(E, CODE), "p1": _sb(E, PLANE), "q2": _sb(C, CODE), "p2": _sb(C, PLANE),
    "aq0": _sb(K + 128, CODE), "ap0": _sb(K + 128, PLANE), "aq1": _sb(K + 128, CODE), "ap1": _sb(K + 128, PLANE),
    "tl": _sb(4 * 1168, BF), "ql": _sb(1152, CODE), "pl": _sb(1152, PLANE),
    "tF": _sb(4 * E, BF), "qF": _sb(E, CODE), "pF": _sb(E, PLANE),
    "at": _sb(512, BF), "a32": _sb(4 * K, BF),
    "tm": _sb(E + 16, BF), "ih": _sb(E, F16), "wd": _sb(520, BF), "gi": _sb(256, BF), "mr": _sb(128, BF), "gt": _sb(1040, BF),
    "col": _sb(16, F32), "pi": _sb(16, F32), "ul": _sb(8, U16), "uf": _sb(16, F32), "lt_": _sb(2, U16),
    "m1": _sb(E + 16, BF), "c1": _sb(E, BF), "k16": _sb(E, BF),
    "inc": _sb(E, F32), "kn": _sb(E, F32), "xf": _sb(E, F32), "it": _sb(E, F32), "ib": _sb(C, BF), "kx": _sb(E + 16, BF), "cc": _sb(K, BF),
    "eqa": _sb(E, BF), "t1": _sb(E, F16), "sp": _sb(E, F16), "tab": _sb(E, F16),
    "tm4": _sb(E + 4, BF), "k4a": _sb(E + 4, BF), "k4": _sb(E + 4, BF), "eq4": _sb(E, BF), "t14": _sb(E, F16), "sp4": _sb(E, F16), "tab4": _sb(E, F16),
    "lead": _sb(C, BF), "neg": _sb(E, BF), "one": _sb(E, BF), "iws": _sb(16, F32),
    "val": _sb(E, F32), "hold": _sb(E, F32), "sg": _sb(6 * E, BF), "junk": _sb(16 * 210, BF), "rs": _sb(20, F32), "dr": _sb(C, BF), "dh": _sb(H, F32),
    "wb": _sb(STEP + 640, BF), "tb": _sb(640, BF), "k32": _sb(512, BF), "hf": _sb(STEP + 32, BF), "c128": _sb(32, BF), "lh": _sb(16, U16), "xh": _sb(2 * C, BF),
    "uu": _sb(E, BF), "ne": _sb(E, BF), "na": _sb(E, BF), "qf": _sb(E + 16, BF), "qb": _sb(E + 16, BF),
    "capb": _sb(E, F16), "capv": _sb(E, F16), "cap2": _sb(E, F16), "cap3": _sb(K, F32), "nd": _sb(E, BF), "vv": _sb(E, BF),
    "mx": _sb(E, BF), "nen": _sb(E + 16, BF), "cs": _sb(E, BF), "ra": _sb(E, F16), "sm": _sb(E, F16), "ww": _sb(C, BF), "sc": _sb(2, F32),
    "nh": _sb(C, BF), "xm": _sb(C + 32, BF), "xx": _sb(C + 32, BF), "tr": _sb(544, BF), "tn": _sb(544, BF), "su": _sb(544, BF), "eb": _sb(C, BF),
    "f3": _sb(16, F32), "f4": _sb(16, F32), "f5": _sb(16, F32), "f6": _sb(16, F32),
    "lpos": _sb(20, U16), "lo": _sb(80, U16), "lmir": _sb(64, U16), "lrk": _sb(16, U16), "le": _sb(24, U16), "lsel": _sb(16, U16),
    "ff": _sb(4 * E, BF), "yy": _sb(4 * E, BF), "gg": _sb(4 * C, BF), "ge": _sb(4 * K, BF), "zw": _sb(4 * W, BF),
    "lmo": _sb(E, F32), "ob": _sb(E, F32), "yo": _sb(C, F32),
}
PART = {}
for _n, _names in (("cf", "uf iws"), ("df", "f3 f4 f5 f6 rs sc"), ("ls", "lpos lo lmir lrk le lsel"), ("lc", "ul lt_ lh"),
                   ("cb", "hf c128 cc eq4 eqa lead neg one ib")):
    _at = 0
    for _k in _names.split():
        _w, (_p, _c), _d = SCRATCH.pop(_k)
        PART[_k] = (_n, _at, _c)
        _at += -(-_c // 16) * 16
    SCRATCH[_n] = _sb(_at, _d)
for _b in range(8):
    SCRATCH["ps%d" % _b] = ("psum", [128, 512], F32)
SEMAPHORES = ["sV", "sS", "sP", "sG", "ldx0", "ldx1", "ldu", "ldv", "ldw", "ldp", "ldz0", "ldz1", "ldz2", "arH0", "arH1", "arA0", "arA1", "sent",
              "st0", "st1", "st2", "st3", "st4", "st5", "st6", "st7"]
CYC, WAKE, ISSUE, FIRST, FLIGHT, LOAD = 0.83, 200.0, 300.0, 1000.0, 1900.0, 1400.0


def _meet(a, b):
    if a[0] != b[0]:
        return False
    if a[0].startswith("ps"):
        return True
    if a[2] <= b[1] or b[2] <= a[1]:
        return False
    return not (a[3] == b[3] and a[3] > 1 and (a[1] - b[1]) % a[3] != 0)


def rank_program(g, core, T, topo):
    rank = T.rank_of(core)
    if rank is None:
        return
    N = len(T.cores)
    ops = []

    def v(name, a=0, b=None, s=1):
        if name in PART:
            name, at, n = PART[name]
            a, b = at + a, at + (n if b is None else b)
        b = SCRATCH[name][1][1] if b is None else b
        return (T[name][:, a:b:s] if s > 1 else T[name][:, a:b], (name, a, b, s))

    def rev(name, a, b, s=1):
        return (T[name][:, b - 1::-s] if a < s else T[name][:, b - 1:a - 1:-s], (name, a, b, s))

    def ind(win, off):
        return (win[0].indirect(off[0]), win[1], off[1])

    def ap(x):
        return x[0] if isinstance(x, tuple) else x

    def regs(*xs):
        return [r for x in xs if isinstance(x, tuple) for r in x[1:]]

    def num(x):
        n, a, b, s = x[-1]
        return 16 * (b - a) if len(x) == 3 else -(-(b - a) // s)

    def cost(out, *ins, rate=None):
        if len(out) == 3:
            return 50 + 3.5 * CYC * num(out)
        if len(ins[0]) == 3:
            return 60 + 1.5 * CYC * num(out)
        if rate is None:
            rate = 0.5 if all(SCRATCH[x[1][0]][2] in (BF, F16, U16) for x in (out,) + ins) else 1.0
        return 25 + CYC * max(64, rate * num(ins[0]))

    def op(q, call, reads, writes, busy, sem=None, count=16, done=None):
        ops.append([q, call, reads, writes, sem, count, busy, busy if done is None else done])

    def ts(out, in0, s1, o0, s2=None, o1=None):
        if o1 is None:
            op("V", lambda: g.vector.tensor_scalar(out[0], in0[0], ap(s1), None, o0), regs(in0, s1), regs(out), cost(out, in0))
        else:
            op("V", lambda: g.vector.tensor_scalar(out[0], in0[0], ap(s1), ap(s2), o0, o1), regs(in0, s1, s2), regs(out), cost(out, in0))

    def tt(out, a, b, o):
        both = not (a[1][0].startswith("ps") or b[1][0].startswith("ps"))
        op("V", lambda: g.vector.tensor_tensor(out[0], a[0], b[0], o), regs(a, b), regs(out), cost(out, a, rate=2.0 if both else 1.0))

    def cp(out, a):
        op("V", lambda: g.vector.tensor_copy(out[0], a[0]), regs(a) + list(out[2:]), [out[1]], cost(out, a))

    def scan(out, d0, d1, init, o0, o1):
        op("V", lambda: g.vector.tensor_tensor_scan(out[0], d0[0], d1[0], ap(init), o0, o1), regs(d0, d1, init), regs(out), cost(out, d0, d1))

    def turn(out, a):
        op("V", lambda: g.vector.transpose(out[0], a[0]), regs(a), regs(out), cost(out, a))

    def fill(out, c):
        op("V", lambda: g.vector.memset(out[0], c), [], regs(out), cost(out, out))

    def quant(q, p, t):
        op("V", lambda: g.vector.quantize_mx(q[0], p[0], t[0]), regs(t), regs(q, p), 37 + 0.22 * num(t))

    def act(out, a, f, bias=None, scale=1.0, acc=None):
        kw = {} if scale == 1.0 else {"scale": ap(scale)}
        if bias is not None:
            kw["bias"] = ap(bias)
        if acc is not None:
            kw["accum_out"] = acc[0]
        op("S", lambda: g.scalar.activation(out[0], a[0], f, **kw), regs(a, bias, scale), regs(out, acc), cost(out, a, rate=1.0) + (20 if acc else 0))

    def lin(out, a, scale, bias):
        act(out, a, AF.Identity, bias=bias, scale=scale)

    def mm(bank, n, w, x, start=True, stop=True):
        out = v("ps%d" % bank, 0, n)
        op("P", lambda: g.tensor.matmul_mx(out[0], w[0][0], w[1][0], x[0][0], x[1][0], start, stop), regs(*w, *x), regs(out), 0.63 * (n + 16))

    def iota(out, pat, base, cm):
        op("G", lambda: g.iota(out[0], pat, base, cm, allow_small_or_imprecise_dtypes=True), [], regs(out), 130 + 2 * CYC * num(out))

    def gfill(out, c):
        iota(out, [[0, num(out)]], c, 0)

    def dma(q, out, in_, reads, writes, sem):
        e = g.sync if q == "Y" else g.scalar
        op(q, lambda: e.dma_start(out, in_), reads, writes, 60, sem, done=LOAD)

    sent = [0]

    def send(dst, qn, pn, a, b, at, sem):
        rid, pid = topo.addr(dst)[:2]
        mask = topo.mask(core, dst)
        n = len(topo.engines(core, dst))
        so, si = v(pn, at, at + b - a), v(pn, a, b)
        co, ci = v(qn, at, at + b - a), v(qn, a, b)
        op("G", lambda: g.remote_dma(co[0].bitcast(dt.uint8), ci[0].bitcast(dt.uint8), T.sem[sem], T.sem.sent, pid, rid, mask), regs(ci), [(sem, 0, 1, 1)], ISSUE + (0 if sent[0] else FIRST), "remote")
        op("G", lambda: g.remote_dma(so[0], si[0], T.sem[sem], T.sem.sent, pid, rid, mask), regs(si), [(sem, 1, 2, 1)], ISSUE, "remote")
        sent[0] += 2 * n

    def lands(src, qn, pn, a, b, sem):
        op("far", None, [(sem, 0, 2, 1)], regs(v(qn, a, b), v(pn, a, b)), 0, sem, 2 * len(topo.engines(src, core)), done=FLIGHT)

    def ps(b, a=0, e=E):
        return v("ps%d" % b, a, e)

    def col(i):
        return v("col", i, i + 1)

    def pair(qn, pn, a, b):
        return (v(qn, a, b), v(pn, a, b))

    prev, nxt = T.cores[(rank - 1) % N], T.cores[(rank + 1) % N]
    far_to, far_from = T.cores[(rank + J) % N], T.cores[(rank - J) % N]

    dma("Y", T.xt[:, 0:512], T.x[:, 0:512], [], regs(v("xt", 0, 512)), "ldx0")
    dma("S", T.ut[:], T.u[:], [], regs(v("ut")), "ldu")
    dma("Y", T.xt[:, 512:1024], T.x[:, 512:1024], [], regs(v("xt", 512, 1024)), "ldx1")

    ca, cg, cpar = col(0), col(15), col(1)
    cp_, M1 = v("pi", 0, 1), 1.5 * 2.0 ** 23
    iota(cp_, [[0, 1]], 0, 1)
    ts(v("pi", 4, 5), cp_, 1 / 16, A.mult, 1 / 64 - 0.5, A.add)
    ts(cg, v("pi", 4, 5), M1, A.add, M1, A.subtract)
    ts(ca, cg, -16.0, A.mult, cp_, A.add)
    for k, m in enumerate((1 / 32, 1 / 4, 17 / 32)):
        lin(v("pi", 1 + k, 2 + k), cp_, m, 1 / 64 - 0.5)
    lin(v("pi", 5, 8), v("pi", 1, 4), 1.0, M1)
    lin(v("pi", 10, 13), v("pi", 5, 8), 1.0, -M1)
    lin(col(14), v("pi", 10, 11), -32.0, cp_)
    lin(col(11), v("pi", 11, 12), -4.0, cp_)
    lin(col(3), cg, -4.0, v("pi", 11, 12))
    lin(col(2), v("pi", 12, 13), -2.0, cp_)
    lin(cpar, cg, 1.0, col(2))
    iota(v("uf"), [[16, 16]], 0, 0)
    iota(v("gi"), [[1, 8], [0, 32]], 0, 0)
    iota(v("mr"), [[1, 128]], 0, 0)
    iota(v("tm"), [[0, 21], [1, 16]], 0, 0)
    fill(v("wd"), 0.0)
    ts(v("wd", 3, 515, 4), v("mr"), cp_, A.is_equal)
    for b in range(4):
        quant(v("eq", 128 * b, 128 * b + 128), v("ep", 128 * b, 128 * b + 128), v("wd", 3 - b, 515 - b))
    cp(v("ul"), v("uf", 0, 8))
    ts(v("m1"), v("tm"), ca, A.not_equal, BIG, A.mult)
    act(v("kx"), v("m1"), AF.Sign)
    kb, kf = v("kx", 0, E), v("kx", 15, 15 + E)
    act(v("k16", 0, E), v("tm", 0, E), AF.Sign)
    lin(v("c1"), v("k16", 0, E), -2 * BIG, 2 * BIG)
    fill(v("tl", 4 * 656, 4 * 832), 0.0)
    for k, (a, b) in enumerate(((464, 576), (208, 320), (1088, 1168))):
        dma("Y", T.tl[:, 4 * a:4 * b], T.tl[:, 4 * 656:4 * (656 + b - a)], regs(v("tl", 4 * 656, 4 * (656 + b - a)), v("xt")), regs(v("tl", 4 * a, 4 * b)), "ldz%d" % k)
    lin(v("rs", 0, 1), ca, 0.0, 0.0)
    lin(col(6), v("kx", 0, 1), -DROP, DROP - LIFT)
    lin(col(9), cpar, 272.0, 0.0)
    lin(col(10), ca, 1.0, 0.5)
    ts(v("lt_", 0, 1), ca, 16.0, A.mult, col(9), A.add)
    lin(v("iws"), v("uf"), 1.0, ca)
    lin(v("iws"), v("iws"), 1.0, float(K))
    fill(v("gt", 512, 1026, 2), 0.0)
    for a in (0, 1, 513):
        ts(v("gt", a, a + 511, 2), v("gi"), cg, A.is_equal)
    for k, a in enumerate((0, 513)):
        quant(v("gq", 128 * k, 128 * k + 128), v("gp", 128 * k, 128 * k + 128), v("gt", a, a + 512))
    lin(v("kn", 0, 1), ca, 32.0, 15.5 - 32.0 * 192)
    lin(v("inc"), kf, -512.0, 479.0)
    scan(v("kn", 1, E), v("inc", 1, E), v("kx", 0, E - 1), v("kn", 0, 1), A.add, A.min)
    quant(v("q0", 0, 128), v("p0", 0, 128), v("xt", 0, 512))
    quant(v("q0", 128, C), v("p0", 128, C), v("xt", 512, 1024))
    send(prev, "q0", "p0", 0, H, C, "arH0")
    gfill(v("hf", STEP, STEP + 32), 0)
    act(v("hf", 0, STEP), v("tm", 0, STEP), AF.Identity, bias=-0.5, scale=0.0)
    for c in range(16, 20):
        lin(v("kn", 16 * c, 16 * c + 16), v("kn", 16 * c, 16 * c + 16), 1.0, 128.0 if c < V_SUMS else 8.0 * c)
    ts(v("lh"), v("uf"), 2.0, A.mult, col(14), A.add)
    gfill(v("k32"), 1)
    gfill(v("k32", 0, 512, 32), 0)
    gfill(v("xh"), 0)
    gfill(v("c128"), -128)
    iota(v("it"), [[1, E]], int(LIFT + DROP), 0)
    lin(v("eqa"), kb, -1.0, 1.0)
    lin(v("t1"), v("kx", 1, E + 1), DROP, -DROP)
    act(v("ih"), v("it"), AF.Copy)
    scan(v("sp"), v("ih"), v("eqa"), 0.0, A.max, A.mult)
    scan(v("tab"), v("t1"), v("sp"), -DROP, A.min, A.add)
    iota(v("tm4"), [[0, 81], [1, 4]], 0, 0)
    act(v("k4a"), v("tm4"), AF.Abs, bias=col(3), scale=-1.0)
    act(v("k4"), v("k4a"), AF.Sign)
    lin(v("eq4"), v("k4", 0, E), -1.0, 1.0)
    lin(v("t14"), v("k4", 1, E + 1), DROP, -DROP)
    scan(v("sp4"), v("ih"), v("eq4"), 0.0, A.max, A.mult)
    scan(v("tab4"), v("t14"), v("sp4"), -DROP, A.min, A.add)
    lin(v("cc"), v("k4", 0, K), -18 * HOLD, 17 * HOLD)
    lin(col(12), col(11), 1.0, 4 * (DROP - LIFT))
    lin(col(8), v("k4", 0, 1), -4 * DROP, col(12))
    lin(col(13), col(11), 1.0, 12 * HOLD)
    lin(col(7), col(3), -4 * HOLD, col(13))
    gfill(v("one"), 1)
    gfill(v("neg"), -1)
    gfill(v("nen", 0, 16), 0)
    for x in ("xx", "xm"):
        gfill(v(x, 0, 16), 0)
        gfill(v(x, C + 16, C + 32), 0)
    gfill(v("lead", 0, 1), -C)
    gfill(v("lead", 1, C), 0)
    iota(v("ib"), [[1, C]], 0, 0)
    gfill(v("at", 4 * K, 512), 0)
    quant(v("uq"), v("up"), v("ut"))
    op("V", lambda: g.vector.tensor_copy(T.udq[:].bitcast(dt.uint32), T.uq[:].bitcast(dt.uint32).indirect(v("ul")[0])), regs(v("uq"), v("ul")), regs(v("udq")), 220)
    act(v("udp"), ind(v("up"), v("ul")), AF.Copy)

    UD, GS, GE = pair("udq", "udp", 0, 128), pair("gq", "gp", 0, 128), pair("gq", "gp", 128, 256)

    def slot(c, a, b):
        first, at = TILE["ABCDE"[min((c - 1) // 4, 3) if c < 16 else 4]]
        return v("tl", 4 * (at + a) + c - first, 4 * (at + b), 4)

    def pivot(c):
        return v("hold", 16 * c + 15, 16 * c + 16)

    def row(c, bank_v, bank_s):
        n, total = 16 * c, v("rs", c, c + 1)
        if c in S_ROWS:
            at = E * S_ROWS.index(c)
            act(v("sg", at, at + n), ps(bank_s, 0, n), AF.Sign, bias=pivot(c), scale=-1.0)
            act(slot(c, 0, n), v("sg", at, at + n), AF.Relu, acc=total)
            return
        ts(slot(c, 0, n), ps(bank_v, 0, n), pivot(c), A.is_lt)
        if c >= V_SUMS:
            end = STEP + 32 * (c - 15)
            scan(v("wb", end - n - 32, end), v("hf", STEP - n, STEP + 32), slot(c, 0, n + 32), v("dh", n + 15 - C, n + 16 - C), A.add, A.add)
        else:
            act(v("junk", 8 * c * (c - 1), 8 * c * (c + 1)), slot(c, 0, n), AF.Copy, acc=total)

    def flags(a, b):
        quant(v("ql", a, b), v("pl", a, b), v("tl", 4 * a, 4 * b))

    def down(bank, a, n, start=False, stop=False):
        mm(bank, n, GS, pair("ql", "pl", a, a + n), start, stop)

    def hold(a, b, bank, at):
        tt(v("val", a, b), ps(bank, a - at, b - at), v("m1", a, b), A.add)
        scan(v("hold", a, b), v("c1", a, b), v("val", a, b), 0.0, A.add, A.min)

    def catch(out, data, a, b, tab="tab"):
        scan(v(out, a, b), data, v(tab, a, b), -DROP, A.max, A.add)

    def listed(out, caught, n):
        ts(v(out, 0, n // 16), v(caught, 15, n, 16), col(6), A.add)

    def listed4(out, caught, n):
        ts(v(out), v(caught, 3, n, 4), 4.0, A.mult, col(8), A.add)

    X, first, late = ["xt", "x1", "x2"], len(ops), set()
    for t in range(R):
        qn, pn, last = "q%d" % t, "p%d" % t, t == R - 1
        pad = 64 if t == 0 else 0
        if t:
            send(prev, qn, pn, 0, H, C, "arH%d" % t)
        lands(nxt, qn, pn, C, E, "arH%d" % t)
        if t == 0:
            behind = regs(v("q0", C, E))
            dma("Y", T.wq[:].bitcast(dt.uint8), T.wc[:], behind, regs(v("wq")), "ldw")
            dma("Y", T.wp[:], T.ws[:], behind, regs(v("wp")), "ldp")
            dma("Y", T.vt[:], T.v[:], behind, regs(v("vt")), "ldv")
        mm(6, 128, UD, pair(qn, pn, 0, 128))
        mm(0, C, UD, pair(qn, pn, 0, C))
        mm(1, C, UD, pair(qn, pn, 0, C))
        d_own, d_far = v("tl", 3, 4 * C, 4), slot(16, C, E)
        for a, b in H_CUTS:
            hold(a, b, 0, 0)
        hold(0, 128, 6, 0)
        mm(5, 128, UD, pair(qn, pn, E - 128, E))
        mm(3, E, UD, pair(qn, pn, 0, E))
        mm(2, E, UD, pair(qn, pn, 0, E))
        hold(C, E, 5, E - 128)
        for c in range(15, 0, -1):
            row(c, 0, 1)
        tt(d_own, ps(0, 0, C), v("hold", 0, C), A.is_le)
        scan(v("dr", 0, C), v("k16", 0, C), d_own, 0.0, A.mult, A.add)
        flags(0, 256 + pad)
        down(4, 0, 128, start=True)
        down(7, 128, 192, start=True)
        tt(v("xh", 0, 512, 32), v("dr", 15, C, 16), v("rs", 0, 16), A.add)
        scan(v("wb", STEP + 128), v("k32"), v("xh"), 0.0, A.mult, A.add)
        turn(v("tb", 128), v("wb", STEP + 128))
        tt(d_far, ps(5, 64, 128), v("hold", C, E), A.is_le)
        scan(v("dh"), v("k16", 0, H), d_far, 0.0, A.mult, A.add)
        for c in FAR_ROWS:
            row(c, 2, 3)
        for c in range(16, V_SUMS):
            ts(v("wb", STEP + 32 * (c - 16), STEP + 32 * (c - 15)), v("c128"), v("rs", c, c + 1), A.add, v("dh", 16 * c + 15 - C, 16 * c + 16 - C), A.add)
        turn(v("tb", 0, 128), v("wb", STEP, STEP + 128))
        flags(320, 512 + pad)
        down(4, 320, 128)
        down(7, 448, 128)
        flags(576, 768 + pad)
        down(4, 576, 128)
        down(4, 704, 128)
        flags(832, 960)
        down(4, 832, 128, stop=True)
        flags(960, 1152)
        down(7, 960, 192, stop=True)
        for b in range(4):
            mm(b, E, pair("eq", "ep", 128 * b, 128 * b + 128), pair(qn, pn, 0, E))
            act(v("ff", b, 4 * E, 4), ps(b), AF.Copy)
        tt(v("xf", 0, 128), ps(4, 0, 128), v("kn", 0, 128), A.subtract)
        tt(v("xf", 128, E), ps(7, 0, 192), v("kn", 128, E), A.subtract)
        for a, b in U_CUTS:
            tt(v("uu", 16 * a, 16 * b), ind(v("tb", 128), v("lh", a, b)), v("xf", 16 * a, 16 * b), A.subtract)
        tt(v("uu", C, E), ind(v("tb", 0, 128), v("lh", 0, 4)), v("xf", C, E), A.subtract)
        mid, halves = -32.0 * 192, ((0, HF), (HF, E))
        for a, b in halves:
            act(v("na", a, b), v("uu", a, b), AF.Abs, bias=-mid)
        for a, b in halves:
            act(v("ne", a, b), v("na", a, b), AF.Relu, bias=1.0, scale=-1.0)
        for a, b in ((0, HF + 16), (HF + 16, E)):
            ts(v("tF", 4 * a + 1, 4 * b, 4), v("uu", a, b), mid, A.is_lt, -1.0, A.mult)
            ts(v("tF", 4 * a + 3, 4 * b, 4), v("uu", a, b), mid, A.is_gt)
        scan(v("qf", 0, HF), v("kx", 15, 15 + HF), v("tF", 1, 4 * HF, 4), 0.0, A.mult, A.add)
        scan(v("qf", HF, E + 16), v("kx", HF - 1, E + 15), v("tF", 4 * (HF - 16) + 1, 4 * E, 4), 0.0, A.mult, A.add)
        scan(rev("qb", 0, HF + 16), rev("kx", 0, HF + 16), rev("tF", 3, 4 * (HF + 16), 4), 0.0, A.mult, A.add)
        scan(rev("qb", HF + 16, E + 16), rev("kx", HF, E), rev("tF", 4 * HF + 3, 4 * E, 4), 0.0, A.mult, A.add)
        for k, (a, b) in enumerate(halves):
            scan(v("tF", 4 * a, 4 * b, 4), v("qf", a + 16 * k, b + 16 * k), v("ne", a, b), 0.0, A.min, A.mult)
            scan(v("tF", 4 * a + 2, 4 * b, 4), v("qb", a + 16 * k, b + 16 * k), v("ne", a, b), 0.0, A.max, A.mult)
            quant(v("qF", a, b), v("pF", a, b), v("tF", 4 * a, 4 * b))
            mm(5 + k, b - a, GE, pair("qF", "pF", a, b))
            mm(4 + 3 * k, b - a, GE, pair("qF", "pF", a, b))
            act(v("nd", a, b), ps(4 + 3 * k, 0, b - a), AF.Copy, scale=-1.0)
            catch("capb", ps(5 + k, 0, b - a), a, b)
        listed("lpos", "capb", E)
        scan(v("mx"), v("one"), v("nd"), 0.0, A.add, A.min)
        act(v("nen", 16, 16 + E), v("mx"), AF.Sign, scale=-1.0)
        lin(v("cs"), v("nen", 16, 16 + E), HOLD, 2.0 - HOLD)
        cp(ind(v("vv"), v("lpos")), v("nd"))
        act(v("ww"), v("vv", 0, C), AF.Abs)
        act(v("junk", 0, C), v("ww"), AF.Sign, bias=col(10), scale=-1.0, acc=v("sc", 0, 1))
        catch("capv", v("vv"), 0, E, "tab4")
        listed4("lo", "capv", E)
        act(v("yy"), ind(v("ff"), v("lo")), AF.Copy)
        ts(v("nh"), v("ww"), ca, A.is_equal, -2.0, A.mult)
        scan(v("xx", 16, C + 16), v("lead"), v("nh"), v("sc", 0, 1), A.add, A.add)
        ts(v("xm", 16, C + 16), v("ww"), ca, A.is_le, -HOLD, A.mult)
        for x, y in (("xx", "tr"), ("xm", "tn")):
            turn(v(y, 0, C), v(x, 16, C + 16))
            turn(v(y, C, 544), v(x))
        scan(rev("su", 0, 544), rev("tn", 0, 544), rev("tr", 0, 544), 0.0, A.add, A.max)
        ts(v("lrk"), ind(v("su"), v("lt_", 0, 1)), 2.0, A.add, -0.5, A.mult)
        scan(v("ra"), v("neg"), v("nen", 15, 15 + E), 0.0, A.add, A.mult)
        scan(rev("sm", 0, E), rev("cs", 0, E), rev("ra", 0, E), 0.0, A.add, A.max)
        catch("cap2", v("sm", 0, C), 0, C, "tab4")
        listed4("lmir", "cap2", C)
        act(v("gg", 0, 16 * G_CUT), ind(v("yy"), v("lmir", 0, G_CUT)), AF.Copy, scale=-0.5)
        cp(ind(v("eb"), v("lrk")), v("ib"))
        scan(v("cap3"), v("cc"), v("eb", 0, K), 0.0, A.add, A.min)
        ts(v("le"), v("cap3", 3, K, 4), 4.0, A.mult, col(7), A.add)
        if G_CUT < 64:
            ts(v("gg", 16 * G_CUT, 4 * C), ind(v("yy"), v("lmir", G_CUT, 64)), -0.5, A.mult)
            ops[-1][2] += regs(v("eb"))
        for q, a, b in A_CUTS:
            if q == "S":
                act(v("ge", 16 * a, 16 * b), ind(v("gg"), v("le", a, b)), AF.Copy)
            else:
                cp(v("ge", 16 * a, 16 * b), ind(v("gg"), v("le", a, b)))
        for q, a, b in A_CUTS:
            tt(v("at", 16 * a, 16 * b), ind(v("yy"), v("le", a, b)), v("ge", 16 * a, 16 * b), A.add)
        an, sn = "aq%d" % t, "ap%d" % t
        quant(v(an, K, K + 128), v(sn, K, K + 128), v("at"))
        send(far_to, an, sn, K, 2 * K, 0, "arA%d" % t)
        lands(far_from, an, sn, 0, K, "arA%d" % t)
        mark = len(ops)
        ts(v("f4"), ind(v("su"), v("lt_", 0, 1)), 2.0, A.add, -0.5, A.mult)
        ts(v("f5"), v("f4"), float(K), A.is_ge, HOLD, A.mult)
        tt(v("f6"), v("f5"), v("f4"), A.add)
        tt(v("f3"), v("f6"), v("iws"), A.min)
        cp(v("lsel"), v("f3"))
        act(v("a32"), v("at", 0, 4 * K), AF.Copy, scale=32.0)
        for b in (2, 3, 0, 1):
            tt(v("zw", W * b + K, W * b + W), v("yy", b, 4 * C, 4), v("gg", b, 4 * C, 4), A.add)
            act(v("zw", W * b + K, W * b + W), v("zw", W * b + K, W * b + W), AF.Copy, scale=32.0)
        if not last:
            quant(v("vq"), v("vp"), v("vt"))
        else:
            catch("capb", v("sm"), 0, E)
            listed("lpos", "capb", E)
            scan(v("ob"), v("vv"), v("it"), LIFT, A.min, A.add)
        late.update(range(mark, len(ops)))
        for b in (2, 3, 0, 1):
            mm(b, 128, pair("wq", "wp", 128 * b, 128 * b + 128), pair(an, sn, 0, 128))
            tt(v("zw", W * b, W * b + K), ps(b, 0, K), v("a32", b, 4 * K, 4), A.add)
        for q, b, lo, hi in X_CUTS:
            out, src = v(X[t + 1], 64 * lo + b, 64 * hi, 4), ind(v("zw", W * b, W * b + W), v("lsel", lo, hi))
            if q == "S":
                act(out, src, AF.Copy, scale=0.03125)
            else:
                ts(out, src, 0.03125, A.mult)
        for k in range(2):
            quant(v("q%d" % (t + 1), 128 * k, 128 * k + 128), v("p%d" % (t + 1), 128 * k, 128 * k + 128), v(X[t + 1], 512 * k, 512 * k + 512))

    act(v("lmo"), ind(v("ob"), v("lpos")), AF.Identity, bias=-(LIFT + DROP))
    ops[-1][2] += regs(v("x2"))
    dma("Y", T.lm[:], T.lmo[0:128:16, :], regs(v("lmo")), [], "st0")
    for k in range(2):
        mm(4 + k, 128, pair("vq", "vp", 0, 128), pair("q2", "p2", 128 * k, 128 * k + 128))
        cp(v("yo", 128 * k, 128 * k + 128), ps(4 + k, 0, 128))
        dma("YS"[k], T.y[:, 128 * k:128 * k + 128], T.yo[:, 128 * k:128 * k + 128], regs(v("yo", 128 * k, 128 * k + 128)), [], "st%d" % (2 + 5 * k))
    dma("Y", T.oc[:], T.q2[:].bitcast(dt.uint8), regs(v("q2")), [], "st1")
    for k in range(4):
        dma("S" if k % 2 else "Y", T.osc[4 * k:4 * k + 4, :], T.p2[32 * k:32 * k + 4, :], regs(v("p2")), [], "st%d" % (3 + k))
    emit(g, T, ops, sent[0], first, late)


def ordered(ops, deps, first, late):
    n, place = len(ops), {}

    def visit(i):
        if i not in place:
            for j in deps[i]:
                visit(j)
            place[i] = len(place)
    for i in list(range(first, n)) + list(range(first)):
        visit(i)
    users, tail = [[] for o in ops], [o[7] for o in ops]
    for i in range(n - 1, -1, -1):
        for j in deps[i]:
            users[j].append(i)
            tail[j] = max(tail[j], ops[j][7] + WAKE + tail[i])
    plain, best = eager(ops, deps, users, place, late), None
    for share in SHARES:
        ahead = sorted(range(n), key=lambda i: (plain[i] - share * (plain[i] + tail[i]), place[i]))
        start = eager(ops, deps, users, {i: k for k, i in enumerate(ahead)}, late) if share else plain
        back = placed(ops, users, sorted(range(n), key=lambda i: (-start[i] - ops[i][7], -place[i])), True)
        start = placed(ops, deps, sorted(range(n), key=lambda i: (-back[i] - ops[i][6], place[i])), False)
        end = max(start[i] + ops[i][7] for i in start)
        if best is None or end < best[0]:
            best = (end, start)
    return sorted(range(n), key=lambda i: (best[1][i], place[i]))


SHARES = (0.0, 0.2, 0.5, 1.0)


def eager(ops, deps, users, place, late):
    n, open_ = len(ops), [len(d) for d in deps]
    ready, start, free, now = {i: 0.0 for i in range(n) if not deps[i]}, {}, {}, 0.0
    while ready:
        moved = False
        for q in "YGPVSf":
            if free.get(q, 0.0) > now:
                continue
            soon = BIG
            for i in sorted((i for i in ready if ops[i][0][0] == q), key=lambda i: place[i]):
                if ready[i] > now:
                    soon = min(soon, ready[i])
                elif i not in late or now + ops[i][6] <= soon:
                    start[i], free[q], moved = now, now + ops[i][6], True
                    del ready[i]
                    for k in users[i]:
                        open_[k] -= 1
                        if not open_[k]:
                            ready[k] = max(start[j] + (ops[j][6] if ops[k][0] == ops[j][0] in "PG" else ops[j][7] + WAKE) for j in deps[k])
                    break
        if not moved:
            now = min(x for x in list(ready.values()) + list(free.values()) if x > now)
    return start


def placed(ops, before, order, back):
    start, taken = {}, {}
    for i in order:
        busy, done = ops[i][6], ops[i][7]
        at = done - busy if back else 0.0
        for j in before[i]:
            if ops[i][0] == ops[j][0] in "PG":
                at = max(at, start[j] + ops[j][6])
            else:
                at = max(at, start[j] + ops[j][6] + WAKE + done - busy if back else start[j] + ops[j][7] + WAKE)
        row = taken.setdefault(ops[i][0], [])
        for a, b in row:
            if at + busy <= a:
                break
            at = max(at, b)
        start[i] = at
        row.append((at, at + busy))
        row.sort()
    return start


KEPT = {}


def emit(g, T, ops, sent, first, late):
    eng = {"V": g.vector, "S": g.scalar, "P": g.tensor, "G": g, "Y": g.sync}
    if not KEPT:
        deps = []
        for i, o in enumerate(ops):
            d = []
            for j in range(i):
                p = ops[j]
                hit = any(_meet(a, b) for a in o[2] + o[3] for b in p[3]) or any(_meet(a, b) for a in o[3] for b in p[2])
                if not hit and o[0] != p[0]:
                    hit = any(a[0].startswith("ps") and a[0] == b[0] for a in o[2] for b in p[2])
                if hit:
                    d.append(j)
            deps.append(d)
        row = [i for i, o in enumerate(ops) if o[0] == "G"]
        KEPT[0] = (deps, ordered(ops, [d + [row[row.index(i) - 1]] if i in row[1:] else d for i, d in enumerate(deps)], first, late))
    deps, order = KEPT[0]
    place = {i: k for k, i in enumerate(order)}
    known = {q: {} for q in eng}
    clock, waits, marked = {}, {}, set()
    for i in order:
        o = ops[i]
        if o[0] == "far":
            clock[i] = {o[4]: place[i]}
            continue
        k, need = known[o[0]], {}
        for j in deps[i]:
            if ops[j][4] == "remote" or o[0] == ops[j][0] == "P":
                continue
            key = ops[j][4] or ops[j][0]
            need[key] = max(need.get(key, -1), place[j])
        w = []
        for key, at in sorted(need.items(), key=lambda e: -e[1]):
            if k.get(key, -1) < at:
                w.append(order[at])
                for kk, jj in clock[order[at]].items():
                    k[kk] = max(k.get(kk, -1), jj)
        marked.update(w)
        waits[i] = w
        c = dict(k)
        c[o[4] or o[0]] = place[i]
        clock[i] = c
    count, value = {q: 0 for q in eng}, {}
    for i in order:
        if ops[i][4] is None and i in marked:
            count[ops[i][0]] += 1
            value[i] = count[ops[i][0]]
    for i in order:
        o = ops[i]
        if o[0] == "far":
            continue
        for j in waits[i]:
            if ops[j][4] is None:
                eng[o[0]].wait_ge(T.sem["s" + ops[j][0]], value[j])
            else:
                eng[o[0]].wait_ge(T.sem[ops[j][4]], ops[j][5])
        ins = o[1]()
        if o[4] is None:
            if i in marked:
                ins.then_inc(T.sem["s" + o[0]], 1)
        elif o[4] != "remote":
            ins.then_inc(T.sem[o[4]], 16)
    g.wait_ge(T.sem.sent, sent)
    for o in ops:
        if o[4] is not None and o[4].startswith("st"):
            g.wait_ge(T.sem[o[4]], 16)
